import numpy as np, ml_dtypes
CORES = [242,247,114,119]
N = 4
BF = ml_dtypes.bfloat16
def gentries(a):
    return np.ascontiguousarray(a.reshape(8, 16, -1).transpose(0, 2, 1)).reshape(8, -1)
def gtable(e):
    e = np.asarray(e); return np.ascontiguousarray(e.reshape(8, -1, 16).transpose(0, 2, 1)).reshape(128, -1).astype(np.int32)
F, STEP, CAPP, V, R, D = 2048, 128, 160, 4096, 2, 3
def aim(rng, s):
    p = rng.integers(1, 64, F); o = rng.permutation(F); k = s - int(np.sum(p)); room = (63 - p if k > 0 else p - 1)[o]
    p[o] += np.sign(k) * np.clip(abs(k) - (np.add.accumulate(room) - room), 0, room)
    return p
def rise(rng):
    top = N * CAPP * STEP + int(rng.integers(62, STEP + 1)); lo, hi, best = F, N * CAPP * STEP, -1
    for k in range(20):
        s = (lo + hi) // 2 if k else F; v = aim(rng, s); z = v.copy()
        for a in range(R - 1):
            z[np.flatnonzero(np.diff(np.add.accumulate(z) // STEP, prepend=0))] = 63
        u = int(np.sum(z))
        if u >= top: hi = s
        else:
            lo = s
            if u > best: best, p, last = u, v, z
    total = np.concatenate([np.zeros(1, np.int64), np.add.accumulate(last)]) + 63 * (F - np.arange(F + 1))
    p[np.flatnonzero(total < top)[0]:] = 63
    return p
def links(rng):
    lab = rng.integers(0, rng.integers(8, 257), F); o = np.argsort(lab, kind="stable"); b, c = o[:-1], o[1:]
    on = (lab[b] == lab[c]) & (rng.random(F - 1) > 0.05); v = np.stack([np.arange(F), np.arange(F)])
    v[0, c[on]] = b[on]; v[1, b[on]] = c[on]
    return v
def whole(rng, m, *shape):
    return rng.integers(-m, m + 1, shape).astype(np.float32).astype(BF)
def draw(rng, lo, hi):
    v = np.stack([np.stack([links(rng) for g in range(8)]) for r in range(N)]).astype(np.int32)
    return {"x": whole(rng, 8, N, 128, F), "prv": np.ascontiguousarray(v[:, :, 0]), "nxt": np.ascontiguousarray(v[:, :, 1]), "key": rng.integers(0, V, (N, 8, F)).astype(np.int32), "rw": rng.integers(-255, 256, (N, 8, F)).astype(np.int32),
            "pri": np.stack([gtable(np.stack([aim(rng, int(rng.integers(lo * F, hi * F))) for g in range(8)])) for r in range(N)]), "w": whole(rng, 4, N, 128, 2 * D + 1), "val": whole(rng, 8, N, 128, V)}
def put(d, r, g, p):
    e = gentries(d["pri"][r]); e[g] = p; d["pri"][r] = gtable(e)
def setup_inputs(rng):
    return draw(rng, 24, 34)
def setup_inputs_full(rng):
    d = draw(rng, 24, 34); o = rng.permutation(N); late = rng.random((N, 8)) < 0.2; late[o[1], rng.permutation(8)[:4]] = True; late[o[0]] = False
    m = rng.random((N, 8)) < 0.3; m[o[0]] = True; m = m & ~late
    for r, g in np.argwhere(m):
        put(d, r, g, aim(rng, N * CAPP * STEP + int(rng.integers(0, STEP))))
        d["x"][r, 16 * g:16 * g + 16] = whole(rng, 1, 16, F); d["rw"][r, g] = rng.integers(-60, 61, F)
    for r, g in np.argwhere(late):
        put(d, r, g, rise(rng))
        d["x"][r, 16 * g:16 * g + 16] = 0; d["rw"][r, g] = 340; d["rw"][r, g, 0] = 0
    return d
def setup_inputs_even(rng):
    d = draw(rng, 24, 34)
    for r in range(N):
        d["pri"][r] = gtable(np.repeat(rng.permutation(np.array([16, 16, 16, 32, 32, 32, 32, 32]))[:, None], F, 1))
    return d
def setup_inputs_few(rng):
    d = draw(rng, 24, 34)
    for r in range(N):
        o = rng.permutation(8)[:4]
        for g in o[1:]: d["x"][r, 16 * g:16 * g + 16] = 0
        for g in o[:2]: put(d, r, g, np.ones(F, np.int64))
        for g in o[2:]: put(d, r, g, aim(rng, int(rng.integers(12 * F, 17 * F))))
        d["rw"][r, o[1]] = 0; d["rw"][r, o[2]] = rng.choice(np.array([0, 8, -8, 16, -16, 5, -5]), F); d["rw"][r, o[3]] = rng.choice(np.array([-336, -342, 336, 341, 335, 330]), F)
    return d
def setup_inputs_loose(rng):
    d = draw(rng, 8, 17); d["prv"] = rng.integers(0, F, (N, 8, F)).astype(np.int32); d["nxt"] = rng.integers(0, F, (N, 8, F)).astype(np.int32)
    for n, m in (("x", 8), ("w", 4), ("val", 8)):
        d[n] = (m * (2 * rng.integers(0, 2, d[n].shape) - 1)).astype(np.float32).astype(BF)
    d["rw"] = (1023 * rng.integers(-1, 2, (N, 8, F))).astype(np.int32)
    for r in range(N):
        o = rng.permutation(8)
        d["prv"][r, o[0]] = 0; d["nxt"][r, o[0]] = F - 1; d["prv"][r, o[1]] = np.arange(F); d["nxt"][r, o[1]] = np.arange(F)
        d["prv"][r, o[2]] = (np.arange(F) - 1) % F; d["nxt"][r, o[2]] = (np.arange(F) + 1) % F
        d["key"][r, o[3]] = V - 1; d["key"][r, o[4]] = rng.choice(np.array([0, V - 1]), F)
        d["x"][r, 16 * o[5]:16 * o[5] + 16] = 8
    q = rng.integers(0, N); d["w"][q] = 4; d["val"][q] = 8
    return d
def setup_inputs_spread(rng):
    d = draw(rng, 8, 17)
    for n, m in (("x", F), ("val", V)):
        s = np.left_shift(1, rng.integers(0, 4, (N, 1, m))) * (rng.random((N, 1, m)) > 0.0625)
        d[n] = (rng.integers(-1, 2, (N, 128, m)) * s).astype(np.float32).astype(BF)
    d["w"] = (rng.integers(-4, 5, (N, 128, 2 * D + 1)) * (rng.random((N, 128, 1)) > 0.4)).astype(np.float32).astype(BF)
    d["key"] = np.minimum(rng.random((N, 8, F)) ** 3 * V, V - 1).astype(np.int32)
    d["rw"] = np.right_shift(rng.integers(-1023, 1024, (N, 8, F)), rng.integers(0, 11, (N, 8, F))).astype(np.int32)
    return d
def play(x, prv, nxt, key, rw, pri, w, val):
    X = x.astype(np.float32).reshape(N, 8, 16, F); W = w.astype(np.float32).reshape(N, 8, 16, 2 * D + 1); A = val.astype(np.float32).reshape(N, 8, 16, V)
    P = np.stack([gentries(pri[r]) for r in range(N)]).astype(np.int64); most = 0
    for a in range(R):
        for r in range(N):
            for g in range(8):
                t = np.flatnonzero(np.diff(np.add.accumulate(P[r, g]) // STEP, prepend=0)); most = max(most, len(t))
                q = np.arange(len(t)) % N
                pt = {0: t}
                for k in range(1, D + 1):
                    pt[k] = nxt[r, g][pt[k - 1]]; pt[-k] = prv[r, g][pt[1 - k]]
                h = np.zeros((len(t), 16), np.float32)
                for k in range(-D, D + 1):
                    h += W[q, g, :, D + k] * X[r, g][:, pt[k]].T
                e = np.sum(A[q, g, :, key[r, g][t]] * h, axis=1) + (rw[r, g][pt[0]] + rw[r, g][pt[1]] + rw[r, g][pt[2]])
                P[r, g, t] = np.minimum(np.maximum(np.abs(e).astype(np.int64) >> 4, 1), 63)
    return P, most
def check_inputs(d):
    bad = []
    for n, lo, hi in (("x", -8, 8), ("prv", 0, F - 1), ("nxt", 0, F - 1), ("key", 0, V - 1), ("rw", -1023, 1023), ("pri", 1, 63), ("w", -4, 4), ("val", -8, 8)):
        v = np.asarray(d[n]).astype(np.float32)
        if not (np.isfinite(v).all() and (v == np.floor(v)).all() and v.min() >= lo and v.max() <= hi): bad.append(n)
    if not bad and play(**d)[1] > N * CAPP: bad.append("CAPP")
    return bad
def reference(x, prv, nxt, key, rw, pri, w, val):
    P, most = play(x, prv, nxt, key, rw, pri, w, val)
    y = np.stack([gtable(P[r]) for r in range(N)])
    return {"y": y.astype(np.float32)}

@@ -1,0 +1,441 @@
+from concourse.bass import DstId, RemoteDMATransfer
+from concourse.mybir import dt, AluOpType, AxisListType, ActivationFunctionType
+
+F16, BF, F32, I32, U16 = "float16", "bfloat16", "float32", "int32", "uint16"
+LISTS = ["L0", "L1", "M1", "L2", "M2", "L3", "M3"]
+SCRATCH = {
+    "PRI": ("sbuf", [128, 128], I32), "PB0": ("sbuf", [128, 128], BF), "PB1": ("sbuf", [128, 128], BF),
+    "TI": ("sbuf", [128, 16, 32], I32), "TX": ("sbuf", [128, 16, 32], F16), "TT": ("sbuf", [128, 16, 32], F16),
+    "X": ("sbuf", [128, 2048], BF), "VALB": ("sbuf", [128, 4096], BF), "PW": ("sbuf", [128, 2048], I32),
+    "IM": ("sbuf", [128, 160], I32), "I16": ("sbuf", [128, 128], I32), "KP": ("sbuf", [128, 1], I32), "T8I": ("sbuf", [128, 64], I32),
+    "CI": ("sbuf", [128, 8], I32), "CF": ("sbuf", [128, 8], F32), "CG": ("sbuf", [128, 8], F32),
+    "BO": ("sbuf", [128, 128], BF), "TM": ("sbuf", [128, 128], BF), "IDW": ("sbuf", [128, 160], BF), "ONB": ("sbuf", [128, 144], BF),
+    "C16": ("sbuf", [128, 128], BF), "PM": ("sbuf", [128, 512], BF), "Z2": ("sbuf", [128, 144], F16), "Z2T": ("sbuf", [128, 144], F16),
+    "ZN": ("sbuf", [128, 144], BF), "ZP": ("sbuf", [128, 144], BF), "ES": ("sbuf", [128, 256], BF), "ER": ("sbuf", [128, 256], BF),
+    "T8H": ("sbuf", [128, 64], F16), "PV": ("sbuf", [128, 128], U16),
+    "ONE": ("sbuf", [128, 128], F32), "CS": ("sbuf", [128, 128], F32), "SI": ("sbuf", [128, 128], I32), "RI": ("sbuf", [128, 128], I32),
+    "K2": ("sbuf", [128, 128], I32), "NF": ("sbuf", [128, 128], F32), "CODE": ("sbuf", [128, 128], F16), "M4": ("sbuf", [128, 512], F16),
+    "MK": ("sbuf", [128, 512], F16), "MN": ("sbuf", [128, 512], F16), "MP": ("sbuf", [128, 512], F16), "RW4": ("sbuf", [128, 512], F16),
+    "KS0": ("sbuf", [128, 64], U16), "KS1": ("sbuf", [128, 64], U16), "KL0": ("sbuf", [128, 64], U16), "KL1": ("sbuf", [128, 64], U16),
+    "VS0": ("sbuf", [128, 1024], BF), "VS1": ("sbuf", [128, 1024], BF), "VR0": ("sbuf", [128, 1024], BF), "VR1": ("sbuf", [128, 1024], BF),
+    "PROD": ("sbuf", [128, 1024], F16), "EM": ("sbuf", [128, 256], F32), "EA": ("sbuf", [128, 128], F32), "EB": ("sbuf", [128, 128], F32),
+    "EC": ("sbuf", [128, 128], F32), "AB": ("sbuf", [128, 128], F32), "NI": ("sbuf", [128, 128], I32), "PK": ("sbuf", [128, 128], F32),
+    "KEEP": ("sbuf", [128, 128], F32), "YO": ("sbuf", [128, 128], F32), "WS": ("sbuf", [128, 7], BF), "WF": ("sbuf", [128, 7], F32),
+    "WR": ("sbuf", [128, 32], BF), "WG": ("sbuf", [128, 32], F32), "DG": ("sbuf", [128, 28 * 128], BF),
+    "QA": ("psum", [128, 512], F32), "QB": ("psum", [128, 512], F32), "QT": ("psum", [128, 512], F32), "QE": ("psum", [128, 512], F32),
+    "XT1": ("sbuf", [128, 2048], BF), "XT2": ("sbuf", [128, 2048], BF),
+}
+for _n in LISTS:
+    SCRATCH[_n] = ("sbuf", [128, 64], U16)
+    SCRATCH["X" + _n] = ("sbuf", [128, 1024], BF)
+for _n in LISTS[1:5]:
+    SCRATCH["R" + _n] = ("sbuf", [128, 1024], F16)
+for _q in range(4):
+    SCRATCH["H%d" % _q] = ("psum", [128, 512], F32)
+SEMAPHORES = (["dpri", "dtab", "dw", "dx", "dval", "dpw", "dy", "gi", "gz", "gsel", "ges", "ges2", "vz", "vcon", "vc", "vc2", "vc3", "vi8", "vbo", "vtm",
+               "vtm2", "vpb", "sperm", "vcv", "vtr", "vz4", "vone", "vid", "vpv", "vscan", "vS", "vr", "vnf", "vcode", "vm0", "vm1", "vm2", "vm3",
+               "vmk", "vmn", "vmp", "vpk", "vkeep", "eK", "eO", "gV", "gU", "vrw4", "vdg", "vpr", "vem", "va1", "va2", "va3", "vab", "vni", "vP", "ptab",
+               "pA", "pB", "pK", "ph0", "ph1", "ph2", "ph3", "pE", "swf", "sdg", "swg", "sdg2", "st1", "st2", "wl", "wr", "kl", "vl",
+               "kr0", "kr1", "ko0", "ko1"]
+              + ["e" + n for n in LISTS] + ["p" + n for n in LISTS] + ["s" + n for n in LISTS] + ["g" + n for n in LISTS[1:5]]
+              + ["vr%d_%d" % (a, q) for a in range(2) for q in range(4)])
+
+
+def rank_program(g, core, T, topo):
+    rank = T.rank_of(core)
+    if rank is None:
+        return
+    A = AluOpType
+    COPY, ABS = ActivationFunctionType.Copy, ActivationFunctionType.Abs
+    V, S, P = g.vector, g.scalar, g.tensor
+    Q = {"v": V, "s": S, "t": P, "y": g.sync, "g": g}
+    tot, got = {}, {}
+
+    def done(ins, name, n=1):
+        ins.then_inc(T.sem[name], n)
+        tot[name] = tot.get(name, 0) + n
+
+    def need(q, *names):
+        for n in names:
+            if got.get((q, n), 0) < tot[n]:
+                Q[q].wait_ge(T.sem[n], tot[n])
+                got[(q, n)] = tot[n]
+
+    def off_of(src):
+        return [c for c in T.cores if c not in topo.cores_of(src)]
+
+    def on_of(src):
+        return [c for c in T.cores if c != src and c in topo.cores_of(src)]
+
+    def engines_of(src):
+        off, out = off_of(src), {}
+        eo = topo.engines(src, off[0])
+        n = len(eo) // len(off)
+        for k, c in enumerate(off):
+            out[c] = eo[k * n:(k + 1) * n]
+        for c in on_of(src):
+            out[c] = [e for e in topo.engines(src, c) if e not in eo]
+        return out
+
+    def place(c, at):
+        return (off_of(at) + on_of(at) + [at]).index(c)
+
+    off, on = off_of(core), on_of(core)
+    peers = on + off
+    others = [T.rank_of(c) for c in peers]
+    half = len(off)
+    eng = engines_of(core)
+    inc = {c: len(engines_of(c)[core]) for c in peers}
+
+    def send(to, src_of, dst_of, sem_of, local):
+        tr = []
+        for c in to:
+            rid, pid = topo.addr(c, core)
+            m = 0
+            for e in eng[c]:
+                m |= 1 << e
+            tr.append(RemoteDMATransfer(dst_ids=[DstId(rid=rid, pnc=pid)], dma_engine_mask=m, remote_sem=sem_of(c), src=src_of(c), dst=dst_of(c)))
+        g.remote_dma_fused(tr, local_sem=T.sem[local])
+        tot[local] = tot.get(local, 0) + sum(len(eng[c]) for c in to)
+
+    done(g.sync.dma_start(T.PRI[:], T.pri[:]), "dpri", 16)
+    done(S.dma_start(T.WS[:], T.w[:]), "dw", 16)
+    done(g.sync.dma_start(T.TI[:, 0:4, :], T.key[:]), "dtab", 16)
+    done(S.dma_start(T.TI[:, 4:8, :], T.nxt[:]), "dtab", 16)
+    done(g.sync.dma_start(T.TI[:, 8:12, :], T.prv[:]), "dtab", 16)
+    done(S.dma_start(T.TI[:, 12:16, :], T.rw[:]), "dtab", 16)
+    done(S.dma_start(T.X[:], T.x[:]), "dx", 16)
+
+    done(g.iota(T.IM[:], [[1, 160]], -16, 0), "gi")
+    done(g.iota(T.KP[:], [[0, 1]], 0, 1), "gi")
+    done(g.iota(T.T8I[:], [[0, 4], [128, 16]], 0, 0), "gi")
+    done(g.iota(T.PW[:, 1024:2048], [[0, 1024]], 0, 0), "gz")
+    done(V.memset(T.PW[:, 0:1024], 0), "vz")
+    need("y", "gz", "vz")
+    done(g.sync.dma_start(T.PW[0:128:16, :], T.nxt[:]), "dpw", 16)
+    done(g.sync.dma_start(T.PW[1:128:16, :], T.prv[:]), "dpw", 16)
+    done(g.sync.dma_start(T.PW[2:128:16, :], T.rw[:]), "dpw", 16)
+    done(g.sync.dma_start(T.VALB[:], T.val[:]), "dval", 16)
+    need("g", "dw")
+    send(peers, lambda c: T.WS[:], lambda c: T.WR[:, 8 * rank:8 * rank + 7], lambda c: T.sem.wr, "wl")
+    tot["wr"] = sum(inc.values())
+
+    done(V.memset(T.ONE[:], 1.0), "vone")
+    need("v", "gi")
+    kp = T.KP[:]
+    m = T.IM[:, 16:144]
+    ident = T.IDW[:, 16:144]
+
+    def bits(j, sh, msk):
+        done(V.tensor_scalar(T.CI[:, j:j + 1], kp, sh, msk, A.logical_shift_right, A.bitwise_and), "vc")
+
+    cf = lambda j: T.CF[:, j:j + 1]
+    cg = lambda j: T.CG[:, j:j + 1]
+    bits(0, 4, 7)
+    bits(1, 4, 1)
+    bits(2, 0, 127)
+    bits(3, 0, 15)
+    bits(4, 0, 7)
+    bits(5, 0, 112)
+    bits(6, 3, 1)
+    done(V.tensor_scalar(T.I16[:], m, 4, None, A.logical_shift_right), "vi8")
+    need("v", "vc")
+    done(V.tensor_copy(T.CF[:, 0:7], T.CI[:, 0:7]), "vc2")
+    need("v", "vc2", "vi8")
+    done(V.tensor_scalar(T.BO[:], T.I16[:], cf(0), None, A.is_equal), "vbo")
+    done(V.tensor_scalar(T.TM[:], m, cf(2), -1.0, A.is_lt, A.mult), "vtm")
+    done(V.tensor_scalar(cg(5), cf(1), 0.0, None, A.is_equal), "vc3")
+    done(V.tensor_tensor(cg(1), cf(5), cf(6), A.add), "vc3")
+    done(V.tensor_scalar(cg(7), cf(3), 8.0, None, A.mult), "vc3")
+    need("v", "vbo", "vtm")
+    done(V.tensor_tensor(T.TM[:], T.TM[:], T.BO[:], A.mult), "vtm2")
+    done(V.tensor_scalar(T.IDW[:], T.IM[:], cf(2), None, A.is_equal), "vid")
+    need("v", "dpri")
+    done(V.tensor_copy(T.PB0[:], T.PRI[:]), "vpb")
+    need("v", "vc3")
+    done(V.tensor_scalar(T.Z2T[:], T.IM[:, 0:144], cg(1), cf(4), A.is_equal, A.mult), "vz4")
+    done(V.tensor_scalar(T.Z2[:], T.IM[:, 0:144], cg(1), None, A.is_equal), "vz4")
+    done(V.tensor_scalar(T.T8H[:], T.T8I[:], cg(7), None, A.add), "vz4")
+
+    need("s", "vid", "vc3", "vc2")
+    for n, (lo, msk) in enumerate([(16, cg(5)), (32, cf(1)), (0, cg(5)), (16, cf(1))]):
+        done(S.activation(T.PM[:, 128 * n:128 * n + 128], T.IDW[:, lo:lo + 128], COPY, scale=msk), "sperm")
+    need("s", "dw")
+    done(S.activation(T.WF[:], T.WS[:], COPY), "swf")
+    need("s", "swf")
+    for d in range(7):
+        o = (7 * rank + d) * 128
+        done(S.activation(T.DG[:, o:o + 128], ident, COPY, scale=T.WF[:, d:d + 1]), "sdg")
+
+    def sums(a):
+        pb = T.PB0 if a == 0 else T.PB1
+        need("t", "vbo", "vpb" if a == 0 else "vP")
+        done(P.matmul(T.QA[:, 0:128], T.BO[:], pb[:], True, True), "pA")
+        need("t", "vtm2")
+        done(P.matmul(T.QB[:, 0:128], T.TM[:], pb[:], True, True), "pB")
+
+    def tables_out():
+        need("t", "sperm", "vtr")
+        for b1 in range(8):
+            bt = b1 % 2
+            for ga in range(2):
+                n = 2 * ga + bt
+                ins = P.matmul(T.QT[:, b1:512:8], T.PM[:, 128 * n:128 * n + 128], T.TT[:, b1 // 2:16:4, 16 * ga:16 * ga + 16], ga == 0, ga == 1)
+            if b1 == 7:
+                done(ins, "ptab")
+
+    def gpsimd_selectors():
+        need("g", "vcon")
+        done(g.affine_select(T.ZN[:], T.ONB[:], [[-16, 9], [-1000, 16]], A.is_equal, 0.0, 16, 1), "gsel")
+        done(g.affine_select(T.ZP[:], T.ONB[:], [[-16, 9], [-1000, 16]], A.is_equal, 0.0, 15, 1), "gsel")
+        for ih in range(2):
+            pat, base = [[-16, 8], [1000 if ih else -1000, 2], [0, 8]], -1000 if ih else 0
+            o = slice(128 * ih, 128 * ih + 128)
+            done(g.affine_select(T.ER[:, o], T.C16[:], pat, A.is_equal, 0.0, base - 2, 1), "ges2")
+            done(g.affine_select(T.ES[:, o], T.C16[:], pat, A.is_ge, 0.0, base, 1), "ges")
+        need("g", "ges")
+        for ih in range(2):
+            o = slice(128 * ih, 128 * ih + 128)
+            done(g.affine_select(T.ES[:, o], T.ES[:, o], [[16, 8], [0, 2], [0, 8]], A.is_ge, 0.0, 15, -1), "ges2")
+
+    KEYC, NXTC, PRVC, RWC = 0, 128, 256, 384
+    STEP = {"L0": 3, "L1": 4, "L2": 5, "L3": 6, "M1": 2, "M2": 1, "M3": 0}
+    MASKS = ["vm0", "vm1", "vm2", "vm3"]
+
+    def blocksum(name, bank, sel, rows, first=True):
+        for cl in range(8):
+            ins = P.matmul(T[bank][:, 0:64], T[sel][:, 16 - 2 * cl:144 - 2 * cl], T[rows][:, cl:512:8], first and cl == 0, cl == 7)
+        done(ins, name)
+
+    def wrap(lst, bank, sel, rows):
+        need("t", "gsel")
+        for ro in range(16):
+            ins = P.matmul(T[bank][:, 0:64], T[sel][:, 16 - ro:144 - ro], T[rows][:, ro:1024:16], ro == 0, ro == 15)
+        done(ins, "p" + lst)
+
+    def evac(lst, bank):
+        need("v", "p" + lst)
+        done(V.tensor_copy(T[lst][:], T[bank][:, 0:64]), "e" + lst)
+
+    def mul(out, col, sem, qs=range(4)):
+        for q in qs:
+            need("v", MASKS[q])
+            done(V.tensor_tensor(T[out][:, 128 * q:128 * q + 128], T.M4[:, 128 * q:128 * q + 128], T.QT[:, col:col + 128], A.mult), sem)
+
+    def pick_x(lst, on_q="s", table="X", at=None):
+        at = at or lst
+        need(on_q, "dx", "e" + at)
+        src = T[table][:].indirect(T[at][:])
+        if on_q == "s":
+            done(S.activation(T["X" + lst][:], src, COPY), "s" + lst)
+        else:
+            done(V.tensor_copy(T["X" + lst][:], src), "s" + lst)
+
+    def pick_p(lst):
+        need("v", "dpw", "e" + lst)
+        done(V.tensor_copy(T["R" + lst][:], T.PW[:].indirect(T[lst][:])), "g" + lst)
+
+    def hsum(lst, k):
+        need("t", "s" + lst)
+        for q in [rank] + others:
+            o = (7 * q + STEP[lst]) * 128
+            ins = P.matmul(T["H%d" % q][:, 0:256], T.DG[:, o:o + 128], T["X" + lst][:, 256 * q:256 * q + 256], k == 0, k == 6)
+            if k == 6:
+                done(ins, "ph%d" % q)
+
+    def esum(sel, rows, last):
+        for ih in range(2):
+            ins = P.matmul(T.QE[:], T[sel][:, 128 * ih:128 * ih + 128], T[rows][:, ih:1024:2], False, last and ih == 1)
+        if last:
+            done(ins, "pE")
+
+    def rewards():
+        need("t", "vrw4", "ges2")
+        P.matmul(T.QE[:], ident, T.RW4[:], True, False)
+        esum("ER", "RL1", False)
+        esum("ER", "RL2", False)
+
+    def serve(a):
+        KL, VS, VR = T["KL%d" % a], T["VS%d" % a], T["VR%d" % a]
+        src = lambda c: VS[:, 256 * place(c, core):256 * place(c, core) + 256]
+        dst = lambda c: VR[:, 256 * rank:256 * rank + 256]
+        sem = lambda c: T.sem["vr%d_%d" % (a, rank)]
+        need("s", "dval", "ko%d" % a)
+        done(S.activation(VS[:, 0:256 * half], T.VALB[:].indirect(KL[:, 0:16 * half]), COPY), "gU")
+        need("s", "kr%d" % a, "eO")
+        done(S.activation(VS[:, 256 * half:1024], T.VALB[:].indirect(KL[:, 16 * half:64]), COPY), "gV")
+        need("g", "gU")
+        send(off, src, dst, sem, "vl")
+        need("g", "gV")
+        send(on, src, dst, sem, "vl")
+        for c in peers:
+            tot["vr%d_%d" % (a, T.rank_of(c))] = inc[c]
+
+    for a in range(2):
+        pb = T.PB0 if a == 0 else T.PB1
+        KS, KL, VS, VR = T["KS%d" % a], T["KL%d" % a], T["VS%d" % a], T["VR%d" % a]
+        sums(a)
+        need("v", "pA", "vone")
+        done(V.tensor_tensor_scan(T.CS[:], T.ONE[:], T.QA[:, 0:128], 0.0, A.mult, A.add), "vscan")
+        need("v", "pB", "vscan")
+        done(V.tensor_tensor(T.SI[:], T.CS[:], T.QB[:, 0:128], A.add), "vS")
+        need("v", "vS")
+        done(V.tensor_scalar(T.RI[:], T.SI[:], 127, None, A.bitwise_and), "vr")
+        done(V.tensor_scalar(T.K2[:], T.SI[:], 6, 6, A.arith_shift_right, A.bitwise_and), "vr")
+        if a == 0:
+            need("v", "dtab")
+            done(V.tensor_scalar(T.TX[:, 0:4, :], T.TI[:, 0:4, :], 2048.0, None, A.subtract), "vcv")
+            done(V.tensor_copy(T.TX[:, 4:16, :], T.TI[:, 4:16, :]), "vcv")
+        need("v", "vr")
+        done(V.tensor_tensor(T.NF[:], T.RI[:], pb[:], A.is_ge), "vnf")
+        if a == 0:
+            need("v", "vcv")
+            done(V.transpose(T.TT[:], T.TX[:]), "vtr")
+            tables_out()
+        need("v", "vnf")
+        done(V.tensor_tensor(T.CODE[:], T.K2[:], T.NF[:], A.add), "vcode")
+        need("v", "vcode")
+        for q in range(4):
+            done(V.tensor_scalar(T.M4[:, 128 * q:128 * q + 128], T.CODE[:], float(2 * ((q + 1) % 4)), None, A.is_equal), MASKS[q])
+        need("t", "vz4", "vid", "vscan", *MASKS)
+        P.matmul(T.QA[:, 0:64], ident, T.T8H[:], True, False)
+        blocksum("pL0", "QA", "Z2T", "M4", False)
+        need("v", "ptab")
+        mul("MK", KEYC, "vmk")
+        need("t", "vmk", "vS")
+        blocksum("pK", "QB", "Z2", "MK")
+        evac("L0", "QA")
+        pick_x("L0")
+        mul("MN", NXTC, "vmn", (0, 1))
+        need("v", "pK")
+        done(V.tensor_scalar(KS[:], T.QB[:, 0:64], 2048.0, None, A.add), "eK")
+        need("g", "eK")
+        send(peers, lambda c: KS[:, 16 * T.rank_of(c):16 * T.rank_of(c) + 16], lambda c: KL[:, 16 * place(core, c):16 * place(core, c) + 16],
+             lambda c: T.sem[("ko%d" if c in off else "kr%d") % a], "kl")
+        tot["ko%d" % a] = sum(inc[c] for c in off)
+        tot["kr%d" % a] = sum(inc[c] for c in on)
+        mul("MN", NXTC, "vmn", (2, 3))
+        need("t", "vmn", "eL0")
+        blocksum("pL1", "QA", "Z2", "MN")
+        mine = 16 * place(core, core)
+        done(V.tensor_scalar(KL[:, mine:mine + 16], T.QB[:, 16 * rank:16 * rank + 16], 2048.0, None, A.add), "eO")
+        if a == 0:
+            done(V.memset(T.ONB[:], 1.0), "vcon")
+            done(V.memset(T.C16[:], 0.0625), "vcon")
+            gpsimd_selectors()
+        mul("MP", PRVC, "vmp")
+        need("t", "vmp", "eK", "eO")
+        blocksum("pM1", "QB", "Z2", "MP")
+        evac("L1", "QA")
+        pick_p("L1")
+        if a == 0:
+            evac("M1", "QB")
+            pick_p("M1")
+            need("t", "eL1", "gL1")
+            wrap("L2", "QA", "ZN", "RL1")
+            need("s", "wr")
+            o = others[0]
+            done(S.activation(T.WG[:, 0:7], T.WR[:, 8 * o:8 * o + 7], COPY), "swg")
+            need("s", "swg")
+            for d in range(7):
+                done(S.activation(T.DG[:, (7 * o + d) * 128:(7 * o + d) * 128 + 128], ident, COPY, scale=T.WG[:, d:d + 1]), "sdg2")
+            pick_x("L1")
+            pick_x("M1")
+            serve(a)
+            evac("L2", "QA")
+            pick_x("L2")
+            need("t", "eM1", "gM1")
+            wrap("M2", "QB", "ZP", "RM1")
+            need("v", "wr")
+            for o in others[1:]:
+                for d in range(7):
+                    done(V.tensor_scalar(T.DG[:, (7 * o + d) * 128:(7 * o + d) * 128 + 128], ident, T.WR[:, 8 * o + d:8 * o + d + 1], None, A.mult), "vdg")
+            pick_p("L2")
+            evac("M2", "QB")
+            pick_p("M2")
+            pick_x("M2")
+            need("t", "sdg", "sdg2", "vdg")
+            hsum("L0", 0)
+            hsum("L1", 1)
+            need("t", "eL2", "gL2")
+            wrap("L3", "QA", "ZN", "RL2")
+            hsum("M1", 2)
+            evac("L3", "QA")
+            pick_x("L3")
+            need("t", "eM2", "gM2")
+            wrap("M3", "QB", "ZP", "RM2")
+            done(V.tensor_copy(T.PV[:], T.QT[:, PRVC:PRVC + 128]), "vpv")
+            for q in range(4):
+                done(V.tensor_scalar(T.RW4[:, 128 * q:128 * q + 128], T.QT[:, RWC:RWC + 128], 0.0625, None, A.mult), "vrw4")
+            hsum("L2", 3)
+            rewards()
+            evac("M3", "QB")
+            pick_x("M3", "v")
+            need("s", "vpv")
+            done(S.activation(T.XT1[:], T.X[:].indirect(T.PV[:]), COPY), "st1")
+            need("s", "st1")
+            done(S.activation(T.XT2[:], T.XT1[:].indirect(T.PV[:]), COPY), "st2")
+            done(V.tensor_tensor(T.PK[:], T.NF[:], pb[:], A.mult), "vpk")
+            hsum("M2", 4)
+            hsum("M3", 5)
+            hsum("L3", 6)
+        else:
+            need("s", "st1", "st2")
+            pick_x("M1", "s", "XT1", "L0")
+            pick_x("M2", "s", "XT2", "L0")
+            serve(a)
+            hsum("L0", 0)
+            need("t", "eL1", "gL1")
+            wrap("L2", "QA", "ZN", "RL1")
+            hsum("M1", 1)
+            evac("L2", "QA")
+            evac("M1", "QB")
+            pick_x("M3", "s", "XT2", "M1")
+            pick_x("L1", "s")
+            pick_p("L2")
+            pick_x("L2", "v")
+            hsum("M2", 2)
+            need("t", "eL2", "gL2")
+            wrap("L3", "QA", "ZN", "RL2")
+            rewards()
+            evac("L3", "QA")
+            pick_x("L3", "v")
+            done(V.tensor_tensor(T.PK[:], T.NF[:], pb[:], A.mult), "vpk")
+            hsum("M3", 3)
+            hsum("L2", 4)
+            hsum("L1", 5)
+            hsum("L3", 6)
+        need("v", "vpk")
+        done(V.tensor_scalar(T.KEEP[:], T.PK[:], 1.0, None, A.max), "vkeep")
+        for q in [rank] + others:
+            need("v", "ph%d" % q, "gV" if q == rank else "vr%d_%d" % (a, q))
+            src = VS[:, 256 * place(core, core):256 * place(core, core) + 256] if q == rank else VR[:, 256 * q:256 * q + 256]
+            done(V.tensor_tensor(T.PROD[:, 256 * q:256 * q + 256], src, T["H%d" % q][:, 0:256], A.mult), "vpr")
+        need("t", "vpr")
+        esum("ES", "PROD", True)
+        need("v", "pE")
+        done(V.tensor_tensor(T.EM[:], T.M4[:, 0:256], T.QE[:, 0:256], A.mult), "vem")
+        done(V.tensor_tensor(T.QA[:, 0:256], T.M4[:, 256:512], T.QE[:, 256:512], A.mult), "vem")
+        need("v", "vem")
+        done(V.tensor_tensor(T.QB[:, 0:128], T.EM[:, 128:256], T.QA[:, 128:256], A.add), "va1")
+        done(V.tensor_tensor(T.EA[:], T.EM[:, 0:128], T.QA[:, 0:128], A.add), "va1")
+        need("v", "va1")
+        done(V.tensor_tensor(T.EB[:], T.EA[:], T.QB[:, 0:128], A.add), "va2")
+        if a == 0:
+            need("v", "va2")
+            done(V.tensor_scalar(T.EC[:], T.EB[:], -1.0, None, A.mult), "va3")
+            need("v", "va3")
+            done(V.tensor_tensor(T.AB[:], T.EB[:], T.EC[:], A.max), "vab")
+        else:
+            need("s", "va2")
+            done(S.activation(T.AB[:], T.EB[:], ABS), "vab")
+        need("v", "vab", "vkeep")
+        done(V.tensor_scalar(T.NI[:], T.AB[:], 0.46875, 63.0, A.subtract, A.min), "vni")
+        need("v", "vni")
+        done(V.tensor_tensor((T.YO if a else T.PB1)[:], T.NI[:], T.KEEP[:], A.max), "vP")
+    need("y", "vP")
+    done(g.sync.dma_start(T.y[:], T.YO[:]), "dy", 16)
+    need("y", "dy")
+    for n in sorted(tot):
+        if max([got.get((q, n), 0) for q in Q]) < tot[n]:
+            need("g", n)

@@ -2,41 +2,44 @@ from concourse.bass import DstId, RemoteDMATransfer
 from concourse.mybir import dt, AluOpType, AxisListType, ActivationFunctionType
 
 F16, BF, F32, I32, U16 = "float16", "bfloat16", "float32", "int32", "uint16"
+NS, NC, NQ = 640, 40, 160
 LISTS = ["L0", "L1", "M1", "L2", "M2", "L3", "M3"]
 SCRATCH = {
     "PRI": ("sbuf", [128, 128], I32), "PB0": ("sbuf", [128, 128], BF), "PB1": ("sbuf", [128, 128], BF),
-    "TI": ("sbuf", [128, 16, 32], I32), "TX": ("sbuf", [128, 16, 32], F16), "TT": ("sbuf", [128, 16, 32], F16),
     "X": ("sbuf", [128, 2048], BF), "VALB": ("sbuf", [128, 4096], BF), "PW": ("sbuf", [128, 2048], I32),
-    "IM": ("sbuf", [128, 160], I32), "I16": ("sbuf", [128, 128], I32), "KP": ("sbuf", [128, 1], I32), "T8I": ("sbuf", [128, 64], I32),
+    "IM": ("sbuf", [128, 160], I32), "I16": ("sbuf", [128, 128], I32), "KP": ("sbuf", [128, 1], I32), "THR": ("sbuf", [128, NS], I32),
     "CI": ("sbuf", [128, 8], I32), "CF": ("sbuf", [128, 8], F32), "CG": ("sbuf", [128, 8], F32),
-    "BO": ("sbuf", [128, 128], BF), "TM": ("sbuf", [128, 128], BF), "IDW": ("sbuf", [128, 160], BF), "ONB": ("sbuf", [128, 144], BF),
-    "C16": ("sbuf", [128, 128], BF), "PM": ("sbuf", [128, 512], BF), "Z2": ("sbuf", [128, 144], F16), "Z2T": ("sbuf", [128, 144], F16),
-    "ZN": ("sbuf", [128, 144], BF), "ZP": ("sbuf", [128, 144], BF), "ES": ("sbuf", [128, 256], BF), "ER": ("sbuf", [128, 256], BF),
-    "T8H": ("sbuf", [128, 64], F16), "PV": ("sbuf", [128, 128], U16),
-    "ONE": ("sbuf", [128, 128], F32), "CS": ("sbuf", [128, 128], F32), "SI": ("sbuf", [128, 128], I32), "RI": ("sbuf", [128, 128], I32),
-    "K2": ("sbuf", [128, 128], I32), "NF": ("sbuf", [128, 128], F32), "CODE": ("sbuf", [128, 128], F16), "M4": ("sbuf", [128, 512], F16),
-    "MK": ("sbuf", [128, 512], F16), "MN": ("sbuf", [128, 512], F16), "MP": ("sbuf", [128, 512], F16), "RW4": ("sbuf", [128, 512], F16),
-    "KS0": ("sbuf", [128, 64], U16), "KS1": ("sbuf", [128, 64], U16), "KL0": ("sbuf", [128, 64], U16), "KL1": ("sbuf", [128, 64], U16),
-    "VS0": ("sbuf", [128, 1024], BF), "VS1": ("sbuf", [128, 1024], BF), "VR0": ("sbuf", [128, 1024], BF), "VR1": ("sbuf", [128, 1024], BF),
-    "PROD": ("sbuf", [128, 1024], F16), "EM": ("sbuf", [128, 256], F32), "EA": ("sbuf", [128, 128], F32), "EB": ("sbuf", [128, 128], F32),
-    "EC": ("sbuf", [128, 128], F32), "AB": ("sbuf", [128, 128], F32), "NI": ("sbuf", [128, 128], I32), "PK": ("sbuf", [128, 128], F32),
-    "KEEP": ("sbuf", [128, 128], F32), "YO": ("sbuf", [128, 128], F32), "WS": ("sbuf", [128, 7], BF), "WF": ("sbuf", [128, 7], F32),
-    "WR": ("sbuf", [128, 32], BF), "WG": ("sbuf", [128, 32], F32), "DG": ("sbuf", [128, 28 * 128], BF),
-    "QA": ("psum", [128, 512], F32), "QB": ("psum", [128, 512], F32), "QT": ("psum", [128, 512], F32), "QE": ("psum", [128, 512], F32),
-    "XT1": ("sbuf", [128, 2048], BF), "XT2": ("sbuf", [128, 2048], BF),
+    "BO": ("sbuf", [128, 8, 16], BF), "TU": ("sbuf", [128, 128], BF), "IDW": ("sbuf", [128, 160], BF), "ONB": ("sbuf", [128, NC], BF),
+    "BY": ("sbuf", [128, 8, NC], BF), "BZ": ("sbuf", [128, 8, NC], BF), "JI": ("sbuf", [128, 448], BF), "C128": ("sbuf", [128, 128], BF),
+    "CNEG": ("sbuf", [128, 128], BF), "ZER": ("sbuf", [128, 144], BF), "EQP": ("sbuf", [128, 8, 48], BF), "UU": ("sbuf", [128, 128], F16),
+    "SG": ("sbuf", [128, 8 * NC], BF), "PM": ("sbuf", [128, 512], BF), "ZA": ("sbuf", [128, 144], BF), "ZN": ("sbuf", [128, 144], BF),
+    "ZP": ("sbuf", [128, 144], BF), "ER": ("sbuf", [128, 128], BF), "LB": ("sbuf", [128, 144], BF), "PS": ("sbuf", [128, 3, 144], BF),
+    "SD": ("sbuf", [128, 3, 128], BF),
+    "ONE": ("sbuf", [128, 128], F32), "CS": ("sbuf", [128, 128], F32), "SS": ("sbuf", [128, 128], F32),
+    "NA": ("sbuf", [128, 128], BF), "NK": ("sbuf", [128, 128], F16), "K1": ("sbuf", [128, 144], F16), "K4": ("sbuf", [128, 128], F16),
+    "K40": ("sbuf", [128, 128], BF), "COL": ("sbuf", [128, NC], U16), "C16": ("sbuf", [128, NC], F16), "CM": ("sbuf", [128, NS], BF),
+    "R0": ("sbuf", [128, NS], F16), "RT": ("sbuf", [128, NS // 32, 32], F16), "LM1": ("sbuf", [128, 2 * NC], U16),
+    "KS0": ("sbuf", [128, NC], U16), "KS1": ("sbuf", [128, NC], U16), "KL0": ("sbuf", [128, 32], U16), "KL1": ("sbuf", [128, 32], U16),
+    "VS0": ("sbuf", [128, 3 * NQ], BF), "VS1": ("sbuf", [128, 3 * NQ], BF), "VR0": ("sbuf", [128, NS], BF), "VR1": ("sbuf", [128, NS], BF),
+    "PROD": ("sbuf", [128, NS], F16), "AB": ("sbuf", [128, NS], F32), "PL": ("sbuf", [128, 64], U16), "GB": ("sbuf", [128, 1024], BF),
+    "PK": ("sbuf", [128, 128], F32), "YO": ("sbuf", [128, 128], F32),
+    "WS": ("sbuf", [128, 7], BF), "WF": ("sbuf", [128, 7], F32), "WR": ("sbuf", [128, 32], BF), "WG": ("sbuf", [128, 32], F32),
+    "DG": ("sbuf", [128, 28 * 128], BF), "TI": ("sbuf", [128, 4, 32], I32), "TX": ("sbuf", [128, 4, 32], F16), "TT": ("sbuf", [128, 4, 32], F16),
+    "PV": ("sbuf", [128, 128], U16), "XB1": ("sbuf", [128, 2048], BF), "XB2": ("sbuf", [128, 2048], BF),
 }
 for _n in LISTS:
-    SCRATCH[_n] = ("sbuf", [128, 64], U16)
-    SCRATCH["X" + _n] = ("sbuf", [128, 1024], BF)
+    SCRATCH["X" + _n] = ("sbuf", [128, NS], BF)
+for _n in ["L0", "L2", "M2", "L3", "M3"]:
+    SCRATCH[_n] = ("sbuf", [128, NC], U16)
 for _n in LISTS[1:5]:
-    SCRATCH["R" + _n] = ("sbuf", [128, 1024], F16)
-for _q in range(4):
-    SCRATCH["H%d" % _q] = ("psum", [128, 512], F32)
-SEMAPHORES = (["dpri", "dtab", "dw", "dx", "dval", "dpw", "dy", "gi", "gz", "gsel", "ges", "ges2", "vz", "vcon", "vc", "vc2", "vc3", "vi8", "vbo", "vtm",
-               "vtm2", "vpb", "sperm", "vcv", "vtr", "vz4", "vone", "vid", "vpv", "vscan", "vS", "vr", "vnf", "vcode", "vm0", "vm1", "vm2", "vm3",
-               "vmk", "vmn", "vmp", "vpk", "vkeep", "eK", "eO", "gV", "gU", "vrw4", "vdg", "vpr", "vem", "va1", "va2", "va3", "vab", "vni", "vP", "ptab",
-               "pA", "pB", "pK", "ph0", "ph1", "ph2", "ph3", "pE", "swf", "sdg", "swg", "sdg2", "st1", "st2", "wl", "wr", "kl", "vl",
-               "kr0", "kr1", "ko0", "ko1"]
+    SCRATCH["R" + _n] = ("sbuf", [128, NS], F16)
+for _n in ["QA", "QB", "E0", "E1", "H0", "H1", "H2", "H3"]:
+    SCRATCH[_n] = ("psum", [128, 512], F32)
+SEMAPHORES = (["dpri", "dw", "dx", "dval", "dpw", "dy", "gi", "gj", "gtu", "gthr", "glb", "gps", "gzz", "ger", "gsd", "gsd0", "vz", "sz", "vcon", "vc",
+               "vc2", "vc3", "vi8", "vbo", "vby", "sbz", "vpb", "vid", "vone", "veqp", "vza", "vlate", "sperm", "vscan", "vS", "vna", "vnk", "veq",
+               "vuu", "ssg", "sk", "eC", "eC16", "vcm", "gR0", "vrt", "eK", "gV", "vdg", "vpk", "ePL", "vpr0", "vpr1", "sab", "gG0", "gG1", "vni", "vP",
+               "pA", "pB", "pX", "pY", "pC", "pK", "pPL", "pS", "ph0", "ph1", "ph2", "ph3", "pE0", "pE1", "pO", "swf", "sdg", "swg", "sdg2",
+               "sM3b", "sL3b", "dtab", "vcv", "vtr", "ptab", "vpv", "gXB1", "gXB2", "wl", "wr", "kl", "vl", "kr0", "kr1"]
               + ["e" + n for n in LISTS] + ["p" + n for n in LISTS] + ["s" + n for n in LISTS] + ["g" + n for n in LISTS[1:5]]
               + ["vr%d_%d" % (a, q) for a in range(2) for q in range(4)])
 
@@ -46,7 +49,8 @@ def rank_program(g, core, T, topo):
     if rank is None:
         return
     A = AluOpType
-    COPY, ABS = ActivationFunctionType.Copy, ActivationFunctionType.Abs
+    AF = ActivationFunctionType
+    COPY, IDENT = AF.Copy, AF.Identity
     V, S, P = g.vector, g.scalar, g.tensor
     Q = {"v": V, "s": S, "t": P, "y": g.sync, "g": g}
     tot, got = {}, {}
@@ -57,7 +61,7 @@ def rank_program(g, core, T, topo):
 
     def need(q, *names):
         for n in names:
-            if got.get((q, n), 0) < tot[n]:
+            if got.get((q, n), 0) < tot.get(n, 0):
                 Q[q].wait_ge(T.sem[n], tot[n])
                 got[(q, n)] = tot[n]
 
@@ -74,16 +78,15 @@ def rank_program(g, core, T, topo):
         for k, c in enumerate(off):
             out[c] = eo[k * n:(k + 1) * n]
         for c in on_of(src):
-            out[c] = [e for e in topo.engines(src, c) if e not in eo]
+            out[c] = [e for e in topo.engines(src, c) if e not in eo][::2]
         return out
 
     def place(c, at):
-        return (off_of(at) + on_of(at) + [at]).index(c)
+        return (off_of(at) + on_of(at)).index(c)
 
     off, on = off_of(core), on_of(core)
     peers = on + off
     others = [T.rank_of(c) for c in peers]
-    half = len(off)
     eng = engines_of(core)
     inc = {c: len(engines_of(c)[core]) for c in peers}
 
@@ -100,339 +103,445 @@ def rank_program(g, core, T, topo):
 
     done(g.sync.dma_start(T.PRI[:], T.pri[:]), "dpri", 16)
     done(S.dma_start(T.WS[:], T.w[:]), "dw", 16)
-    done(g.sync.dma_start(T.TI[:, 0:4, :], T.key[:]), "dtab", 16)
-    done(S.dma_start(T.TI[:, 4:8, :], T.nxt[:]), "dtab", 16)
-    done(g.sync.dma_start(T.TI[:, 8:12, :], T.prv[:]), "dtab", 16)
-    done(S.dma_start(T.TI[:, 12:16, :], T.rw[:]), "dtab", 16)
+    done(g.sync.dma_start(T.TI[:], T.prv[:]), "dtab", 16)
     done(S.dma_start(T.X[:], T.x[:]), "dx", 16)
 
-    done(g.iota(T.IM[:], [[1, 160]], -16, 0), "gi")
     done(g.iota(T.KP[:], [[0, 1]], 0, 1), "gi")
-    done(g.iota(T.T8I[:], [[0, 4], [128, 16]], 0, 0), "gi")
-    done(g.iota(T.PW[:, 1024:2048], [[0, 1024]], 0, 0), "gz")
-    done(V.memset(T.PW[:, 0:1024], 0), "vz")
-    need("y", "gz", "vz")
-    done(g.sync.dma_start(T.PW[0:128:16, :], T.nxt[:]), "dpw", 16)
-    done(g.sync.dma_start(T.PW[1:128:16, :], T.prv[:]), "dpw", 16)
-    done(g.sync.dma_start(T.PW[2:128:16, :], T.rw[:]), "dpw", 16)
-    done(g.sync.dma_start(T.VALB[:], T.val[:]), "dval", 16)
-    need("g", "dw")
-    send(peers, lambda c: T.WS[:], lambda c: T.WR[:, 8 * rank:8 * rank + 7], lambda c: T.sem.wr, "wl")
-    tot["wr"] = sum(inc.values())
+    done(g.iota(T.IM[:], [[1, 160]], -16, 0), "gi")
+    done(g.iota(T.JI[:, 0:128], [[0, 8], [1, 16]], 0, 0, allow_small_or_imprecise_dtypes=True), "gj")
+    done(g.iota(T.JI[:, 128:448], [[0, 8], [1, 4], [4, 10]], 0, 0, allow_small_or_imprecise_dtypes=True), "gj")
 
-    done(V.memset(T.ONE[:], 1.0), "vone")
-    need("v", "gi")
+    done(V.memset(T.PW[:, 0:384], 0), "vz")
+    need("s", "vz")
+    for lo in range(384, 2048, 384):
+        hi = min(lo + 384, 2048)
+        done(S.activation(T.PW[:, lo:hi], T.PW[:, 0:hi - lo], COPY), "sz")
+    need("y", "vz", "sz")
+    for k, n in enumerate(["nxt", "prv", "key", "rw"]):
+        done(g.sync.dma_start(T.PW[k:128:16, :], T[n][:]), "dpw", 16)
+    done(g.sync.dma_start(T.VALB[:], T.val[:]), "dval", 16)
+
     kp = T.KP[:]
     m = T.IM[:, 16:144]
     ident = T.IDW[:, 16:144]
+    bo = T.BO[:]
+    cf = lambda j: T.CF[:, j:j + 1]
+    cg = lambda j: T.CG[:, j:j + 1]
 
     def bits(j, sh, msk):
         done(V.tensor_scalar(T.CI[:, j:j + 1], kp, sh, msk, A.logical_shift_right, A.bitwise_and), "vc")
 
-    cf = lambda j: T.CF[:, j:j + 1]
-    cg = lambda j: T.CG[:, j:j + 1]
+    done(V.memset(T.ONE[:], 1.0), "vone")
+    done(V.memset(T.C128[:], 1.0 / 128), "vcon")
+    need("v", "gi")
     bits(0, 4, 7)
-    bits(1, 4, 1)
-    bits(2, 0, 127)
-    bits(3, 0, 15)
-    bits(4, 0, 7)
-    bits(5, 0, 112)
-    bits(6, 3, 1)
     done(V.tensor_scalar(T.I16[:], m, 4, None, A.logical_shift_right), "vi8")
+    bits(2, 0, 127)
+    bits(1, 4, 1)
     need("v", "vc")
-    done(V.tensor_copy(T.CF[:, 0:7], T.CI[:, 0:7]), "vc2")
+    done(V.tensor_copy(T.CF[:, 0:3], T.CI[:, 0:3]), "vc2")
     need("v", "vc2", "vi8")
-    done(V.tensor_scalar(T.BO[:], T.I16[:], cf(0), None, A.is_equal), "vbo")
-    done(V.tensor_scalar(T.TM[:], m, cf(2), -1.0, A.is_lt, A.mult), "vtm")
-    done(V.tensor_scalar(cg(5), cf(1), 0.0, None, A.is_equal), "vc3")
-    done(V.tensor_tensor(cg(1), cf(5), cf(6), A.add), "vc3")
-    done(V.tensor_scalar(cg(7), cf(3), 8.0, None, A.mult), "vc3")
-    need("v", "vbo", "vtm")
-    done(V.tensor_tensor(T.TM[:], T.TM[:], T.BO[:], A.mult), "vtm2")
-    done(V.tensor_scalar(T.IDW[:], T.IM[:], cf(2), None, A.is_equal), "vid")
+    done(V.tensor_scalar(bo, T.I16[:], cf(0), None, A.is_equal), "vbo")
     need("v", "dpri")
     done(V.tensor_copy(T.PB0[:], T.PRI[:]), "vpb")
-    need("v", "vc3")
-    done(V.tensor_scalar(T.Z2T[:], T.IM[:, 0:144], cg(1), cf(4), A.is_equal, A.mult), "vz4")
-    done(V.tensor_scalar(T.Z2[:], T.IM[:, 0:144], cg(1), None, A.is_equal), "vz4")
-    done(V.tensor_scalar(T.T8H[:], T.T8I[:], cg(7), None, A.add), "vz4")
+    need("v", "vbo")
+    for lo, n in ((0, 16), (16, 16), (32, 8)):
+        done(V.tensor_copy(T.BY[:, :, lo:lo + n], T.BO[:, :, 0:n]), "vby")
+    need("g", "vbo")
+    done(g.affine_select(T.TU[:], bo, [[-1, 128]], A.is_gt, 0.0, 0, 1), "gtu")
+    done(g.iota(T.THR[:], [[128, 4], [512, 10], [5120, 16]], 128, 0), "gthr")
+    need("g", "dw")
+    send(peers, lambda c: T.WS[:], lambda c: T.WR[:, 8 * rank:8 * rank + 7], lambda c: T.sem.wr, "wl")
+    tot["wr"] = sum(inc.values())
+    need("s", "vby")
+    done(S.activation(T.BZ[:], T.BY[:], COPY, scale=-40.0), "sbz")
 
-    need("s", "vid", "vc3", "vc2")
-    for n, (lo, msk) in enumerate([(16, cg(5)), (32, cf(1)), (0, cg(5)), (16, cf(1))]):
-        done(S.activation(T.PM[:, 128 * n:128 * n + 128], T.IDW[:, lo:lo + 128], COPY, scale=msk), "sperm")
-    need("s", "dw")
-    done(S.activation(T.WF[:], T.WS[:], COPY), "swf")
-    need("s", "swf")
-    for d in range(7):
-        o = (7 * rank + d) * 128
-        done(S.activation(T.DG[:, o:o + 128], ident, COPY, scale=T.WF[:, d:d + 1]), "sdg")
+    def consts_a():
+        done(V.tensor_scalar(T.IDW[:], T.IM[:], cf(2), None, A.is_equal), "vid")
+        done(V.tensor_scalar(cg(0), cf(1), 0.0, None, A.is_equal), "vid")
+        done(V.memset(T.EQP[:], 0.0), "veqp")
+        done(V.memset(T.ZER[:], 0.0), "veqp")
+        done(V.memset(T.ONB[:], 1.0), "veqp")
 
-    def sums(a):
-        pb = T.PB0 if a == 0 else T.PB1
-        need("t", "vbo", "vpb" if a == 0 else "vP")
-        done(P.matmul(T.QA[:, 0:128], T.BO[:], pb[:], True, True), "pA")
-        need("t", "vtm2")
-        done(P.matmul(T.QB[:, 0:128], T.TM[:], pb[:], True, True), "pB")
+    def consts_b():
+        bits(3, 0, 15)
+        bits(4, 0, 112)
+        done(V.memset(T.K1[:, 0:16], 1025.0), "vc3")
+        need("v", "vc")
+        done(V.tensor_copy(T.CF[:, 3:5], T.CI[:, 3:5]), "vc2")
+        need("v", "vc2")
+        done(V.tensor_scalar(T.ZA[:], T.IM[:, 0:144], cf(4), None, A.is_equal), "vza")
+        done(V.tensor_scalar(cg(1), cf(3), 2.0, -2048.0, A.is_equal, A.mult), "vc3")
 
-    def tables_out():
+    def perms():
+        need("s", "vid", "vc2")
+        for n, (lo, msk) in enumerate([(16, cg(0)), (32, cf(1)), (0, cg(0)), (16, cf(1))]):
+            done(S.activation(T.PM[:, 128 * n:128 * n + 128], T.IDW[:, lo:lo + 128], COPY, scale=msk), "sperm")
+
+    def mark(out, pattern, base, value, sem):
+        need("g", "veqp")
+        n = pattern[0][1] * 16
+        done(g.affine_select(out, T.ZER[:, 0:n], pattern, A.not_equal, value, base, 1), sem)
+
+    def marks_a():
+        mark(T.ZN[:], [[-16, 9], [-1000, 16]], 16, 1.0, "gzz")
+        mark(T.ZP[:], [[-16, 9], [-1000, 16]], 15, 1.0, "gzz")
+        for n, wt in enumerate((160.0, -624.0, -159.0)):
+            mark(T.PS[:, n, :], [[-16, 9], [-1000, 2], [-2, 8]], 15, wt, "gps")
+
+    def marks_b():
+        mark(T.SD[:, 1, :], [[-16, 8], [-1, 16]], 1, -4096.0, "gsd0")
+        mark(T.SD[:, 0, :], [[-16, 8], [-1, 16]], 0, 4096.0, "gsd")
+        mark(T.SD[:, 2, :], [[-16, 8], [-1000, 16]], -15, -4096.0, "gsd")
+        need("g", "gsd0")
+        done(g.affine_select(T.SD[:, 1, :], T.SD[:, 1, :], [[0, 8], [1, 16]], A.not_equal, 0.0, 0, 0), "gsd")
+        mark(T.ER[:], [[-16, 8], [0, 16]], -3, 1.0, "ger")
+
+    def marks_c():
+        mark(T.LB[:], [[-16, 9], [-1000, 8], [0, 2]], 16, 1.0, "glb")
+
+    def diags(eng_, o, ds=range(7)):
+        if eng_ == "s":
+            if o == rank:
+                need("s", "dw", "vid")
+                done(S.activation(T.WG[:, 8 * o:8 * o + 7], T.WS[:], COPY), "swg")
+            else:
+                need("s", "wr")
+                done(S.activation(T.WG[:, 8 * o:8 * o + 7], T.WR[:, 8 * o:8 * o + 7], COPY), "swg")
+            need("s", "swg")
+        else:
+            need("v", "wr", "vid")
+        for d in ds:
+            out = T.DG[:, (7 * o + d) * 128:(7 * o + d) * 128 + 128]
+            if eng_ == "s":
+                done(S.activation(out, ident, COPY, scale=T.WG[:, 8 * o + d:8 * o + d + 1]), "sdg")
+            else:
+                done(V.tensor_scalar(out, ident, T.WR[:, 8 * o + d:8 * o + d + 1], None, A.mult), "vdg")
+
+    STEP = {"L0": 3, "L1": 4, "L2": 5, "L3": 6, "M1": 2, "M2": 1, "M3": 0}
+
+    def lst_ap(lst, lo, hi):
+        if lst in ("L1", "M1"):
+            o = NC * (lst == "M1")
+            return T.LM1[:, o + lo // 16:o + hi // 16]
+        return T[lst][:, lo // 16:hi // 16]
+
+    def ready(lst):
+        return "eL1" if lst == "M1" else "e" + lst
+
+    def gather(q, out, win, offs, sem):
+        src = win.indirect(offs)
+        done(S.activation(out, src, COPY) if q == "s" else V.tensor_copy(out, src), sem)
+
+    def pick_x(lst, q, lo=0, hi=NS, tag="", win="X", at=None):
+        at = at or lst
+        need(q, "dx" if win == "X" else "g" + win, ready(at))
+        gather(q, T["X" + lst][:, lo:hi], T[win][:], lst_ap(at, lo, hi), "s" + lst + tag)
+
+    def back(k, q, lo, hi):
+        need(q, "vpv", "dx" if k == 1 else "gXB1")
+        gather(q, T["XB%d" % k][:, lo:hi], (T.X if k == 1 else T.XB1)[:], T.PV[:, lo // 16:hi // 16], "gXB%d" % k)
+
+    def prv_turn():
+        need("v", "dtab")
+        done(V.tensor_copy(T.TX[:], T.TI[:]), "vcv")
+        need("v", "vcv")
+        done(V.transpose(T.TT[:], T.TX[:]), "vtr")
         need("t", "sperm", "vtr")
         for b1 in range(8):
-            bt = b1 % 2
             for ga in range(2):
-                n = 2 * ga + bt
-                ins = P.matmul(T.QT[:, b1:512:8], T.PM[:, 128 * n:128 * n + 128], T.TT[:, b1 // 2:16:4, 16 * ga:16 * ga + 16], ga == 0, ga == 1)
-            if b1 == 7:
-                done(ins, "ptab")
+                n = 2 * ga + b1 % 2
+                ins = P.matmul(T.E0[:, b1:128:8], T.PM[:, 128 * n:128 * n + 128], T.TT[:, b1 // 2, 16 * ga:16 * ga + 16], ga == 0, ga == 1)
+        done(ins, "ptab")
 
-    def gpsimd_selectors():
-        need("g", "vcon")
-        done(g.affine_select(T.ZN[:], T.ONB[:], [[-16, 9], [-1000, 16]], A.is_equal, 0.0, 16, 1), "gsel")
-        done(g.affine_select(T.ZP[:], T.ONB[:], [[-16, 9], [-1000, 16]], A.is_equal, 0.0, 15, 1), "gsel")
-        for ih in range(2):
-            pat, base = [[-16, 8], [1000 if ih else -1000, 2], [0, 8]], -1000 if ih else 0
-            o = slice(128 * ih, 128 * ih + 128)
-            done(g.affine_select(T.ER[:, o], T.C16[:], pat, A.is_equal, 0.0, base - 2, 1), "ges2")
-            done(g.affine_select(T.ES[:, o], T.C16[:], pat, A.is_ge, 0.0, base, 1), "ges")
-        need("g", "ges")
-        for ih in range(2):
-            o = slice(128 * ih, 128 * ih + 128)
-            done(g.affine_select(T.ES[:, o], T.ES[:, o], [[16, 8], [0, 2], [0, 8]], A.is_ge, 0.0, 15, -1), "ges2")
+    def keeps():
+        need("t", "eK", "eM3", "vlate")
+        P.matmul(T.QA[:, 0:128], T.C128[:], T.CNEG[:], True, False)
+        sampled("QA", False, False)
 
-    KEYC, NXTC, PRVC, RWC = 0, 128, 256, 384
-    STEP = {"L0": 3, "L1": 4, "L2": 5, "L3": 6, "M1": 2, "M2": 1, "M3": 0}
-    MASKS = ["vm0", "vm1", "vm2", "vm3"]
+    def pick_p(lst, q, lo=0, hi=NS):
+        need(q, "dpw", ready(lst))
+        gather(q, T["R" + lst][:, lo:hi], T.PW[:], lst_ap(lst, lo, hi), "g" + lst)
 
-    def blocksum(name, bank, sel, rows, first=True):
-        for cl in range(8):
-            ins = P.matmul(T[bank][:, 0:64], T[sel][:, 16 - 2 * cl:144 - 2 * cl], T[rows][:, cl:512:8], first and cl == 0, cl == 7)
-        done(ins, name)
-
-    def wrap(lst, bank, sel, rows):
-        need("t", "gsel")
+    def wrap(lst, bank, sel, rows, first=True):
         for ro in range(16):
-            ins = P.matmul(T[bank][:, 0:64], T[sel][:, 16 - ro:144 - ro], T[rows][:, ro:1024:16], ro == 0, ro == 15)
+            ins = P.matmul(T[bank][:, 0:NC], T[sel][:, 16 - ro:144 - ro], T[rows][:, ro:NS:16], first and ro == 0, ro == 15)
         done(ins, "p" + lst)
+
+    def chase(lst, bank, after):
+        src = lst[0] + str(int(lst[1]) - 1)
+        need("t", "gzz", "g" + src, after)
+        wrap(lst, bank, "ZN" if lst[0] == "L" else "ZP", "R" + src)
 
     def evac(lst, bank):
         need("v", "p" + lst)
-        done(V.tensor_copy(T[lst][:], T[bank][:, 0:64]), "e" + lst)
+        done(V.tensor_copy(T[lst][:], T[bank][:, 0:NC]), "e" + lst)
 
-    def mul(out, col, sem, qs=range(4)):
-        for q in qs:
-            need("v", MASKS[q])
-            done(V.tensor_tensor(T[out][:, 128 * q:128 * q + 128], T.M4[:, 128 * q:128 * q + 128], T.QT[:, col:col + 128], A.mult), sem)
-
-    def pick_x(lst, on_q="s", table="X", at=None):
-        at = at or lst
-        need(on_q, "dx", "e" + at)
-        src = T[table][:].indirect(T[at][:])
-        if on_q == "s":
-            done(S.activation(T["X" + lst][:], src, COPY), "s" + lst)
-        else:
-            done(V.tensor_copy(T["X" + lst][:], src), "s" + lst)
-
-    def pick_p(lst):
-        need("v", "dpw", "e" + lst)
-        done(V.tensor_copy(T["R" + lst][:], T.PW[:].indirect(T[lst][:])), "g" + lst)
-
-    def hsum(lst, k):
-        need("t", "s" + lst)
-        for q in [rank] + others:
+    def hsum(lst, k, qs=None, tag=""):
+        need("t", "s" + lst + tag, "sdg", "vdg")
+        for q in qs or [rank] + others:
             o = (7 * q + STEP[lst]) * 128
-            ins = P.matmul(T["H%d" % q][:, 0:256], T.DG[:, o:o + 128], T["X" + lst][:, 256 * q:256 * q + 256], k == 0, k == 6)
+            ins = P.matmul(T["H%d" % q][:, 0:NQ], T.DG[:, o:o + 128], T["X" + lst][:, NQ * q:NQ * q + NQ], k == 0, k == 6)
             if k == 6:
                 done(ins, "ph%d" % q)
 
-    def esum(sel, rows, last):
-        for ih in range(2):
-            ins = P.matmul(T.QE[:], T[sel][:, 128 * ih:128 * ih + 128], T[rows][:, ih:1024:2], False, last and ih == 1)
-        if last:
-            done(ins, "pE")
+    def reward(rows, sem, first=False):
+        need("t", "ger", sem)
+        for h in range(2):
+            P.matmul(T["E%d" % h][:, 0:320], T.ER[:], T[rows][:, 320 * h:320 * h + 320], first, False)
 
-    def rewards():
-        need("t", "vrw4", "ges2")
-        P.matmul(T.QE[:], ident, T.RW4[:], True, False)
-        esum("ER", "RL1", False)
-        esum("ER", "RL2", False)
+    def sampled(bank, first, last):
+        need("t", "gsd", "sk")
+        P.matmul(T[bank][:, 0:128], T.SD[:, 0, :], T.K1[:, 16:144], first, False)
+        P.matmul(T[bank][:, 0:128], T.SD[:, 1, :], T.K1[:, 16:144], False, False)
+        return P.matmul(T[bank][:, 0:128], T.SD[:, 2, :], T.K1[:, 15:143], False, last)
 
-    def serve(a):
+    def serve(a, q):
         KL, VS, VR = T["KL%d" % a], T["VS%d" % a], T["VR%d" % a]
-        src = lambda c: VS[:, 256 * place(c, core):256 * place(c, core) + 256]
-        dst = lambda c: VR[:, 256 * rank:256 * rank + 256]
-        sem = lambda c: T.sem["vr%d_%d" % (a, rank)]
-        need("s", "dval", "ko%d" % a)
-        done(S.activation(VS[:, 0:256 * half], T.VALB[:].indirect(KL[:, 0:16 * half]), COPY), "gU")
-        need("s", "kr%d" % a, "eO")
-        done(S.activation(VS[:, 256 * half:1024], T.VALB[:].indirect(KL[:, 16 * half:64]), COPY), "gV")
-        need("g", "gU")
-        send(off, src, dst, sem, "vl")
+        need(q, "dval", "kr%d" % a)
+        gather(q, VS[:], T.VALB[:], KL[:, 0:30], "gV")
         need("g", "gV")
-        send(on, src, dst, sem, "vl")
+        send(peers, lambda c: VS[:, NQ * place(c, core):NQ * place(c, core) + NQ], lambda c: VR[:, NQ * rank:NQ * rank + NQ],
+             lambda c: T.sem["vr%d_%d" % (a, rank)], "vl")
         for c in peers:
             tot["vr%d_%d" % (a, T.rank_of(c))] = inc[c]
 
+    def serve_own(a, q):
+        need(q, "dval", "eK")
+        gather(q, T["VR%d" % a][:, NQ * rank:NQ * rank + NQ], T.VALB[:], T["KS%d" % a][:, 10 * rank:10 * rank + 10], "vr%d_%d" % (a, rank))
+
+    def heads():
+        need("t", "gj", "vcon")
+        P.matmul(T.H0[:, 0:128], T.C128[:], T.JI[:, 0:128], True, False)
+        P.matmul(T.H1[:, 0:320], T.C128[:], T.JI[:, 128:448], True, False)
+
+    def tails(pb):
+        need("t", "gtu")
+        done(P.matmul(T.QB[:, 0:128], T.TU[:], pb[:], True, True), "pB")
+
+    def frame_sums():
+        need("v", "pB")
+        done(V.tensor_tensor(T.SS[:], T.CS[:], T.QB[:, 0:128], A.subtract), "vS")
+
+    def counts():
+        need("s", "vS", "vc3")
+        done(S.activation(T.K1[:, 16:144], T.SS[:], IDENT, bias=1024.50390625, scale=1.0 / 128), "sk")
+        done(S.activation(T.K4[:], T.SS[:], IDENT, bias=1025.2509765625, scale=1.0 / 512), "sk")
+        done(S.activation(T.K40[:], T.SS[:], IDENT, bias=129.4751, scale=1.0 / 5120), "sk")
+
+    def pairs_t():
+        need("t", "gps", "sk", "sab")
+        for cp in range(2):
+            for n, src in enumerate((T.K1[:, 16 + cp:144:2], T.K4[:, cp:128:2], T.K40[:, cp:128:2])):
+                ins = P.matmul(T.E0[:, 0:64], T.PS[:, n, 16 - 8 * cp:144 - 8 * cp], src, cp + n == 0, cp + n == 3)
+        done(ins, "pPL")
+        done(sampled("E1", True, True), "pS")
+
+    def pairs_v(pb):
+        need("v", "pPL", "gG0", "gG1")
+        done(V.tensor_scalar(T.PL[:], T.E0[:, 0:64], 496734.0, None, A.add), "ePL")
+        need("v", "pS")
+        done(V.tensor_tensor(T.PK[:], pb[:], T.E1[:, 0:128], A.subtract), "vpk")
+
     for a in range(2):
         pb = T.PB0 if a == 0 else T.PB1
-        KS, KL, VS, VR = T["KS%d" % a], T["KL%d" % a], T["VS%d" % a], T["VR%d" % a]
-        sums(a)
+        KS, KL, VR = T["KS%d" % a], T["KL%d" % a], T["VR%d" % a]
+        if a:
+            heads()
+        need("t", "vbo", "vpb", "vP")
+        done(P.matmul(T.QA[:, 0:128], bo, pb[:], True, True), "pA")
+        if a:
+            tails(pb)
+        else:
+            heads()
         need("v", "pA", "vone")
         done(V.tensor_tensor_scan(T.CS[:], T.ONE[:], T.QA[:, 0:128], 0.0, A.mult, A.add), "vscan")
-        need("v", "pB", "vscan")
-        done(V.tensor_tensor(T.SI[:], T.CS[:], T.QB[:, 0:128], A.add), "vS")
-        need("v", "vS")
-        done(V.tensor_scalar(T.RI[:], T.SI[:], 127, None, A.bitwise_and), "vr")
-        done(V.tensor_scalar(T.K2[:], T.SI[:], 6, 6, A.arith_shift_right, A.bitwise_and), "vr")
+        need("v", "vscan")
+        need("s", "vscan")
+        done(S.activation(T.NA[:], T.CS[:], IDENT, bias=-128.5001 / 16, scale=-1.0 / 81920), "vna")
+        done(V.tensor_scalar(T.NK[:], T.CS[:], -1.0 / 2048, -1024.50390625 / 16, A.mult, A.add), "vnk")
+        if a:
+            back(2, "s", 0, 256)
+        need("t", "vnk", "vby")
+        P.matmul(T.H1[:, 0:320], T.NK[:], T.BY[:], False, False)
+        need("t", "vna", "sbz")
+        done(P.matmul(T.H1[:, 0:320], T.NA[:], T.BZ[:], False, True), "pY")
+        done(P.matmul(T.H0[:, 0:128], T.NA[:], bo, False, True), "pX")
         if a == 0:
-            need("v", "dtab")
-            done(V.tensor_scalar(T.TX[:, 0:4, :], T.TI[:, 0:4, :], 2048.0, None, A.subtract), "vcv")
-            done(V.tensor_copy(T.TX[:, 4:16, :], T.TI[:, 4:16, :]), "vcv")
-        need("v", "vr")
-        done(V.tensor_tensor(T.NF[:], T.RI[:], pb[:], A.is_ge), "vnf")
+            consts_a()
+        else:
+            frame_sums()
+        need("v", "pX", "veqp")
+        done(V.tensor_scalar(T.EQP[:, :, 16:32], T.H0[:, 0:128], -129.0, 0.5, A.is_equal, A.mult), "veq")
+        done(V.tensor_scalar(T.UU[:], T.H0[:, 0:128], -129.5, -128.5, A.max, A.min), "vuu")
+        need("s", "pY")
+        done(S.activation(T.SG[:], T.H1[:, 0:320], AF.Sign, bias=-4134.5), "ssg")
+        need("t", "veqp")
+        P.matmul(T.H2[:, 0:NC], bo, T.ZER[:, 0:NC], True, False)
+        need("t", "veq", "ssg")
+        for gr in range(8):
+            lo = 16 - 16 * (gr % 2)
+            P.matmul(T.H2[32 * (gr // 2):32 * (gr // 2) + 32, 0:NC], T.EQP[:, gr, lo:lo + 32], T.SG[:, NC * gr:NC * gr + NC], False, False)
+        need("t", "vuu")
+        done(P.matmul(T.H2[:, 0:NC], T.UU[:], T.ONB[:], False, True), "pC")
         if a == 0:
-            need("v", "vcv")
-            done(V.transpose(T.TT[:], T.TX[:]), "vtr")
-            tables_out()
-        need("v", "vnf")
-        done(V.tensor_tensor(T.CODE[:], T.K2[:], T.NF[:], A.add), "vcode")
-        need("v", "vcode")
-        for q in range(4):
-            done(V.tensor_scalar(T.M4[:, 128 * q:128 * q + 128], T.CODE[:], float(2 * ((q + 1) % 4)), None, A.is_equal), MASKS[q])
-        need("t", "vz4", "vid", "vscan", *MASKS)
-        P.matmul(T.QA[:, 0:64], ident, T.T8H[:], True, False)
-        blocksum("pL0", "QA", "Z2T", "M4", False)
-        need("v", "ptab")
-        mul("MK", KEYC, "vmk")
-        need("t", "vmk", "vS")
-        blocksum("pK", "QB", "Z2", "MK")
-        evac("L0", "QA")
-        pick_x("L0")
-        mul("MN", NXTC, "vmn", (0, 1))
+            tails(pb)
+            consts_b()
+            marks_a()
+            perms()
+            diags("s", rank)
+        need("v", "pC")
+        done(V.tensor_scalar(T.COL[:], T.H2[:, 0:NC], 16576.0, 127.0, A.add, A.min), "eC")
+        done(V.tensor_scalar(T.C16[:], T.H2[:, 0:NC], 16576.0, 16.0, A.add, A.mult), "eC16")
+        if a == 0:
+            frame_sums()
+        counts()
+        need("v", "eC", "vS", "gthr")
+        done(V.tensor_tensor(T.CM[:], T.SS[:].indirect(T.COL[:]), T.THR[:], A.is_lt), "vcm")
+        need("t", "eC16", "vid", "vza")
+        P.matmul(T.H3[:, 0:NC], ident, T.C16[:], True, False)
+        if a:
+            pairs_t()
+            back(2, "s", 256, 1536)
+        need("t", "vcm")
+        wrap("L0", "H3", "ZA", "CM", False)
+        if a == 0:
+            prv_turn()
+        else:
+            pairs_v(pb)
+            back(2, "v", 1536, 1792)
+        need("v", "pL0")
+        done(V.tensor_scalar(T.L0[:], T.H3[:, 0:NC], 2047.0, None, A.min), "eL0")
+        need("v", "eL0", "dpw", "vc3")
+        done(V.tensor_scalar(T.R0[:, 0:320], T.PW[:].indirect(T.L0[:, 0:20]), cg(1), None, A.add), "gR0")
+        need("s", "eL0", "dpw", "vc3")
+        done(S.activation(T.R0[:, 320:NS], T.PW[:].indirect(T.L0[:, 20:40]), IDENT, bias=cg(1)), "gR0")
+        pick_x("L0", "s")
+        need("v", "gR0")
+        done(V.transpose(T.RT[:], T.R0[:]), "vrt")
+        need("t", "vrt", "sperm", "vscan", "vS")
+        for bank, col, row, sem in (("QA", 0, 2, "pK"), ("QB", 0, 0, None), ("QB", NC, 1, "pL1")):
+            for h in range(2):
+                for gb in range(2):
+                    n = 2 * gb + h
+                    ins = P.matmul(T[bank][:, col + h:col + NC:2], T.PM[:, 128 * n:128 * n + 128], T.RT[:, :, 16 * gb + row], gb == 0, gb == 1)
+            if sem:
+                done(ins, sem)
+        if a == 0:
+            need("v", "ptab")
+            done(V.tensor_copy(T.PV[:], T.E0[:, 0:128]), "vpv")
         need("v", "pK")
-        done(V.tensor_scalar(KS[:], T.QB[:, 0:64], 2048.0, None, A.add), "eK")
+        done(V.tensor_scalar(KS[:], T.QA[:, 0:NC], 2048.0, None, A.add), "eK")
         need("g", "eK")
-        send(peers, lambda c: KS[:, 16 * T.rank_of(c):16 * T.rank_of(c) + 16], lambda c: KL[:, 16 * place(core, c):16 * place(core, c) + 16],
-             lambda c: T.sem[("ko%d" if c in off else "kr%d") % a], "kl")
-        tot["ko%d" % a] = sum(inc[c] for c in off)
-        tot["kr%d" % a] = sum(inc[c] for c in on)
-        mul("MN", NXTC, "vmn", (2, 3))
-        need("t", "vmn", "eL0")
-        blocksum("pL1", "QA", "Z2", "MN")
-        mine = 16 * place(core, core)
-        done(V.tensor_scalar(KL[:, mine:mine + 16], T.QB[:, 16 * rank:16 * rank + 16], 2048.0, None, A.add), "eO")
+        send(peers, lambda c: KS[:, 10 * T.rank_of(c):10 * T.rank_of(c) + 10], lambda c: KL[:, 10 * place(core, c):10 * place(core, c) + 10],
+             lambda c: T.sem["kr%d" % a], "kl")
+        tot["kr%d" % a] = sum(inc.values())
         if a == 0:
-            done(V.memset(T.ONB[:], 1.0), "vcon")
-            done(V.memset(T.C16[:], 0.0625), "vcon")
-            gpsimd_selectors()
-        mul("MP", PRVC, "vmp")
-        need("t", "vmp", "eK", "eO")
-        blocksum("pM1", "QB", "Z2", "MP")
-        evac("L1", "QA")
-        pick_p("L1")
+            marks_b()
+        need("v", "pL1")
+        done(V.tensor_copy(T.LM1[:], T.QB[:, 0:2 * NC]), "eL1")
+        need("t", "eC16", "eL0", "vuu", "ssg")
+        halves = [(h, [q for q in [rank] + others if q // 2 == h]) for h in (rank // 2, 1 - rank // 2)]
         if a == 0:
-            evac("M1", "QB")
-            pick_p("M1")
-            need("t", "eL1", "gL1")
-            wrap("L2", "QA", "ZN", "RL1")
-            need("s", "wr")
-            o = others[0]
-            done(S.activation(T.WG[:, 0:7], T.WR[:, 8 * o:8 * o + 7], COPY), "swg")
-            need("s", "swg")
-            for d in range(7):
-                done(S.activation(T.DG[:, (7 * o + d) * 128:(7 * o + d) * 128 + 128], ident, COPY, scale=T.WG[:, d:d + 1]), "sdg2")
-            pick_x("L1")
-            pick_x("M1")
-            serve(a)
-            evac("L2", "QA")
-            pick_x("L2")
-            need("t", "eM1", "gM1")
-            wrap("M2", "QB", "ZP", "RM1")
-            need("v", "wr")
-            for o in others[1:]:
-                for d in range(7):
-                    done(V.tensor_scalar(T.DG[:, (7 * o + d) * 128:(7 * o + d) * 128 + 128], ident, T.WR[:, 8 * o + d:8 * o + d + 1], None, A.mult), "vdg")
-            pick_p("L2")
-            evac("M2", "QB")
-            pick_p("M2")
-            pick_x("M2")
-            need("t", "sdg", "sdg2", "vdg")
+            pick_p("M1", "v")
+            pick_p("L1", "s")
+            chase("M2", "QA", "eK")
+            chase("L2", "QB", "eL1")
+            pick_x("L1", "s")
+            diags("v", others[0])
+            evac("M2", "QA")
+            done(V.memset(T.CNEG[:], -4224.0), "vlate")
+            evac("L2", "QB")
+            need("t", "vpv")
+            pairs_t()
+            serve(a, "s")
+            marks_c()
+            pick_p("L2", "v")
+            pick_p("M2", "s")
+            chase("L3", "QB", "eL2")
+            chase("M3", "QA", "eM2")
+            diags("v", others[1])
+            diags("v", others[2])
+            pick_x("M1", "s")
+            evac("L3", "QB")
+            evac("M3", "QA")
             hsum("L0", 0)
             hsum("L1", 1)
-            need("t", "eL2", "gL2")
-            wrap("L3", "QA", "ZN", "RL2")
-            hsum("M1", 2)
-            evac("L3", "QA")
-            pick_x("L3")
-            need("t", "eM2", "gM2")
-            wrap("M3", "QB", "ZP", "RM2")
-            done(V.tensor_copy(T.PV[:], T.QT[:, PRVC:PRVC + 128]), "vpv")
-            for q in range(4):
-                done(V.tensor_scalar(T.RW4[:, 128 * q:128 * q + 128], T.QT[:, RWC:RWC + 128], 0.0625, None, A.mult), "vrw4")
-            hsum("L2", 3)
-            rewards()
-            evac("M3", "QB")
-            pick_x("M3", "v")
-            need("s", "vpv")
-            done(S.activation(T.XT1[:], T.X[:].indirect(T.PV[:]), COPY), "st1")
-            need("s", "st1")
-            done(S.activation(T.XT2[:], T.XT1[:].indirect(T.PV[:]), COPY), "st2")
-            done(V.tensor_tensor(T.PK[:], T.NF[:], pb[:], A.mult), "vpk")
-            hsum("M2", 4)
-            hsum("M3", 5)
-            hsum("L3", 6)
-        else:
-            need("s", "st1", "st2")
-            pick_x("M1", "s", "XT1", "L0")
-            pick_x("M2", "s", "XT2", "L0")
-            serve(a)
-            hsum("L0", 0)
-            need("t", "eL1", "gL1")
-            wrap("L2", "QA", "ZN", "RL1")
-            hsum("M1", 1)
-            evac("L2", "QA")
-            evac("M1", "QB")
-            pick_x("M3", "s", "XT2", "M1")
-            pick_x("L1", "s")
-            pick_p("L2")
+            pairs_v(pb)
             pick_x("L2", "v")
-            hsum("M2", 2)
-            need("t", "eL2", "gL2")
-            wrap("L3", "QA", "ZN", "RL2")
-            rewards()
-            evac("L3", "QA")
-            pick_x("L3", "v")
-            done(V.tensor_tensor(T.PK[:], T.NF[:], pb[:], A.mult), "vpk")
-            hsum("M3", 3)
-            hsum("L2", 4)
-            hsum("L1", 5)
-            hsum("L3", 6)
-        need("v", "vpk")
-        done(V.tensor_scalar(T.KEEP[:], T.PK[:], 1.0, None, A.max), "vkeep")
-        for q in [rank] + others:
-            need("v", "ph%d" % q, "gV" if q == rank else "vr%d_%d" % (a, q))
-            src = VS[:, 256 * place(core, core):256 * place(core, core) + 256] if q == rank else VR[:, 256 * q:256 * q + 256]
-            done(V.tensor_tensor(T.PROD[:, 256 * q:256 * q + 256], src, T["H%d" % q][:, 0:256], A.mult), "vpr")
-        need("t", "vpr")
-        esum("ES", "PROD", True)
-        need("v", "pE")
-        done(V.tensor_tensor(T.EM[:], T.M4[:, 0:256], T.QE[:, 0:256], A.mult), "vem")
-        done(V.tensor_tensor(T.QA[:, 0:256], T.M4[:, 256:512], T.QE[:, 256:512], A.mult), "vem")
-        need("v", "vem")
-        done(V.tensor_tensor(T.QB[:, 0:128], T.EM[:, 128:256], T.QA[:, 128:256], A.add), "va1")
-        done(V.tensor_tensor(T.EA[:], T.EM[:, 0:128], T.QA[:, 0:128], A.add), "va1")
-        need("v", "va1")
-        done(V.tensor_tensor(T.EB[:], T.EA[:], T.QB[:, 0:128], A.add), "va2")
-        if a == 0:
-            need("v", "va2")
-            done(V.tensor_scalar(T.EC[:], T.EB[:], -1.0, None, A.mult), "va3")
-            need("v", "va3")
-            done(V.tensor_tensor(T.AB[:], T.EB[:], T.EC[:], A.max), "vab")
+            pick_x("M2", "s")
+            serve_own(a, "v")
+            hsum("M1", 2)
+            need("t", "ePL", "vpk")
+            reward("R0", "gR0", True)
+            reward("RL1", "gL1")
+            reward("RL2", "gL2")
+            hsum("L2", 3)
+            keeps()
+            hsum("M2", 4)
+            last = (("M3", "v", "X", "M3"), ("L3", "s", "X", "L3"))
         else:
-            need("s", "va2")
-            done(S.activation(T.AB[:], T.EB[:], ABS), "vab")
-        need("v", "vab", "vkeep")
-        done(V.tensor_scalar(T.NI[:], T.AB[:], 0.46875, 63.0, A.subtract, A.min), "vni")
-        need("v", "vni")
-        done(V.tensor_tensor((T.YO if a else T.PB1)[:], T.NI[:], T.KEEP[:], A.max), "vP")
+            pick_p("L1", "v")
+            pick_x("M1", "s")
+            hsum("L0", 0)
+            need("t", "ePL", "vpk")
+            reward("R0", "gR0", True)
+            chase("L2", "QB", "eL1")
+            keeps()
+            pick_x("L1", "v")
+            evac("L2", "QB")
+            back(2, "s", 1792, 2048)
+            serve(a, "s")
+            pick_p("L2", "v")
+            pick_x("M2", "s", win="XB1", at="M1")
+            hsum("M1", 1)
+            reward("RL1", "gL1")
+            hsum("L1", 2)
+            chase("L3", "QB", "eL2")
+            serve_own(a, "v")
+            pick_x("L2", "s")
+            reward("RL2", "gL2")
+            hsum("M2", 3)
+            pick_x("M3", "v", 0, 320, "", "XB2", "M1")
+            evac("L3", "QB")
+            pick_x("M3", "v", 320, NS, "", "XB2", "M1")
+            hsum("L2", 4)
+            hsum("M3", 5)
+            last = (("L3", "s", "X", "L3"),)
+        for tag, (h, qs) in zip(("", "b"), halves):
+            for lst, q, win, at in last:
+                pick_x(lst, "v" if a and tag else q, 320 * h, 320 * h + 320, tag, win, at)
+            for k, (lst, q, win, at) in enumerate(last):
+                hsum(lst, 7 - len(last) + k, qs, tag)
+        if a == 0:
+            back(1, "s", 0, 768)
+        for h, qs in halves:
+            for q in qs:
+                need("v", "ph%d" % q, "vr%d_%d" % (a, q))
+                done(V.tensor_tensor(T.PROD[:, NQ * q:NQ * q + NQ], VR[:, NQ * q:NQ * q + NQ], T["H%d" % q][:, 0:NQ], A.mult), "vpr%d" % h)
+            need("t", "vpr%d" % h)
+            done(P.matmul(T["E%d" % h][:, 0:320], bo, T.PROD[:, 320 * h:320 * h + 320], False, True), "pE%d" % h)
+            need("s", "pE%d" % h)
+            done(S.activation(T.AB[:, 320 * h:320 * h + 320], T["E%d" % h][:, 0:320], AF.Abs, scale=0.0625), "sab")
+        if a == 0:
+            back(1, "v", 768, 1152)
+        need("v", "sab", "ePL")
+        need("s", "sab", "ePL")
+        for b in range(2):
+            lo = 512 * b
+            done(V.tensor_scalar(T.GB[:, lo:lo + 256], T.AB[:].indirect(T.PL[:, lo // 16:lo // 16 + 16]), 127.53125, None, A.add), "gG%d" % b)
+            done(S.activation(T.GB[:, lo + 256:lo + 512], T.AB[:].indirect(T.PL[:, lo // 16 + 16:lo // 16 + 32]), IDENT, bias=127.53125), "gG%d" % b)
+            need("t", "gG%d" % b, "glb")
+            for h in range(8):
+                ins = P.matmul(T.QA[:, 64 * b:64 * b + 64], T.LB[:, 16 - 2 * h:144 - 2 * h], T.GB[:, lo + h:lo + 512:8], False, b == 1 and h == 7)
+        done(ins, "pO")
+        if a == 0:
+            back(1, "v", 1152, 1408)
+            back(1, "s", 1408, 2048)
+        need("v", "pO")
+        done(V.tensor_scalar(T.QB[:, 0:128], T.QA[:, 0:128], 1.0, 63.0, A.max, A.min), "vni")
+        need("v", "vni", "vpk")
+        done(V.tensor_tensor((T.YO if a else T.PB1)[:], T.QB[:, 0:128], T.PK[:], A.max), "vP")
     need("y", "vP")
     done(g.sync.dma_start(T.y[:], T.YO[:]), "dy", 16)
     need("y", "dy")

@@ -6,42 +6,42 @@ NS, NC, NQ = 640, 40, 160
 LISTS = ["L0", "L1", "M1", "L2", "M2", "L3", "M3"]
 SCRATCH = {
     "PRI": ("sbuf", [128, 128], I32), "PB0": ("sbuf", [128, 128], BF), "PB1": ("sbuf", [128, 128], BF),
-    "X": ("sbuf", [128, 2048], BF), "VALB": ("sbuf", [128, 4096], BF), "PW": ("sbuf", [128, 2048], I32),
+    "X": ("sbuf", [128, 2048], BF), "VALB": ("sbuf", [128, 8192], BF), "KO": ("sbuf", [128, NC], BF), "PW": ("sbuf", [128, 2048], I32),
     "IM": ("sbuf", [128, 160], I32), "I16": ("sbuf", [128, 128], I32), "KP": ("sbuf", [128, 1], I32), "THR": ("sbuf", [128, NS], I32),
     "CI": ("sbuf", [128, 8], I32), "CF": ("sbuf", [128, 8], F32), "CG": ("sbuf", [128, 8], F32),
     "BO": ("sbuf", [128, 8, 16], BF), "TU": ("sbuf", [128, 128], BF), "IDW": ("sbuf", [128, 160], BF), "ONB": ("sbuf", [128, NC], BF),
-    "BY": ("sbuf", [128, 8, NC], BF), "BZ": ("sbuf", [128, 8, NC], BF), "JI": ("sbuf", [128, 448], BF), "C128": ("sbuf", [128, 128], BF),
-    "CNEG": ("sbuf", [128, 128], BF), "ZER": ("sbuf", [128, 144], BF), "EQP": ("sbuf", [128, 8, 48], BF), "UU": ("sbuf", [128, 128], F16),
+    "BY": ("sbuf", [128, 8, NC], BF), "BX": ("sbuf", [128, 128], BF), "C1K": ("sbuf", [128, 128], BF), "CK": ("sbuf", [128, 4], F32), "JI": ("sbuf", [128, 448], BF), "C128": ("sbuf", [128, 128], BF),
+    "CNEG": ("sbuf", [128, 128], BF), "ZER": ("sbuf", [128, 144], BF), "EQP": ("sbuf", [128, 8, 48], BF), "UU": ("sbuf", [128, 128], BF),
     "SG": ("sbuf", [128, 8 * NC], BF), "PM": ("sbuf", [128, 512], BF), "ZA": ("sbuf", [128, 144], BF), "ZN": ("sbuf", [128, 144], BF),
-    "ZP": ("sbuf", [128, 144], BF), "ER": ("sbuf", [128, 128], BF), "LB": ("sbuf", [128, 144], BF), "PS": ("sbuf", [128, 3, 144], BF),
-    "SD": ("sbuf", [128, 3, 128], BF),
+    "BS": ("sbuf", [128, 128], BF), "KEEP": ("sbuf", [128, 128], F32), "ER": ("sbuf", [128, 128], BF), "LB": ("sbuf", [128, 144], BF),
+    "PS": ("sbuf", [128, 3, 144], BF), "SD": ("sbuf", [128, 3, 128], BF),
     "ONE": ("sbuf", [128, 128], F32), "CS": ("sbuf", [128, 128], F32), "SS": ("sbuf", [128, 128], F32),
-    "NA": ("sbuf", [128, 128], BF), "NK": ("sbuf", [128, 128], F16), "K1": ("sbuf", [128, 144], F16), "K4": ("sbuf", [128, 128], F16),
+    "KA": ("sbuf", [128, 128], F16), "K1": ("sbuf", [128, 144], F16), "K4": ("sbuf", [128, 128], F16),
     "K40": ("sbuf", [128, 128], BF), "COL": ("sbuf", [128, NC], U16), "C16": ("sbuf", [128, NC], F16), "CM": ("sbuf", [128, NS], BF),
-    "R0": ("sbuf", [128, NS], F16), "RT": ("sbuf", [128, NS // 32, 32], F16), "LM1": ("sbuf", [128, 2 * NC], U16),
+    "R0": ("sbuf", [128, NS], F16), "RT": ("sbuf", [128, NS // 32, 32], F16), "L0": ("sbuf", [128, NC], U16),
     "KS0": ("sbuf", [128, NC], U16), "KS1": ("sbuf", [128, NC], U16), "KL0": ("sbuf", [128, 32], U16), "KL1": ("sbuf", [128, 32], U16),
-    "VS0": ("sbuf", [128, 3 * NQ], BF), "VS1": ("sbuf", [128, 3 * NQ], BF), "VR0": ("sbuf", [128, NS], BF), "VR1": ("sbuf", [128, NS], BF),
+    "VS0": ("sbuf", [128, 3 * NQ], BF), "VS1": ("sbuf", [128, 2 * NQ], BF), "VR0": ("sbuf", [128, NS], BF), "VR1": ("sbuf", [128, NS], BF),
     "PROD": ("sbuf", [128, NS], F16), "AB": ("sbuf", [128, NS], F32), "PL": ("sbuf", [128, 64], U16), "GB": ("sbuf", [128, 1024], BF),
     "PK": ("sbuf", [128, 128], F32), "YO": ("sbuf", [128, 128], F32),
-    "WS": ("sbuf", [128, 7], BF), "WF": ("sbuf", [128, 7], F32), "WR": ("sbuf", [128, 32], BF), "WG": ("sbuf", [128, 32], F32),
-    "DG": ("sbuf", [128, 28 * 128], BF), "TI": ("sbuf", [128, 4, 32], I32), "TX": ("sbuf", [128, 4, 32], F16), "TT": ("sbuf", [128, 4, 32], F16),
-    "PV": ("sbuf", [128, 128], U16), "XB1": ("sbuf", [128, 2048], BF), "XB2": ("sbuf", [128, 2048], BF),
+    "WS": ("sbuf", [128, 7], BF), "WF": ("sbuf", [128, 7], F32), "WR": ("sbuf", [128, 32], BF),
+    "DG": ("sbuf", [128, 28 * 128], BF), "TI": ("sbuf", [128, 8, 32], I32), "TX": ("sbuf", [128, 8, 32], F16), "TT": ("sbuf", [128, 8, 32], F16),
+    "PV": ("sbuf", [128, 256], U16), "PN": ("sbuf", [128, 2048], I32), "XB": ("sbuf", [128, 2048], BF),
 }
 for _n in LISTS:
     SCRATCH["X" + _n] = ("sbuf", [128, NS], BF)
-for _n in ["L0", "L2", "M2", "L3", "M3"]:
-    SCRATCH[_n] = ("sbuf", [128, NC], U16)
-for _n in LISTS[1:5]:
-    SCRATCH["R" + _n] = ("sbuf", [128, NS], F16)
+for _n in "123":
+    SCRATCH["LM" + _n] = ("sbuf", [128, 3 * NC], U16)
+for _n in "12":
+    SCRATCH["R" + _n] = ("sbuf", [128, 2, NS], F16)
 for _n in ["QA", "QB", "E0", "E1", "H0", "H1", "H2", "H3"]:
     SCRATCH[_n] = ("psum", [128, 512], F32)
-SEMAPHORES = (["dpri", "dw", "dx", "dval", "dpw", "dy", "gi", "gj", "gtu", "gthr", "glb", "gps", "gzz", "ger", "gsd", "gsd0", "vz", "sz", "vcon", "vc",
-               "vc2", "vc3", "vi8", "vbo", "vby", "sbz", "vpb", "vid", "vone", "veqp", "vza", "vlate", "sperm", "vscan", "vS", "vna", "vnk", "veq",
-               "vuu", "ssg", "sk", "eC", "eC16", "vcm", "gR0", "vrt", "eK", "gV", "vdg", "vpk", "ePL", "vpr0", "vpr1", "sab", "gG0", "gG1", "vni", "vP",
-               "pA", "pB", "pX", "pY", "pC", "pK", "pPL", "pS", "ph0", "ph1", "ph2", "ph3", "pE0", "pE1", "pO", "swf", "sdg", "swg", "sdg2",
-               "sM3b", "sL3b", "dtab", "vcv", "vtr", "ptab", "vpv", "gXB1", "gXB2", "wl", "wr", "kl", "vl", "kr0", "kr1"]
-              + ["e" + n for n in LISTS] + ["p" + n for n in LISTS] + ["s" + n for n in LISTS] + ["g" + n for n in LISTS[1:5]]
-              + ["vr%d_%d" % (a, q) for a in range(2) for q in range(4)])
+SEMAPHORES = (["dpri", "dw", "dx", "dval", "dpw", "dy", "dtab", "gi", "gj", "gtu", "gthr", "glb0", "glb", "gps", "gz0", "gzz", "gsd0", "gsd", "gko",
+               "vz", "sz", "vcon", "vc", "vc2", "vc3", "vi8", "vbo", "vby", "vck", "vpb", "vid", "vone", "veqp", "vza", "vlate", "sperm", "sbs", "ser",
+               "vscan", "vS", "vka", "vpr2", "pE2", "veq", "vuu", "ssg", "sk", "eC", "eC16", "vcm", "gR0", "gR1", "gR2", "vrt", "eK", "gV", "vpk", "vkeep",
+               "ePL", "vpr0", "vpr1", "vab", "gG0", "gG1", "vP", "pA", "pB", "pX", "pY", "pC", "pK", "pPL", "pS", "ph0", "ph1", "ph2", "ph3",
+               "pE0", "pE1", "pO", "swf", "sdg", "vcv", "vtr", "ptab", "vpv", "gXB", "gPN", "dpn", "gz4", "tl", "tr", "wl", "wr", "kl", "vl", "kr0", "kr1",
+               "eL0", "eL1", "eL2", "eL3", "pL0", "pL1", "pL2", "pL3", "vr0_0", "vr0_1", "vr0_2", "vr0_3", "vr1_0", "vr1_1"]
+              + ["w" + n for n in LISTS] + ["s" + n for n in LISTS] + ["s" + n + k for n in ("L3", "M3") for k in "bc"])
 
 
 def rank_program(g, core, T, topo):
@@ -89,8 +89,11 @@ def rank_program(g, core, T, topo):
     others = [T.rank_of(c) for c in peers]
     eng = engines_of(core)
     inc = {c: len(engines_of(c)[core]) for c in peers}
+    twin = [c for c in off if topo.die(c) == topo.die(core)][0]
+    wide = {twin: topo.engines(core, twin)}
+    mine, theirs = rank // 2, 1 - rank // 2
 
-    def send(to, src_of, dst_of, sem_of, local):
+    def send(to, src_of, dst_of, sem_of, local, eng=eng):
         tr = []
         for c in to:
             rid, pid = topo.addr(c, core)
@@ -101,14 +104,16 @@ def rank_program(g, core, T, topo):
         g.remote_dma_fused(tr, local_sem=T.sem[local])
         tot[local] = tot.get(local, 0) + sum(len(eng[c]) for c in to)
 
+    own_val = T.VALB[:, 4096 * (rank % 2):4096 * (rank % 2) + 4096]
     done(g.sync.dma_start(T.PRI[:], T.pri[:]), "dpri", 16)
     done(S.dma_start(T.WS[:], T.w[:]), "dw", 16)
-    done(g.sync.dma_start(T.TI[:], T.prv[:]), "dtab", 16)
-    done(S.dma_start(T.X[:], T.x[:]), "dx", 16)
+    done(g.sync.dma_start(T.TI[:, 0:4, :], T.prv[:]), "dtab", 16)
+    done(S.dma_start(T.TI[:, 4:8, :], T.nxt[:]), "dtab", 16)
+    done(g.sync.dma_start(T.X[:], T.x[:]), "dx", 16)
 
     done(g.iota(T.KP[:], [[0, 1]], 0, 1), "gi")
     done(g.iota(T.IM[:], [[1, 160]], -16, 0), "gi")
-    done(g.iota(T.JI[:, 0:128], [[0, 8], [1, 16]], 0, 0, allow_small_or_imprecise_dtypes=True), "gj")
+    done(g.iota(T.JI[:, 0:128], [[0, 8], [1, 16]], 1, 0, allow_small_or_imprecise_dtypes=True), "gj")
     done(g.iota(T.JI[:, 128:448], [[0, 8], [1, 4], [4, 10]], 0, 0, allow_small_or_imprecise_dtypes=True), "gj")
 
     done(V.memset(T.PW[:, 0:384], 0), "vz")
@@ -119,7 +124,7 @@ def rank_program(g, core, T, topo):
     need("y", "vz", "sz")
     for k, n in enumerate(["nxt", "prv", "key", "rw"]):
         done(g.sync.dma_start(T.PW[k:128:16, :], T[n][:]), "dpw", 16)
-    done(g.sync.dma_start(T.VALB[:], T.val[:]), "dval", 16)
+    done(g.sync.dma_start(own_val, T.val[:]), "dval", 16)
 
     kp = T.KP[:]
     m = T.IM[:, 16:144]
@@ -127,107 +132,121 @@ def rank_program(g, core, T, topo):
     bo = T.BO[:]
     cf = lambda j: T.CF[:, j:j + 1]
     cg = lambda j: T.CG[:, j:j + 1]
+    ck = lambda j: T.CK[:, j:j + 1]
 
     def bits(j, sh, msk):
         done(V.tensor_scalar(T.CI[:, j:j + 1], kp, sh, msk, A.logical_shift_right, A.bitwise_and), "vc")
 
     done(V.memset(T.ONE[:], 1.0), "vone")
     done(V.memset(T.C128[:], 1.0 / 128), "vcon")
+    done(V.memset(T.C1K[:], 1024.0), "vcon")
+    done(V.memset(T.EQP[:], 0.0), "veqp")
     need("v", "gi")
     bits(0, 4, 7)
     done(V.tensor_scalar(T.I16[:], m, 4, None, A.logical_shift_right), "vi8")
     bits(2, 0, 127)
     bits(1, 4, 1)
+    bits(3, 0, 15)
+    bits(4, 0, 112)
+    bits(5, 0, 3)
+    bits(6, 3, 1)
     need("v", "vc")
-    done(V.tensor_copy(T.CF[:, 0:3], T.CI[:, 0:3]), "vc2")
+    done(V.tensor_copy(T.CF[:, 0:7], T.CI[:, 0:7]), "vc2")
+    done(V.memset(T.ZER[:], 0.0), "veqp")
+    done(V.memset(T.ONB[:], 1.0), "veqp")
     need("v", "vc2", "vi8")
     done(V.tensor_scalar(bo, T.I16[:], cf(0), None, A.is_equal), "vbo")
+    done(V.tensor_scalar(ck(0), cf(6), -5.125, 5.0, A.mult, A.add), "vck")
+    done(V.tensor_scalar(ck(1), cf(6), 0.125, -0.125, A.mult, A.add), "vck")
     need("v", "dpri")
     done(V.tensor_copy(T.PB0[:], T.PRI[:]), "vpb")
-    need("v", "vbo")
+    done(V.tensor_scalar(ck(2), cf(6), 1.0 / 128, 1.0 / 5120, A.mult, A.max), "vck")
+    done(V.tensor_scalar(ck(3), cf(6), 1024.50390625, 1024.5001220703125, A.mult, A.max), "vck")
+    need("v", "vbo", "vck")
     for lo, n in ((0, 16), (16, 16), (32, 8)):
-        done(V.tensor_copy(T.BY[:, :, lo:lo + n], T.BO[:, :, 0:n]), "vby")
+        done(V.tensor_scalar(T.BY[:, :, lo:lo + n], T.BO[:, :, 0:n], ck(0), None, A.mult), "vby")
+    done(V.tensor_scalar(T.BX[:], bo, ck(1), None, A.mult), "vby")
     need("g", "vbo")
     done(g.affine_select(T.TU[:], bo, [[-1, 128]], A.is_gt, 0.0, 0, 1), "gtu")
     done(g.iota(T.THR[:], [[128, 4], [512, 10], [5120, 16]], 128, 0), "gthr")
     need("g", "dw")
     send(peers, lambda c: T.WS[:], lambda c: T.WR[:, 8 * rank:8 * rank + 7], lambda c: T.sem.wr, "wl")
     tot["wr"] = sum(inc.values())
-    need("s", "vby")
-    done(S.activation(T.BZ[:], T.BY[:], COPY, scale=-40.0), "sbz")
 
     def consts_a():
         done(V.tensor_scalar(T.IDW[:], T.IM[:], cf(2), None, A.is_equal), "vid")
         done(V.tensor_scalar(cg(0), cf(1), 0.0, None, A.is_equal), "vid")
-        done(V.memset(T.EQP[:], 0.0), "veqp")
-        done(V.memset(T.ZER[:], 0.0), "veqp")
-        done(V.memset(T.ONB[:], 1.0), "veqp")
+        done(V.tensor_scalar(T.ZA[:], T.IM[:, 0:144], cf(4), None, A.is_equal), "vza")
+        done(V.memset(T.K1[:, 0:16], 1025.0), "vc3")
 
     def consts_b():
-        bits(3, 0, 15)
-        bits(4, 0, 112)
-        done(V.memset(T.K1[:, 0:16], 1025.0), "vc3")
-        need("v", "vc")
-        done(V.tensor_copy(T.CF[:, 3:5], T.CI[:, 3:5]), "vc2")
-        need("v", "vc2")
-        done(V.tensor_scalar(T.ZA[:], T.IM[:, 0:144], cf(4), None, A.is_equal), "vza")
         done(V.tensor_scalar(cg(1), cf(3), 2.0, -2048.0, A.is_equal, A.mult), "vc3")
+        done(V.tensor_scalar(cg(2), cf(3), 1.0, None, A.not_equal), "vc3")
+        done(V.tensor_scalar(cg(3), cf(3), 1.0, None, A.is_equal), "vc3")
+        done(V.tensor_scalar(cg(4), cf(5), 3.0, None, A.is_equal), "vc3")
+        done(V.tensor_scalar(cg(5), cf(3), 4.0, None, A.is_ge), "vc3")
+        done(V.memset(T.CNEG[:], -4416.0), "vlate")
 
     def perms():
         need("s", "vid", "vc2")
         for n, (lo, msk) in enumerate([(16, cg(0)), (32, cf(1)), (0, cg(0)), (16, cf(1))]):
             done(S.activation(T.PM[:, 128 * n:128 * n + 128], T.IDW[:, lo:lo + 128], COPY, scale=msk), "sperm")
 
-    def mark(out, pattern, base, value, sem):
-        need("g", "veqp")
+    def signs():
+        for k in range(2):
+            done(S.activation(T.BS[:, k:128:2], T.BO[:, :, k:16:2], COPY, scale=0.0625 - 0.125 * k), "sbs")
+        need("s", "sbs", "vc3")
+        done(S.activation(T.ER[:], T.BS[:], COPY, scale=cg(4)), "ser")
+
+    def mark(out, pattern, base, value, sem, over=None):
+        need("g", over or "veqp")
         n = pattern[0][1] * 16
-        done(g.affine_select(out, T.ZER[:, 0:n], pattern, A.not_equal, value, base, 1), sem)
+        done(g.affine_select(out, out if over else T.ZER[:, 0:n], pattern, A.not_equal, value, base, 1), sem)
 
     def marks_a():
-        mark(T.ZN[:], [[-16, 9], [-1000, 16]], 16, 1.0, "gzz")
-        mark(T.ZP[:], [[-16, 9], [-1000, 16]], 15, 1.0, "gzz")
-        for n, wt in enumerate((160.0, -624.0, -159.0)):
-            mark(T.PS[:, n, :], [[-16, 9], [-1000, 2], [-2, 8]], 15, wt, "gps")
+        mark(T.ZN[:], [[-16, 9], [-1000, 16]], 16, 1.0, "gz0")
+        mark(T.PS[:, 0, :], [[-16, 9], [-1000, 2], [-2, 8]], 15, 160.0, "gps")
+        mark(T.ZN[:], [[-16, 9], [-1000, 16]], 15, 1.0, "gzz", "gz0")
 
     def marks_b():
         mark(T.SD[:, 1, :], [[-16, 8], [-1, 16]], 1, -4096.0, "gsd0")
+        for n, wt in ((1, -624.0), (2, -159.0)):
+            mark(T.PS[:, n, :], [[-16, 9], [-1000, 2], [-2, 8]], 15, wt, "gps")
         mark(T.SD[:, 0, :], [[-16, 8], [-1, 16]], 0, 4096.0, "gsd")
         mark(T.SD[:, 2, :], [[-16, 8], [-1000, 16]], -15, -4096.0, "gsd")
         need("g", "gsd0")
         done(g.affine_select(T.SD[:, 1, :], T.SD[:, 1, :], [[0, 8], [1, 16]], A.not_equal, 0.0, 0, 0), "gsd")
-        mark(T.ER[:], [[-16, 8], [0, 16]], -3, 1.0, "ger")
 
     def marks_c():
-        mark(T.LB[:], [[-16, 9], [-1000, 8], [0, 2]], 16, 1.0, "glb")
+        mark(T.LB[:], [[-16, 9], [-1000, 8], [0, 2]], 16, 1.0, "glb0")
+        done(g.affine_select(T.KO[:], T.ZER[:, 0:NC], [[0, 2], [1, 2], [0, 10]], A.not_equal, 4096.0, -1, 0), "gko")
+        mark(T.LB[:], [[-16, 9], [-1000, 8], [0, 2]], 15, 1.0, "glb", "glb0")
 
-    def diags(eng_, o, ds=range(7)):
-        if eng_ == "s":
-            if o == rank:
-                need("s", "dw", "vid")
-                done(S.activation(T.WG[:, 8 * o:8 * o + 7], T.WS[:], COPY), "swg")
-            else:
-                need("s", "wr")
-                done(S.activation(T.WG[:, 8 * o:8 * o + 7], T.WR[:, 8 * o:8 * o + 7], COPY), "swg")
-            need("s", "swg")
-        else:
-            need("v", "wr", "vid")
-        for d in ds:
-            out = T.DG[:, (7 * o + d) * 128:(7 * o + d) * 128 + 128]
-            if eng_ == "s":
-                done(S.activation(out, ident, COPY, scale=T.WG[:, 8 * o + d:8 * o + d + 1]), "sdg")
-            else:
-                done(V.tensor_scalar(out, ident, T.WR[:, 8 * o + d:8 * o + d + 1], None, A.mult), "vdg")
+    def marks_d():
+        mark(T.ZN[:], [[-16, 9], [-1000, 16]], 12, 1.0, "gz4", "pL3")
 
     STEP = {"L0": 3, "L1": 4, "L2": 5, "L3": 6, "M1": 2, "M2": 1, "M3": 0}
 
-    def lst_ap(lst, lo, hi):
-        if lst in ("L1", "M1"):
-            o = NC * (lst == "M1")
-            return T.LM1[:, o + lo // 16:o + hi // 16]
-        return T[lst][:, lo // 16:hi // 16]
+    def diags_own():
+        need("s", "dw", "vid")
+        done(S.activation(T.WF[:], T.WS[:], COPY), "swf")
+        need("s", "swf")
+        for d in range(7):
+            done(S.activation(T.DG[:, (7 * rank + d) * 128:(7 * rank + d) * 128 + 128], ident, COPY, scale=T.WF[:, d:d + 1]), "sdg")
 
-    def ready(lst):
-        return "eL1" if lst == "M1" else "e" + lst
+    def diags(*lists):
+        need("v", "wr", "vid")
+        for lst in lists:
+            for o in others:
+                d = STEP[lst]
+                done(V.tensor_scalar(T.DG[:, (7 * o + d) * 128:(7 * o + d) * 128 + 128], ident, T.WR[:, 8 * o + d:8 * o + d + 1], None, A.mult), "w" + lst)
+
+    WHERE = {"L0": ("L0", 0, "eL0")}
+    WHERE.update({d + k: ("LM" + k, NC * (d == "M"), "eL" + k) for d in "LM" for k in "123"})
+
+    def lst_ap(lst, lo, hi):
+        buf, o, _ = WHERE[lst]
+        return T[buf][:, o + lo // 16:o + hi // 16]
 
     def gather(q, out, win, offs, sem):
         src = win.indirect(offs)
@@ -235,60 +254,75 @@ def rank_program(g, core, T, topo):
 
     def pick_x(lst, q, lo=0, hi=NS, tag="", win="X", at=None):
         at = at or lst
-        need(q, "dx" if win == "X" else "g" + win, ready(at))
+        need(q, "dx" if win == "X" else "g" + win, WHERE[at][2])
         gather(q, T["X" + lst][:, lo:hi], T[win][:], lst_ap(at, lo, hi), "s" + lst + tag)
 
-    def back(k, q, lo, hi):
-        need(q, "vpv", "dx" if k == 1 else "gXB1")
-        gather(q, T["XB%d" % k][:, lo:hi], (T.X if k == 1 else T.XB1)[:], T.PV[:, lo // 16:hi // 16], "gXB%d" % k)
+    def back(q, lo, hi):
+        need(q, "vpv", "dx")
+        gather(q, T.XB[:, lo:hi], T.X[:], T.PV[:, lo // 16:hi // 16], "gXB")
+
+    def ahead(q, lo, hi):
+        need(q, "vpv", "dpw")
+        gather(q, T.PN[:, lo:hi], T.PW[:], T.PV[:, 128 + lo // 16:128 + hi // 16], "gPN")
+
+    def merge():
+        need("y", "gPN", "gR0", "gR1", "gR2")
+        done(g.sync.dma_start(T.PW[4:128:16, :], T.PN[0:128:16, :]), "dpn", 16)
+        done(g.sync.dma_start(T.PW[7:128:16, :], T.PN[3:128:16, :]), "dpn", 16)
 
     def prv_turn():
         need("v", "dtab")
         done(V.tensor_copy(T.TX[:], T.TI[:]), "vcv")
+        consts_b()
         need("v", "vcv")
         done(V.transpose(T.TT[:], T.TX[:]), "vtr")
         need("t", "sperm", "vtr")
         for b1 in range(8):
             for ga in range(2):
                 n = 2 * ga + b1 % 2
-                ins = P.matmul(T.E0[:, b1:128:8], T.PM[:, 128 * n:128 * n + 128], T.TT[:, b1 // 2, 16 * ga:16 * ga + 16], ga == 0, ga == 1)
+                ins = P.matmul(T.E0[:, b1:256:8], T.PM[:, 128 * n:128 * n + 128], T.TT[:, b1 // 2:8:4, 16 * ga:16 * ga + 16], ga == 0, ga == 1)
         done(ins, "ptab")
 
     def keeps():
-        need("t", "eK", "eM3", "vlate")
+        need("t", "eK", "ePL", "vpk", "vlate")
         P.matmul(T.QA[:, 0:128], T.C128[:], T.CNEG[:], True, False)
         sampled("QA", False, False)
 
-    def pick_p(lst, q, lo=0, hi=NS):
-        need(q, "dpw", ready(lst))
-        gather(q, T["R" + lst][:, lo:hi], T.PW[:], lst_ap(lst, lo, hi), "g" + lst)
+    def pick_p(lst, q, lo=0, hi=NS, far=False):
+        need(q, "dpw", WHERE[lst][2])
+        bk = int(lst[0] == "M")
+        keep = cg(5 if far else 2 + bk)
+        out, src = T["R" + lst[1]][:, bk, lo:hi], T.PW[:].indirect(lst_ap(lst, lo, hi))
+        done(S.activation(out, src, COPY, scale=keep) if q == "s" else V.tensor_scalar(out, src, keep, None, A.mult), "gR" + lst[1])
 
-    def wrap(lst, bank, sel, rows, first=True):
+    def chase(k, bank, both, after, src=None):
+        src = src or k - 1
+        need("t", "gzz", "gz4", "gR%d" % src, after)
+        rows, n = T["R%d" % src], 1 + both
         for ro in range(16):
-            ins = P.matmul(T[bank][:, 0:NC], T[sel][:, 16 - ro:144 - ro], T[rows][:, ro:NS:16], first and ro == 0, ro == 15)
-        done(ins, "p" + lst)
+            ins = P.matmul(T[bank][:, 0:NC * n], T.ZN[:, 16 - ro:144 - ro], rows[:, 0:n, ro:NS:16], ro == 0, ro == 15)
+        done(ins, "pL%d" % k)
 
-    def chase(lst, bank, after):
-        src = lst[0] + str(int(lst[1]) - 1)
-        need("t", "gzz", "g" + src, after)
-        wrap(lst, bank, "ZN" if lst[0] == "L" else "ZP", "R" + src)
-
-    def evac(lst, bank):
-        need("v", "p" + lst)
-        done(V.tensor_copy(T[lst][:], T[bank][:, 0:NC]), "e" + lst)
+    def evac(k, bank, more):
+        need("v", "pL%d" % k)
+        n = NC * (1 + more)
+        done(V.tensor_copy(T["LM%d" % k][:, 0:n], T[bank][:, 0:n]), "eL%d" % k)
 
     def hsum(lst, k, qs=None, tag=""):
-        need("t", "s" + lst + tag, "sdg", "vdg")
+        need("t", "s" + lst + tag, "sdg", "w" + lst)
         for q in qs or [rank] + others:
             o = (7 * q + STEP[lst]) * 128
             ins = P.matmul(T["H%d" % q][:, 0:NQ], T.DG[:, o:o + 128], T["X" + lst][:, NQ * q:NQ * q + NQ], k == 0, k == 6)
             if k == 6:
                 done(ins, "ph%d" % q)
 
-    def reward(rows, sem, first=False):
-        need("t", "ger", sem)
-        for h in range(2):
-            P.matmul(T["E%d" % h][:, 0:320], T.ER[:], T[rows][:, 320 * h:320 * h + 320], first, False)
+    parts = [("E0", 2 * NQ * mine, 2 * NQ, [rank, others[0]])] + [(b, NQ * q, NQ, [q]) for b, q in zip(("E1", "QB"), others[1:])]
+
+    def reward(k, which=parts[:2]):
+        need("t", "ser", "gR%d" % k, "vpv", "vab", *(["eL3"] if which[0][0] == "QB" else []))
+        for bank, lo, n, qs in which:
+            rows = T["R%d" % k][:, 0, lo:lo + n] if k else T.R0[:, lo:lo + n]
+            P.matmul(T[bank][:, 0:n], T.ER[:], rows, k == 0, False)
 
     def sampled(bank, first, last):
         need("t", "gsd", "sk")
@@ -296,32 +330,44 @@ def rank_program(g, core, T, topo):
         P.matmul(T[bank][:, 0:128], T.SD[:, 1, :], T.K1[:, 16:144], False, False)
         return P.matmul(T[bank][:, 0:128], T.SD[:, 2, :], T.K1[:, 15:143], False, last)
 
-    def serve(a, q):
+    def serve(a):
         KL, VS, VR = T["KL%d" % a], T["VS%d" % a], T["VR%d" % a]
-        need(q, "dval", "kr%d" % a)
-        gather(q, VS[:], T.VALB[:], KL[:, 0:30], "gV")
-        need("g", "gV")
-        send(peers, lambda c: VS[:, NQ * place(c, core):NQ * place(c, core) + NQ], lambda c: VR[:, NQ * rank:NQ * rank + NQ],
-             lambda c: T.sem["vr%d_%d" % (a, rank)], "vl")
-        for c in peers:
-            tot["vr%d_%d" % (a, T.rank_of(c))] = inc[c]
+        if a == 0:
+            for q, lo, hi in (("v", 0, 14), ("s", 14, 30)):
+                need(q, "dval", "kr0")
+                gather(q, VS[:, 16 * lo:16 * hi], own_val, KL[:, lo:hi], "gV")
+            need("g", "gV")
+            send(peers, lambda c: VS[:, NQ * place(c, core):NQ * place(c, core) + NQ], lambda c: VR[:, NQ * rank:NQ * rank + NQ],
+                 lambda c: T.sem["vr0_%d" % rank], "vl")
+            for c in peers:
+                tot["vr0_%d" % T.rank_of(c)] = inc[c]
+            send(on, lambda c: own_val, lambda c: own_val, lambda c: T.sem.tr, "tl", {c: topo.engines(core, c) for c in on})
+            tot["tr"] = len(topo.engines(on[0], core))
+        else:
+            for q, lo, hi in (("v", 0, 10), ("s", 10, 20)):
+                need(q, "tr", "kr1")
+                gather(q, VS[:, 16 * lo:16 * hi], T.VALB[:], KL[:, lo:hi], "gV")
+            need("g", "gV")
+            send([twin], lambda c: VS[:], lambda c: VR[:, 320 * mine:320 * mine + 320], lambda c: T.sem.vr1_0, "vl", wide)
+            tot["vr1_0"] = len(topo.engines(twin, core))
 
     def serve_own(a, q):
-        need(q, "dval", "eK")
-        gather(q, T["VR%d" % a][:, NQ * rank:NQ * rank + NQ], T.VALB[:], T["KS%d" % a][:, 10 * rank:10 * rank + 10], "vr%d_%d" % (a, rank))
+        if a == 0:
+            need(q, "dval", "eK")
+            gather(q, T.VR0[:, NQ * rank:NQ * rank + NQ], own_val, T.KS0[:, 10 * rank:10 * rank + 10], "vr0_%d" % rank)
+        else:
+            need(q, "tr", "eK")
+            gather(q, T.VR1[:, 320 * mine:320 * mine + 320], T.VALB[:], T.KS1[:, 20 * mine:20 * mine + 20], "vr1_1")
 
     def heads():
         need("t", "gj", "vcon")
         P.matmul(T.H0[:, 0:128], T.C128[:], T.JI[:, 0:128], True, False)
+        P.matmul(T.H0[:, 0:128], T.C128[:], T.C1K[:], False, False)
         P.matmul(T.H1[:, 0:320], T.C128[:], T.JI[:, 128:448], True, False)
 
     def tails(pb):
         need("t", "gtu")
         done(P.matmul(T.QB[:, 0:128], T.TU[:], pb[:], True, True), "pB")
-
-    def frame_sums():
-        need("v", "pB")
-        done(V.tensor_tensor(T.SS[:], T.CS[:], T.QB[:, 0:128], A.subtract), "vS")
 
     def counts():
         need("s", "vS", "vc3")
@@ -330,18 +376,20 @@ def rank_program(g, core, T, topo):
         done(S.activation(T.K40[:], T.SS[:], IDENT, bias=129.4751, scale=1.0 / 5120), "sk")
 
     def pairs_t():
-        need("t", "gps", "sk", "sab")
+        need("t", "gps", "sk", "vscan", "eL2")
         for cp in range(2):
             for n, src in enumerate((T.K1[:, 16 + cp:144:2], T.K4[:, cp:128:2], T.K40[:, cp:128:2])):
-                ins = P.matmul(T.E0[:, 0:64], T.PS[:, n, 16 - 8 * cp:144 - 8 * cp], src, cp + n == 0, cp + n == 3)
-        done(ins, "pPL")
-        done(sampled("E1", True, True), "pS")
+                P.matmul(T.QA[:, 128:192], T.PS[:, n, 16 - 8 * cp:144 - 8 * cp], src, cp + n == 0, cp + n == 3)
+        done(sampled("QA", True, True), "pS")
 
     def pairs_v(pb):
-        need("v", "pPL", "gG0", "gG1")
-        done(V.tensor_scalar(T.PL[:], T.E0[:, 0:64], 496734.0, None, A.add), "ePL")
-        need("v", "pS")
-        done(V.tensor_tensor(T.PK[:], pb[:], T.E1[:, 0:128], A.subtract), "vpk")
+        need("v", "pS", "gG0", "gG1")
+        done(V.tensor_scalar(T.PL[:], T.QA[:, 128:192], 496734.0, None, A.add), "ePL")
+        done(V.tensor_tensor(T.PK[:], pb[:], T.QA[:, 0:128], A.subtract), "vpk")
+
+    def keep_v():
+        need("v", "vpk")
+        done(V.tensor_scalar(T.KEEP[:], T.PK[:], 1.0, None, A.max), "vkeep")
 
     for a in range(2):
         pb = T.PB0 if a == 0 else T.PB1
@@ -350,32 +398,25 @@ def rank_program(g, core, T, topo):
             heads()
         need("t", "vbo", "vpb", "vP")
         done(P.matmul(T.QA[:, 0:128], bo, pb[:], True, True), "pA")
-        if a:
-            tails(pb)
-        else:
+        if a == 0:
             heads()
+        tails(pb)
         need("v", "pA", "vone")
         done(V.tensor_tensor_scan(T.CS[:], T.ONE[:], T.QA[:, 0:128], 0.0, A.mult, A.add), "vscan")
         need("v", "vscan")
-        need("s", "vscan")
-        done(S.activation(T.NA[:], T.CS[:], IDENT, bias=-128.5001 / 16, scale=-1.0 / 81920), "vna")
-        done(V.tensor_scalar(T.NK[:], T.CS[:], -1.0 / 2048, -1024.50390625 / 16, A.mult, A.add), "vnk")
-        if a:
-            back(2, "s", 0, 256)
-        need("t", "vnk", "vby")
-        P.matmul(T.H1[:, 0:320], T.NK[:], T.BY[:], False, False)
-        need("t", "vna", "sbz")
-        done(P.matmul(T.H1[:, 0:320], T.NA[:], T.BZ[:], False, True), "pY")
-        done(P.matmul(T.H0[:, 0:128], T.NA[:], bo, False, True), "pX")
+        done(V.tensor_scalar(T.KA[:], T.CS[:], ck(2), ck(3), A.mult, A.add), "vka")
+        need("t", "vka", "vby")
+        done(P.matmul(T.H1[:, 0:320], T.KA[:], T.BY[:], False, True), "pY")
+        done(P.matmul(T.H0[:, 0:128], T.KA[:], T.BX[:], False, True), "pX")
+        need("v", "pB")
+        done(V.tensor_tensor(T.SS[:], T.CS[:], T.QB[:, 0:128], A.subtract), "vS")
         if a == 0:
             consts_a()
-        else:
-            frame_sums()
         need("v", "pX", "veqp")
-        done(V.tensor_scalar(T.EQP[:, :, 16:32], T.H0[:, 0:128], -129.0, 0.5, A.is_equal, A.mult), "veq")
-        done(V.tensor_scalar(T.UU[:], T.H0[:, 0:128], -129.5, -128.5, A.max, A.min), "vuu")
+        done(V.tensor_scalar(T.EQP[:, :, 16:32], T.H0[:, 0:128], 0.0, 0.5, A.is_equal, A.mult), "veq")
+        done(V.tensor_scalar(T.UU[:], T.H0[:, 0:128], -0.5, 0.5, A.max, A.min), "vuu")
         need("s", "pY")
-        done(S.activation(T.SG[:], T.H1[:, 0:320], AF.Sign, bias=-4134.5), "ssg")
+        done(S.activation(T.SG[:], T.H1[:, 0:320], AF.Sign, bias=-39974.5), "ssg")
         need("t", "veqp")
         P.matmul(T.H2[:, 0:NC], bo, T.ZER[:, 0:NC], True, False)
         need("t", "veq", "ssg")
@@ -385,16 +426,13 @@ def rank_program(g, core, T, topo):
         need("t", "vuu")
         done(P.matmul(T.H2[:, 0:NC], T.UU[:], T.ONB[:], False, True), "pC")
         if a == 0:
-            tails(pb)
-            consts_b()
             marks_a()
             perms()
-            diags("s", rank)
+            prv_turn()
+            diags_own()
         need("v", "pC")
-        done(V.tensor_scalar(T.COL[:], T.H2[:, 0:NC], 16576.0, 127.0, A.add, A.min), "eC")
-        done(V.tensor_scalar(T.C16[:], T.H2[:, 0:NC], 16576.0, 16.0, A.add, A.mult), "eC16")
-        if a == 0:
-            frame_sums()
+        done(V.tensor_scalar(T.COL[:], T.H2[:, 0:NC], 64.0, 127.0, A.add, A.min), "eC")
+        done(V.tensor_scalar(T.C16[:], T.H2[:, 0:NC], 64.0, 16.0, A.add, A.mult), "eC16")
         counts()
         need("v", "eC", "vS", "gthr")
         done(V.tensor_tensor(T.CM[:], T.SS[:].indirect(T.COL[:]), T.THR[:], A.is_lt), "vcm")
@@ -402,146 +440,152 @@ def rank_program(g, core, T, topo):
         P.matmul(T.H3[:, 0:NC], ident, T.C16[:], True, False)
         if a:
             pairs_t()
-            back(2, "s", 256, 1536)
+            back("s", 640, 2048)
+        else:
+            signs()
         need("t", "vcm")
-        wrap("L0", "H3", "ZA", "CM", False)
+        for ro in range(16):
+            ins = P.matmul(T.H3[:, 0:NC], T.ZA[:, 16 - ro:144 - ro], T.CM[:, ro:NS:16], False, ro == 15)
+        done(ins, "pL0")
         if a == 0:
-            prv_turn()
+            need("v", "ptab")
+            done(V.tensor_copy(T.PV[:], T.E0[:, 0:256]), "vpv")
+            back("s", 0, 384)
+            back("v", 384, 640)
         else:
             pairs_v(pb)
-            back(2, "v", 1536, 1792)
+            keep_v()
         need("v", "pL0")
         done(V.tensor_scalar(T.L0[:], T.H3[:, 0:NC], 2047.0, None, A.min), "eL0")
-        need("v", "eL0", "dpw", "vc3")
+        need("v", "eL0", "dpw", "vc3", "dpn")
         done(V.tensor_scalar(T.R0[:, 0:320], T.PW[:].indirect(T.L0[:, 0:20]), cg(1), None, A.add), "gR0")
-        need("s", "eL0", "dpw", "vc3")
+        need("s", "eL0", "dpw", "vc3", "dpn")
         done(S.activation(T.R0[:, 320:NS], T.PW[:].indirect(T.L0[:, 20:40]), IDENT, bias=cg(1)), "gR0")
         pick_x("L0", "s")
         need("v", "gR0")
         done(V.transpose(T.RT[:], T.R0[:]), "vrt")
-        need("t", "vrt", "sperm", "vscan", "vS")
-        for bank, col, row, sem in (("QA", 0, 2, "pK"), ("QB", 0, 0, None), ("QB", NC, 1, "pL1")):
+        if a:
+            pick_x("M1", "s", 0, 320, "", "XB", "L0")
+        need("t", "sperm", "vscan", "vS", "gko", "ePL", "vpk")
+        if a:
+            P.matmul(T.QA[:, 0:NC], T.C128[:], T.KO[:], True, False)
+        need("t", "vrt")
+        rows = [("QB", 0, 0, None), ("QB", NC, 1, "pL1"), ("QA", 0, 2, "pK")] + [("E0", 0, 4, "pL2")] * a
+        for bank, col, row, sem in rows:
             for h in range(2):
                 for gb in range(2):
                     n = 2 * gb + h
-                    ins = P.matmul(T[bank][:, col + h:col + NC:2], T.PM[:, 128 * n:128 * n + 128], T.RT[:, :, 16 * gb + row], gb == 0, gb == 1)
+                    first, end = (False, n == 3) if a and bank == "QA" else (gb == 0, gb == 1)
+                    ins = P.matmul(T[bank][:, col + h:col + NC:2], T.PM[:, 128 * n:128 * n + 128], T.RT[:, :, 16 * gb + row], first, end)
             if sem:
                 done(ins, sem)
-        if a == 0:
-            need("v", "ptab")
-            done(V.tensor_copy(T.PV[:], T.E0[:, 0:128]), "vpv")
+        evac(1, "QB", True)
         need("v", "pK")
         done(V.tensor_scalar(KS[:], T.QA[:, 0:NC], 2048.0, None, A.add), "eK")
         need("g", "eK")
-        send(peers, lambda c: KS[:, 10 * T.rank_of(c):10 * T.rank_of(c) + 10], lambda c: KL[:, 10 * place(core, c):10 * place(core, c) + 10],
-             lambda c: T.sem["kr%d" % a], "kl")
-        tot["kr%d" % a] = sum(inc.values())
         if a == 0:
+            send(peers, lambda c: KS[:, 10 * T.rank_of(c):10 * T.rank_of(c) + 10], lambda c: KL[:, 10 * place(core, c):10 * place(core, c) + 10],
+                 lambda c: T.sem.kr0, "kl")
+            tot["kr0"] = sum(inc.values())
             marks_b()
-        need("v", "pL1")
-        done(V.tensor_copy(T.LM1[:], T.QB[:, 0:2 * NC]), "eL1")
+        else:
+            send([twin], lambda c: KS[:, 20 * theirs:20 * theirs + 20], lambda c: KL[:, 0:20], lambda c: T.sem.kr1, "kl", wide)
+            tot["kr1"] = len(topo.engines(twin, core))
         need("t", "eC16", "eL0", "vuu", "ssg")
-        halves = [(h, [q for q in [rank] + others if q // 2 == h]) for h in (rank // 2, 1 - rank // 2)]
         if a == 0:
             pick_p("M1", "v")
             pick_p("L1", "s")
-            chase("M2", "QA", "eK")
-            chase("L2", "QB", "eL1")
+            chase(2, "QA", True, "eK")
             pick_x("L1", "s")
-            diags("v", others[0])
-            evac("M2", "QA")
-            done(V.memset(T.CNEG[:], -4224.0), "vlate")
-            evac("L2", "QB")
-            need("t", "vpv")
-            pairs_t()
-            serve(a, "s")
-            marks_c()
-            pick_p("L2", "v")
-            pick_p("M2", "s")
-            chase("L3", "QB", "eL2")
-            chase("M3", "QA", "eM2")
-            diags("v", others[1])
-            diags("v", others[2])
-            pick_x("M1", "s")
-            evac("L3", "QB")
-            evac("M3", "QA")
+            diags("L0", "L1", "M1", "L2", "M2")
             hsum("L0", 0)
+            evac(2, "QA", True)
+            serve_own(a, "s")
+            diags("M3", "L3")
             hsum("L1", 1)
+            reward(0)
+            reward(1)
+            serve(a)
+            marks_c()
+            pick_p("M2", "v")
+            pick_p("L2", "s")
+            pairs_t()
+            chase(3, "QB", True, "eL1")
+            marks_d()
             pairs_v(pb)
-            pick_x("L2", "v")
-            pick_x("M2", "s")
-            serve_own(a, "v")
-            hsum("M1", 2)
-            need("t", "ePL", "vpk")
-            reward("R0", "gR0", True)
-            reward("RL1", "gL1")
-            reward("RL2", "gL2")
-            hsum("L2", 3)
+            reward(2)
             keeps()
+            pick_x("M1", "v", 0, 448)
+            keep_v()
+            evac(3, "QB", True)
+            pick_x("L2", "s")
+            pick_x("M1", "s", 448, NS)
+            for k in range(3):
+                reward(k, parts[2:])
+            hsum("L2", 2)
+            hsum("M1", 3)
+            pick_x("M2", "v", 0, 320)
+            pick_x("M2", "s", 320, NS)
             hsum("M2", 4)
             last = (("M3", "v", "X", "M3"), ("L3", "s", "X", "L3"))
         else:
-            pick_p("L1", "v")
-            pick_x("M1", "s")
+            WHERE["M2"] = ("LM3", NC, "eL3")
+            pick_p("L1", "v", far=True)
+            pick_p("M1", "s")
             hsum("L0", 0)
-            need("t", "ePL", "vpk")
-            reward("R0", "gR0", True)
-            chase("L2", "QB", "eL1")
             keeps()
-            pick_x("L1", "v")
-            evac("L2", "QB")
-            back(2, "s", 1792, 2048)
-            serve(a, "s")
-            pick_p("L2", "v")
-            pick_x("M2", "s", win="XB1", at="M1")
-            hsum("M1", 1)
-            reward("RL1", "gL1")
-            hsum("L1", 2)
-            chase("L3", "QB", "eL2")
+            chase(3, "QB", True, "eL1", 1)
+            evac(2, "E0", False)
             serve_own(a, "v")
-            pick_x("L2", "s")
-            reward("RL2", "gL2")
+            pick_x("M1", "s", 320, NS, "", "XB", "L0")
+            serve(a)
+            need("t", "eL2")
+            reward(0)
+            reward(1)
+            hsum("M1", 1)
+            evac(3, "QB", True)
+            for k in range(2):
+                reward(k, parts[2:])
+            pick_x("L1", "v")
+            pick_x("M2", "s", win="XB", at="M1")
+            pick_x("L2", "v", 0, 256)
+            pick_x("L2", "s", 256, NS)
+            hsum("L1", 2)
             hsum("M2", 3)
-            pick_x("M3", "v", 0, 320, "", "XB2", "M1")
-            evac("L3", "QB")
-            pick_x("M3", "v", 320, NS, "", "XB2", "M1")
             hsum("L2", 4)
-            hsum("M3", 5)
-            last = (("L3", "s", "X", "L3"),)
-        for tag, (h, qs) in zip(("", "b"), halves):
+            last = (("L3", "v", "X", "L3"), ("M3", "s", "XB", "M2"))
+        for tag, (bank, lo, n, qs) in zip(("", "b", "c"), parts):
             for lst, q, win, at in last:
-                pick_x(lst, "v" if a and tag else q, 320 * h, 320 * h + 320, tag, win, at)
+                pick_x(lst, q, lo, lo + n, tag, win, at)
             for k, (lst, q, win, at) in enumerate(last):
-                hsum(lst, 7 - len(last) + k, qs, tag)
+                hsum(lst, 5 + k, qs, tag)
         if a == 0:
-            back(1, "s", 0, 768)
-        for h, qs in halves:
+            ahead("s", 0, 768)
+        for k, (bank, lo, n, qs) in enumerate(parts):
             for q in qs:
-                need("v", "ph%d" % q, "vr%d_%d" % (a, q))
-                done(V.tensor_tensor(T.PROD[:, NQ * q:NQ * q + NQ], VR[:, NQ * q:NQ * q + NQ], T["H%d" % q][:, 0:NQ], A.mult), "vpr%d" % h)
-            need("t", "vpr%d" % h)
-            done(P.matmul(T["E%d" % h][:, 0:320], bo, T.PROD[:, 320 * h:320 * h + 320], False, True), "pE%d" % h)
-            need("s", "pE%d" % h)
-            done(S.activation(T.AB[:, 320 * h:320 * h + 320], T["E%d" % h][:, 0:320], AF.Abs, scale=0.0625), "sab")
-        if a == 0:
-            back(1, "v", 768, 1152)
-        need("v", "sab", "ePL")
-        need("s", "sab", "ePL")
+                need("v", "ph%d" % q, "vr1_%d" % (k == 0) if a else "vr0_%d" % q)
+                done(V.tensor_tensor(T.PROD[:, NQ * q:NQ * q + NQ], VR[:, NQ * q:NQ * q + NQ], T["H%d" % q][:, 0:NQ], A.mult), "vpr%d" % k)
+            need("t", "vpr%d" % k, "sbs")
+            done(P.matmul(T[bank][:, 0:n], T.BS[:], T.PROD[:, lo:lo + n], False, True), "pE%d" % k)
+        for k, (bank, lo, n, qs) in enumerate(parts):
+            need("v", "pE%d" % k)
+            done(V.tensor_scalar(T.AB[:, lo:lo + n], T[bank][:, 0:n], 0.0, 63.0, A.max, A.min), "vab")
+        need("v", "vab", "ePL")
+        need("s", "vab", "ePL")
         for b in range(2):
             lo = 512 * b
-            done(V.tensor_scalar(T.GB[:, lo:lo + 256], T.AB[:].indirect(T.PL[:, lo // 16:lo // 16 + 16]), 127.53125, None, A.add), "gG%d" % b)
-            done(S.activation(T.GB[:, lo + 256:lo + 512], T.AB[:].indirect(T.PL[:, lo // 16 + 16:lo // 16 + 32]), IDENT, bias=127.53125), "gG%d" % b)
+            done(V.tensor_scalar(T.GB[:, lo:lo + 256], T.AB[:].indirect(T.PL[:, lo // 16:lo // 16 + 16]), 159.53125, None, A.add), "gG%d" % b)
+            done(S.activation(T.GB[:, lo + 256:lo + 512], T.AB[:].indirect(T.PL[:, lo // 16 + 16:lo // 16 + 32]), IDENT, bias=159.53125), "gG%d" % b)
             need("t", "gG%d" % b, "glb")
             for h in range(8):
                 ins = P.matmul(T.QA[:, 64 * b:64 * b + 64], T.LB[:, 16 - 2 * h:144 - 2 * h], T.GB[:, lo + h:lo + 512:8], False, b == 1 and h == 7)
         done(ins, "pO")
         if a == 0:
-            back(1, "v", 1152, 1408)
-            back(1, "s", 1408, 2048)
-        need("v", "pO")
-        done(V.tensor_scalar(T.QB[:, 0:128], T.QA[:, 0:128], 1.0, 63.0, A.max, A.min), "vni")
-        need("v", "vni", "vpk")
-        done(V.tensor_tensor((T.YO if a else T.PB1)[:], T.QB[:, 0:128], T.PK[:], A.max), "vP")
+            ahead("v", 768, 1024)
+            ahead("s", 1024, 2048)
+            merge()
+        need("v", "pO", "vkeep")
+        done(V.tensor_tensor((T.YO if a else T.PB1)[:], T.QA[:, 0:128], T.KEEP[:], A.max), "vP")
     need("y", "vP")
     done(g.sync.dma_start(T.y[:], T.YO[:]), "dy", 16)
     need("y", "dy")

@@ -13,15 +13,15 @@ SCRATCH = {
     "BY": ("sbuf", [128, 8, NC], BF), "BX": ("sbuf", [128, 128], BF), "C1K": ("sbuf", [128, 128], BF), "CK": ("sbuf", [128, 4], F32), "JI": ("sbuf", [128, 448], BF), "C128": ("sbuf", [128, 128], BF),
     "CNEG": ("sbuf", [128, 128], BF), "ZER": ("sbuf", [128, 144], BF), "EQP": ("sbuf", [128, 8, 48], BF), "UU": ("sbuf", [128, 128], BF),
     "SG": ("sbuf", [128, 8 * NC], BF), "PM": ("sbuf", [128, 512], BF), "ZA": ("sbuf", [128, 144], BF), "ZN": ("sbuf", [128, 144], BF),
-    "BS": ("sbuf", [128, 128], BF), "KEEP": ("sbuf", [128, 128], F32), "ER": ("sbuf", [128, 128], BF), "LB": ("sbuf", [128, 144], BF),
-    "PS": ("sbuf", [128, 3, 144], BF), "SD": ("sbuf", [128, 3, 128], BF),
+    "BS": ("sbuf", [128, 128], BF), "KEEP": ("sbuf", [128, 128], BF), "ER": ("sbuf", [128, 128], BF), "LB": ("sbuf", [128, 144], BF),
+    "LC": ("sbuf", [128, 128], BF), "STEP": ("sbuf", [128, 128], F32), "XC": ("sbuf", [128, 2048], BF), "PS": ("sbuf", [128, 4, 144], BF), "SD": ("sbuf", [128, 4, 128], BF),
     "ONE": ("sbuf", [128, 128], F32), "CS": ("sbuf", [128, 128], F32), "SS": ("sbuf", [128, 128], F32),
     "KA": ("sbuf", [128, 128], F16), "K1": ("sbuf", [128, 144], F16), "K4": ("sbuf", [128, 128], F16),
     "K40": ("sbuf", [128, 128], BF), "COL": ("sbuf", [128, NC], U16), "C16": ("sbuf", [128, NC], F16), "CM": ("sbuf", [128, NS], BF),
     "R0": ("sbuf", [128, NS], F16), "RT": ("sbuf", [128, NS // 32, 32], F16), "L0": ("sbuf", [128, NC], U16),
     "KS0": ("sbuf", [128, NC], U16), "KS1": ("sbuf", [128, NC], U16), "KL0": ("sbuf", [128, 32], U16), "KL1": ("sbuf", [128, 32], U16),
     "VS0": ("sbuf", [128, 3 * NQ], BF), "VS1": ("sbuf", [128, 2 * NQ], BF), "VR0": ("sbuf", [128, NS], BF), "VR1": ("sbuf", [128, NS], BF),
-    "PROD": ("sbuf", [128, NS], F16), "AB": ("sbuf", [128, NS], F32), "PL": ("sbuf", [128, 64], U16), "GB": ("sbuf", [128, 1024], BF),
+    "PROD": ("sbuf", [128, NS], F16), "AB": ("sbuf", [128, NS + 16], F32), "PL": ("sbuf", [128, 64], U16), "GB": ("sbuf", [128, 1024], BF),
     "PK": ("sbuf", [128, 128], F32), "YO": ("sbuf", [128, 128], F32),
     "WS": ("sbuf", [128, 7], BF), "WF": ("sbuf", [128, 7], F32), "WR": ("sbuf", [128, 32], BF),
     "DG": ("sbuf", [128, 28 * 128], BF), "TI": ("sbuf", [128, 8, 32], I32), "TX": ("sbuf", [128, 8, 32], F16), "TT": ("sbuf", [128, 8, 32], F16),
@@ -36,10 +36,10 @@ for _n in "12":
 for _n in ["QA", "QB", "E0", "E1", "H0", "H1", "H2", "H3"]:
     SCRATCH[_n] = ("psum", [128, 512], F32)
 SEMAPHORES = (["dpri", "dw", "dx", "dval", "dpw", "dy", "dtab", "gi", "gj", "gtu", "gthr", "glb0", "glb", "gps", "gz0", "gzz", "gsd0", "gsd", "gko",
-               "vz", "sz", "vcon", "vc", "vc2", "vc3", "vi8", "vbo", "vby", "vck", "vpb", "vid", "vone", "veqp", "vza", "vlate", "sperm", "sbs", "ser",
-               "vscan", "vS", "vka", "vpr2", "pE2", "veq", "vuu", "ssg", "sk", "eC", "eC16", "vcm", "gR0", "gR1", "gR2", "vrt", "eK", "gV", "vpk", "vkeep",
+               "vz", "sz", "vcon", "vc", "vc0", "vc2", "vc3", "vi8", "vbo", "vby", "vck", "sck", "vpb", "vid", "vone", "veqp", "vza", "vlate", "sperm", "sbs", "ser",
+               "vscan", "vS", "vka", "vpr2", "pE2", "veq", "vuu", "ssg0", "ssg1", "gneg", "sk", "eC", "eC16", "vcm", "gR0", "gR1", "gR2", "vrt", "eK", "gV", "vpk", "vkeep",
                "ePL", "vpr0", "vpr1", "vab", "gG0", "gG1", "vP", "pA", "pB", "pX", "pY", "pC", "pK", "pPL", "pS", "ph0", "ph1", "ph2", "ph3",
-               "pE0", "pE1", "pO", "swf", "sdg", "vcv", "vtr", "ptab", "vpv", "gXB", "gPN", "dpn", "gz4", "tl", "tr", "wl", "wr", "kl", "vl", "kr0", "kr1",
+               "pE0", "pE1", "pO0", "pO1", "vY0", "vY1", "swf", "sdg", "vcv", "vtr", "ptab", "vpv", "gXB", "gXC", "gp0", "gp1", "slc", "gPN", "dpn", "gz4", "tl", "tr", "wl", "wr", "kl", "vl", "kr0", "kr1",
                "eL0", "eL1", "eL2", "eL3", "pL0", "pL1", "pL2", "pL3", "vr0_0", "vr0_1", "vr0_2", "vr0_3", "vr1_0", "vr1_1"]
               + ["w" + n for n in LISTS] + ["s" + n for n in LISTS] + ["s" + n + k for n in ("L3", "M3") for k in "bc"])
 
@@ -144,28 +144,36 @@ def rank_program(g, core, T, topo):
     need("v", "gi")
     bits(0, 4, 7)
     done(V.tensor_scalar(T.I16[:], m, 4, None, A.logical_shift_right), "vi8")
+    done(V.memset(T.ZER[:], 0.0), "veqp")
+    need("v", "vc")
+    done(V.tensor_copy(cf(0), T.CI[:, 0:1]), "vc0")
     bits(2, 0, 127)
     bits(1, 4, 1)
     bits(3, 0, 15)
+    need("v", "vc0", "vi8")
+    done(V.tensor_scalar(bo, T.I16[:], cf(0), None, A.is_equal), "vbo")
     bits(4, 0, 112)
     bits(5, 0, 3)
     bits(6, 3, 1)
-    need("v", "vc")
-    done(V.tensor_copy(T.CF[:, 0:7], T.CI[:, 0:7]), "vc2")
-    done(V.memset(T.ZER[:], 0.0), "veqp")
+    bits(7, 0, 1)
     done(V.memset(T.ONB[:], 1.0), "veqp")
-    need("v", "vc2", "vi8")
-    done(V.tensor_scalar(bo, T.I16[:], cf(0), None, A.is_equal), "vbo")
-    done(V.tensor_scalar(ck(0), cf(6), -5.125, 5.0, A.mult, A.add), "vck")
-    done(V.tensor_scalar(ck(1), cf(6), 0.125, -0.125, A.mult, A.add), "vck")
+    need("v", "vc")
+    done(V.tensor_copy(T.CF[:, 1:8], T.CI[:, 1:8]), "vc2")
     need("v", "dpri")
     done(V.tensor_copy(T.PB0[:], T.PRI[:]), "vpb")
+    need("v", "vc2")
+    need("s", "vc2")
+    done(S.activation(ck(0), cf(6), IDENT, bias=5.0, scale=-5.125), "sck")
+    done(S.activation(ck(1), cf(6), IDENT, bias=-0.125, scale=0.125), "sck")
     done(V.tensor_scalar(ck(2), cf(6), 1.0 / 128, 1.0 / 5120, A.mult, A.max), "vck")
     done(V.tensor_scalar(ck(3), cf(6), 1024.50390625, 1024.5001220703125, A.mult, A.max), "vck")
-    need("v", "vbo", "vck")
+    done(V.tensor_scalar(T.IDW[:], T.IM[:], cf(2), None, A.is_equal), "vid")
+    done(V.tensor_scalar(cg(0), cf(1), 0.0, None, A.is_equal), "vid")
+    done(V.tensor_scalar(cg(4), cf(5), 3.0, None, A.is_equal), "vid")
+    need("s", "vbo", "sck")
     for lo, n in ((0, 16), (16, 16), (32, 8)):
-        done(V.tensor_scalar(T.BY[:, :, lo:lo + n], T.BO[:, :, 0:n], ck(0), None, A.mult), "vby")
-    done(V.tensor_scalar(T.BX[:], bo, ck(1), None, A.mult), "vby")
+        done(S.activation(T.BY[:, :, lo:lo + n], T.BO[:, :, 0:n], COPY, scale=ck(0)), "vby")
+    done(S.activation(T.BX[:], bo, COPY, scale=ck(1)), "vby")
     need("g", "vbo")
     done(g.affine_select(T.TU[:], bo, [[-1, 128]], A.is_gt, 0.0, 0, 1), "gtu")
     done(g.iota(T.THR[:], [[128, 4], [512, 10], [5120, 16]], 128, 0), "gthr")
@@ -174,8 +182,9 @@ def rank_program(g, core, T, topo):
     tot["wr"] = sum(inc.values())
 
     def consts_a():
-        done(V.tensor_scalar(T.IDW[:], T.IM[:], cf(2), None, A.is_equal), "vid")
-        done(V.tensor_scalar(cg(0), cf(1), 0.0, None, A.is_equal), "vid")
+        perms()
+        need("v", "dtab")
+        done(V.tensor_copy(T.TX[:], T.TI[:]), "vcv")
         done(V.tensor_scalar(T.ZA[:], T.IM[:, 0:144], cf(4), None, A.is_equal), "vza")
         done(V.memset(T.K1[:, 0:16], 1025.0), "vc3")
 
@@ -183,20 +192,19 @@ def rank_program(g, core, T, topo):
         done(V.tensor_scalar(cg(1), cf(3), 2.0, -2048.0, A.is_equal, A.mult), "vc3")
         done(V.tensor_scalar(cg(2), cf(3), 1.0, None, A.not_equal), "vc3")
         done(V.tensor_scalar(cg(3), cf(3), 1.0, None, A.is_equal), "vc3")
-        done(V.tensor_scalar(cg(4), cf(5), 3.0, None, A.is_equal), "vc3")
         done(V.tensor_scalar(cg(5), cf(3), 4.0, None, A.is_ge), "vc3")
-        done(V.memset(T.CNEG[:], -4416.0), "vlate")
+        done(V.tensor_scalar(cg(6), cf(7), -1.0, 159.53125, A.mult, A.add), "vc3")
+        done(V.tensor_scalar(cg(7), cf(3), 1.0, None, A.is_le), "vc3")
+
+    def consts_c():
+        done(V.tensor_scalar(T.AB[:, NS:NS + 16], T.ZER[:, 0:16], cf(7), None, A.add), "vc3")
 
     def perms():
         need("s", "vid", "vc2")
         for n, (lo, msk) in enumerate([(16, cg(0)), (32, cf(1)), (0, cg(0)), (16, cf(1))]):
             done(S.activation(T.PM[:, 128 * n:128 * n + 128], T.IDW[:, lo:lo + 128], COPY, scale=msk), "sperm")
-
-    def signs():
         for k in range(2):
             done(S.activation(T.BS[:, k:128:2], T.BO[:, :, k:16:2], COPY, scale=0.0625 - 0.125 * k), "sbs")
-        need("s", "sbs", "vc3")
-        done(S.activation(T.ER[:], T.BS[:], COPY, scale=cg(4)), "ser")
 
     def mark(out, pattern, base, value, sem, over=None):
         need("g", over or "veqp")
@@ -205,29 +213,38 @@ def rank_program(g, core, T, topo):
 
     def marks_a():
         mark(T.ZN[:], [[-16, 9], [-1000, 16]], 16, 1.0, "gz0")
-        mark(T.PS[:, 0, :], [[-16, 9], [-1000, 2], [-2, 8]], 15, 160.0, "gps")
+        mark(T.PS[:, 0, :], [[-16, 9], [-1000, 2], [-2, 8]], 17, 1024.0, "gp0")
         mark(T.ZN[:], [[-16, 9], [-1000, 16]], 15, 1.0, "gzz", "gz0")
 
     def marks_b():
+        need("g", "gp0")
+        done(g.affine_select(T.PS[:, 0, :], T.PS[:, 0, :], [[0, 9], [1, 16]], A.not_equal, 0.0, 0, 0), "gp1")
         mark(T.SD[:, 1, :], [[-16, 8], [-1, 16]], 1, -4096.0, "gsd0")
+        mark(T.PS[:, 0, :], [[-16, 9], [-1000, 2], [-2, 8]], 15, 160.0 - 1024.0, "gps", "gp1")
         for n, wt in ((1, -624.0), (2, -159.0)):
             mark(T.PS[:, n, :], [[-16, 9], [-1000, 2], [-2, 8]], 15, wt, "gps")
-        mark(T.SD[:, 0, :], [[-16, 8], [-1, 16]], 0, 4096.0, "gsd")
-        mark(T.SD[:, 2, :], [[-16, 8], [-1000, 16]], -15, -4096.0, "gsd")
         need("g", "gsd0")
         done(g.affine_select(T.SD[:, 1, :], T.SD[:, 1, :], [[0, 8], [1, 16]], A.not_equal, 0.0, 0, 0), "gsd")
 
     def marks_c():
+        mark(T.PS[:, 3, :], [[-16, 9], [-1000, 16]], 1, 1024.0, "gps")
+        mark(T.SD[:, 0, :], [[-16, 8], [-1, 16]], 0, 4096.0, "gsd")
+        mark(T.SD[:, 2, :], [[-16, 8], [-1000, 16]], -15, -4096.0, "gsd")
+        mark(T.SD[:, 3, :], [[-16, 8], [-1, 16]], 0, -1.0, "gsd")
+        done(g.iota(T.CNEG[:], [[0, 128]], -4416, 0, allow_small_or_imprecise_dtypes=True), "gneg")
         mark(T.LB[:], [[-16, 9], [-1000, 8], [0, 2]], 16, 1.0, "glb0")
         done(g.affine_select(T.KO[:], T.ZER[:, 0:NC], [[0, 2], [1, 2], [0, 10]], A.not_equal, 4096.0, -1, 0), "gko")
         mark(T.LB[:], [[-16, 9], [-1000, 8], [0, 2]], 15, 1.0, "glb", "glb0")
 
     def marks_d():
+        done(g.iota(T.STEP[:], [[0, 128]], -2560, 0, allow_small_or_imprecise_dtypes=True), "vlate")
         mark(T.ZN[:], [[-16, 9], [-1000, 16]], 12, 1.0, "gz4", "pL3")
 
     STEP = {"L0": 3, "L1": 4, "L2": 5, "L3": 6, "M1": 2, "M2": 1, "M3": 0}
 
     def diags_own():
+        need("s", "sbs")
+        done(S.activation(T.ER[:], T.BS[:], COPY, scale=cg(4)), "ser")
         need("s", "dw", "vid")
         done(S.activation(T.WF[:], T.WS[:], COPY), "swf")
         need("s", "swf")
@@ -257,9 +274,10 @@ def rank_program(g, core, T, topo):
         need(q, "dx" if win == "X" else "g" + win, WHERE[at][2])
         gather(q, T["X" + lst][:, lo:hi], T[win][:], lst_ap(at, lo, hi), "s" + lst + tag)
 
-    def back(q, lo, hi):
-        need(q, "vpv", "dx")
-        gather(q, T.XB[:, lo:hi], T.X[:], T.PV[:, lo // 16:hi // 16], "gXB")
+    def back(out, q, lo, hi):
+        src = "X" if out == "XB" else "XB"
+        need(q, "vpv", "dx" if out == "XB" else "gXB")
+        gather(q, T[out][:, lo:hi], T[src][:], T.PV[:, lo // 16:hi // 16], "g" + out)
 
     def ahead(q, lo, hi):
         need(q, "vpv", "dpw")
@@ -271,11 +289,10 @@ def rank_program(g, core, T, topo):
         done(g.sync.dma_start(T.PW[7:128:16, :], T.PN[3:128:16, :]), "dpn", 16)
 
     def prv_turn():
-        need("v", "dtab")
-        done(V.tensor_copy(T.TX[:], T.TI[:]), "vcv")
-        consts_b()
         need("v", "vcv")
         done(V.transpose(T.TT[:], T.TX[:]), "vtr")
+        consts_b()
+        consts_c()
         need("t", "sperm", "vtr")
         for b1 in range(8):
             for ga in range(2):
@@ -283,10 +300,10 @@ def rank_program(g, core, T, topo):
                 ins = P.matmul(T.E0[:, b1:256:8], T.PM[:, 128 * n:128 * n + 128], T.TT[:, b1 // 2:8:4, 16 * ga:16 * ga + 16], ga == 0, ga == 1)
         done(ins, "ptab")
 
-    def keeps():
-        need("t", "eK", "ePL", "vpk", "vlate")
-        P.matmul(T.QA[:, 0:128], T.C128[:], T.CNEG[:], True, False)
-        sampled("QA", False, False)
+    def keeps(bank="QA"):
+        need("t", "eK", "eL2", "gneg")
+        P.matmul(T[bank][:, 0:128], T.C128[:], T.CNEG[:], True, False)
+        sampled(bank, False, False)
 
     def pick_p(lst, q, lo=0, hi=NS, far=False):
         need(q, "dpw", WHERE[lst][2])
@@ -333,9 +350,8 @@ def rank_program(g, core, T, topo):
     def serve(a):
         KL, VS, VR = T["KL%d" % a], T["VS%d" % a], T["VR%d" % a]
         if a == 0:
-            for q, lo, hi in (("v", 0, 14), ("s", 14, 30)):
-                need(q, "dval", "kr0")
-                gather(q, VS[:, 16 * lo:16 * hi], own_val, KL[:, lo:hi], "gV")
+            need("s", "dval", "kr0")
+            gather("s", VS[:], own_val, KL[:, 0:30], "gV")
             need("g", "gV")
             send(peers, lambda c: VS[:, NQ * place(c, core):NQ * place(c, core) + NQ], lambda c: VR[:, NQ * rank:NQ * rank + NQ],
                  lambda c: T.sem["vr0_%d" % rank], "vl")
@@ -375,36 +391,47 @@ def rank_program(g, core, T, topo):
         done(S.activation(T.K4[:], T.SS[:], IDENT, bias=1025.2509765625, scale=1.0 / 512), "sk")
         done(S.activation(T.K40[:], T.SS[:], IDENT, bias=129.4751, scale=1.0 / 5120), "sk")
 
-    def pairs_t():
-        need("t", "gps", "sk", "vscan", "eL2")
+    def pairs_t(pb, bank, bank2):
+        need("t", "gps", "sk")
         for cp in range(2):
-            for n, src in enumerate((T.K1[:, 16 + cp:144:2], T.K4[:, cp:128:2], T.K40[:, cp:128:2])):
-                P.matmul(T.QA[:, 128:192], T.PS[:, n, 16 - 8 * cp:144 - 8 * cp], src, cp + n == 0, cp + n == 3)
-        done(sampled("QA", True, True), "pS")
+            for n, src in enumerate((T.K1[:, 16 + cp:144:2], T.K4[:, cp:128:2], T.K40[:, cp:128:2], T.K1[:, 15 + cp:143:2])):
+                ins = P.matmul(T[bank][:, 0:64], T.PS[:, n, 16 - 8 * cp:144 - 8 * cp], src, cp + n == 0, cp + n == 4)
+        done(ins, "pPL")
+        need("t", "gsd")
+        P.matmul(T[bank2][:, 0:128], T.SD[:, 3, :], pb[:], True, False)
+        done(sampled(bank2, False, True), "pS")
 
-    def pairs_v(pb):
-        need("v", "pS", "gG0", "gG1")
-        done(V.tensor_scalar(T.PL[:], T.QA[:, 128:192], 496734.0, None, A.add), "ePL")
-        done(V.tensor_tensor(T.PK[:], pb[:], T.QA[:, 0:128], A.subtract), "vpk")
+    def pairs_v(bank):
+        need("v", "pPL", "gG0", "gG1")
+        done(V.tensor_scalar(T.PL[:], T[bank][:, 0:64], 496734.0 + 1024.0, float(NS), A.add, A.min), "ePL")
 
-    def keep_v():
-        need("v", "vpk")
-        done(V.tensor_scalar(T.KEEP[:], T.PK[:], 1.0, None, A.max), "vkeep")
+    def pairs_s(bank):
+        need("s", "pS", "vP")
+        done(S.activation(T.KEEP[:], T[bank][:, 0:128], AF.Relu, scale=-1.0), "vpk")
+
+    def new_priorities(out):
+        need("v", "pO1", "vpk")
+        done(V.tensor_tensor(out[:], T.QA[:, 0:128], T.KEEP[:], A.max), "vP")
 
     for a in range(2):
         pb = T.PB0 if a == 0 else T.PB1
         KS, KL, VR = T["KS%d" % a], T["KL%d" % a], T["VR%d" % a]
-        if a:
-            heads()
-        need("t", "vbo", "vpb", "vP")
-        done(P.matmul(T.QA[:, 0:128], bo, pb[:], True, True), "pA")
         if a == 0:
+            need("t", "vbo", "vpb")
+            done(P.matmul(T.QA[:, 0:128], bo, pb[:], True, True), "pA")
             heads()
-        tails(pb)
-        need("v", "pA", "vone")
-        done(V.tensor_tensor_scan(T.CS[:], T.ONE[:], T.QA[:, 0:128], 0.0, A.mult, A.add), "vscan")
-        need("v", "vscan")
+            tails(pb)
+            need("v", "pA", "vone")
+            done(V.tensor_tensor_scan(T.CS[:], T.ONE[:], T.QA[:, 0:128], 0.0, A.mult, A.add), "vscan")
+        else:
+            need("v", "pA", "vlate")
+            done(V.tensor_tensor_scan(T.CS[:], T.STEP[:], T.H3[:, 0:128], 0.0, A.add, A.add), "vscan")
+            new_priorities(T.PB1)
+        need("v", "vscan", "vck")
         done(V.tensor_scalar(T.KA[:], T.CS[:], ck(2), ck(3), A.mult, A.add), "vka")
+        if a:
+            need("t", "vP")
+            tails(pb)
         need("t", "vka", "vby")
         done(P.matmul(T.H1[:, 0:320], T.KA[:], T.BY[:], False, True), "pY")
         done(P.matmul(T.H0[:, 0:128], T.KA[:], T.BX[:], False, True), "pX")
@@ -416,45 +443,48 @@ def rank_program(g, core, T, topo):
         done(V.tensor_scalar(T.EQP[:, :, 16:32], T.H0[:, 0:128], 0.0, 0.5, A.is_equal, A.mult), "veq")
         done(V.tensor_scalar(T.UU[:], T.H0[:, 0:128], -0.5, 0.5, A.max, A.min), "vuu")
         need("s", "pY")
-        done(S.activation(T.SG[:], T.H1[:, 0:320], AF.Sign, bias=-39974.5), "ssg")
+        for k in range(2):
+            done(S.activation(T.SG[:, 160 * k:160 * k + 160], T.H1[:, 160 * k:160 * k + 160], AF.Sign, bias=-39974.5), "ssg%d" % k)
         need("t", "veqp")
         P.matmul(T.H2[:, 0:NC], bo, T.ZER[:, 0:NC], True, False)
-        need("t", "veq", "ssg")
         for gr in range(8):
+            need("t", "veq", "ssg%d" % (gr // 4))
             lo = 16 - 16 * (gr % 2)
             P.matmul(T.H2[32 * (gr // 2):32 * (gr // 2) + 32, 0:NC], T.EQP[:, gr, lo:lo + 32], T.SG[:, NC * gr:NC * gr + NC], False, False)
         need("t", "vuu")
         done(P.matmul(T.H2[:, 0:NC], T.UU[:], T.ONB[:], False, True), "pC")
-        if a == 0:
+        if a:
+            back("XC", "v", 0, 320)
+        else:
             marks_a()
-            perms()
             prv_turn()
             diags_own()
         need("v", "pC")
         done(V.tensor_scalar(T.COL[:], T.H2[:, 0:NC], 64.0, 127.0, A.add, A.min), "eC")
         done(V.tensor_scalar(T.C16[:], T.H2[:, 0:NC], 64.0, 16.0, A.add, A.mult), "eC16")
+        if a == 0:
+            need("s", "ptab")
+            done(S.activation(T.PV[:], T.E0[:, 0:256], COPY), "vpv")
         counts()
         need("v", "eC", "vS", "gthr")
         done(V.tensor_tensor(T.CM[:], T.SS[:].indirect(T.COL[:]), T.THR[:], A.is_lt), "vcm")
         need("t", "eC16", "vid", "vza")
         P.matmul(T.H3[:, 0:NC], ident, T.C16[:], True, False)
         if a:
-            pairs_t()
-            back("s", 640, 2048)
+            pairs_t(pb, "E0", "E1")
+            back("XC", "s", 320, 1664)
         else:
-            signs()
+            back("XB", "s", 0, 640)
         need("t", "vcm")
         for ro in range(16):
             ins = P.matmul(T.H3[:, 0:NC], T.ZA[:, 16 - ro:144 - ro], T.CM[:, ro:NS:16], False, ro == 15)
         done(ins, "pL0")
         if a == 0:
-            need("v", "ptab")
-            done(V.tensor_copy(T.PV[:], T.E0[:, 0:256]), "vpv")
-            back("s", 0, 384)
-            back("v", 384, 640)
+            back("XB", "v", 640, 1088)
         else:
-            pairs_v(pb)
-            keep_v()
+            pairs_v("E0")
+            pairs_s("E1")
+            back("XC", "v", 1664, 2048)
         need("v", "pL0")
         done(V.tensor_scalar(T.L0[:], T.H3[:, 0:NC], 2047.0, None, A.min), "eL0")
         need("v", "eL0", "dpw", "vc3", "dpn")
@@ -466,11 +496,15 @@ def rank_program(g, core, T, topo):
         done(V.transpose(T.RT[:], T.R0[:]), "vrt")
         if a:
             pick_x("M1", "s", 0, 320, "", "XB", "L0")
+            pick_x("M1", "v", 320, NS, "", "XB", "L0")
+        else:
+            back("XB", "v", 1088, 1344)
+            back("XB", "s", 1344, 1536)
         need("t", "sperm", "vscan", "vS", "gko", "ePL", "vpk")
         if a:
             P.matmul(T.QA[:, 0:NC], T.C128[:], T.KO[:], True, False)
         need("t", "vrt")
-        rows = [("QB", 0, 0, None), ("QB", NC, 1, "pL1"), ("QA", 0, 2, "pK")] + [("E0", 0, 4, "pL2")] * a
+        rows = [("QA", 0, 2, "pK"), ("QB", 0, 0, None), ("QB", NC, 1, "pL1")] + [("E0", 0, 4, "pL2")] * a
         for bank, col, row, sem in rows:
             for h in range(2):
                 for gb in range(2):
@@ -479,9 +513,9 @@ def rank_program(g, core, T, topo):
                     ins = P.matmul(T[bank][:, col + h:col + NC:2], T.PM[:, 128 * n:128 * n + 128], T.RT[:, :, 16 * gb + row], first, end)
             if sem:
                 done(ins, sem)
-        evac(1, "QB", True)
         need("v", "pK")
         done(V.tensor_scalar(KS[:], T.QA[:, 0:NC], 2048.0, None, A.add), "eK")
+        evac(1, "QB", True)
         need("g", "eK")
         if a == 0:
             send(peers, lambda c: KS[:, 10 * T.rank_of(c):10 * T.rank_of(c) + 10], lambda c: KL[:, 10 * place(core, c):10 * place(core, c) + 10],
@@ -491,69 +525,62 @@ def rank_program(g, core, T, topo):
         else:
             send([twin], lambda c: KS[:, 20 * theirs:20 * theirs + 20], lambda c: KL[:, 0:20], lambda c: T.sem.kr1, "kl", wide)
             tot["kr1"] = len(topo.engines(twin, core))
-        need("t", "eC16", "eL0", "vuu", "ssg")
+        need("t", "eC16", "eL0", "vuu", "ssg1")
         if a == 0:
             pick_p("M1", "v")
             pick_p("L1", "s")
             chase(2, "QA", True, "eK")
             pick_x("L1", "s")
-            diags("L0", "L1", "M1", "L2", "M2")
+            back("XB", "v", 1536, 2048)
+            diags("L0", "L1")
             hsum("L0", 0)
             evac(2, "QA", True)
             serve_own(a, "s")
-            diags("M3", "L3")
             hsum("L1", 1)
             reward(0)
             reward(1)
+            pick_p("L2", "v")
             serve(a)
             marks_c()
-            pick_p("M2", "v")
-            pick_p("L2", "s")
-            pairs_t()
-            chase(3, "QB", True, "eL1")
-            marks_d()
-            pairs_v(pb)
-            reward(2)
-            keeps()
-            pick_x("M1", "v", 0, 448)
-            keep_v()
-            evac(3, "QB", True)
             pick_x("L2", "s")
-            pick_x("M1", "s", 448, NS)
+            chase(3, "QB", False, "eL1")
+            marks_d()
+            diags("L2", "M1", "M2")
+            reward(2)
+            hsum("L2", 2)
+            pick_x("M1", "v", win="XB", at="L0")
+            evac(3, "QB", False)
+            diags("M3", "L3")
+            pick_x("M2", "s", win="XB", at="M1")
+            hsum("M1", 3)
             for k in range(3):
                 reward(k, parts[2:])
-            hsum("L2", 2)
-            hsum("M1", 3)
-            pick_x("M2", "v", 0, 320)
-            pick_x("M2", "s", 320, NS)
             hsum("M2", 4)
-            last = (("M3", "v", "X", "M3"), ("L3", "s", "X", "L3"))
+            last = (("L3", "v", "X", "L3"), ("M3", "s", "XB", "M2"))
         else:
-            WHERE["M2"] = ("LM3", NC, "eL3")
             pick_p("L1", "v", far=True)
-            pick_p("M1", "s")
+            pick_x("L1", "s")
             hsum("L0", 0)
             keeps()
-            chase(3, "QB", True, "eL1", 1)
+            hsum("M1", 1)
+            chase(3, "QB", False, "eL1", 1)
             evac(2, "E0", False)
             serve_own(a, "v")
-            pick_x("M1", "s", 320, NS, "", "XB", "L0")
+            pick_x("M2", "s", 0, 320, "", "XB", "M1")
             serve(a)
             need("t", "eL2")
             reward(0)
             reward(1)
-            hsum("M1", 1)
-            evac(3, "QB", True)
+            hsum("L1", 2)
+            evac(3, "QB", False)
             for k in range(2):
                 reward(k, parts[2:])
-            pick_x("L1", "v")
-            pick_x("M2", "s", win="XB", at="M1")
-            pick_x("L2", "v", 0, 256)
-            pick_x("L2", "s", 256, NS)
-            hsum("L1", 2)
+            pick_x("M2", "s", 320, NS, "", "XB", "M1")
+            pick_x("L2", "v", 0, 448)
+            pick_x("L2", "s", 448, NS)
             hsum("M2", 3)
             hsum("L2", 4)
-            last = (("L3", "v", "X", "L3"), ("M3", "s", "XB", "M2"))
+            last = (("L3", "v", "X", "L3"), ("M3", "s", "XC", "M1"))
         for tag, (bank, lo, n, qs) in zip(("", "b", "c"), parts):
             for lst, q, win, at in last:
                 pick_x(lst, q, lo, lo + n, tag, win, at)
@@ -561,33 +588,53 @@ def rank_program(g, core, T, topo):
                 hsum(lst, 5 + k, qs, tag)
         if a == 0:
             ahead("s", 0, 768)
+            done(S.activation(T.LC[:], bo, COPY, scale=cg(7)), "slc")
         for k, (bank, lo, n, qs) in enumerate(parts):
             for q in qs:
                 need("v", "ph%d" % q, "vr1_%d" % (k == 0) if a else "vr0_%d" % q)
                 done(V.tensor_tensor(T.PROD[:, NQ * q:NQ * q + NQ], VR[:, NQ * q:NQ * q + NQ], T["H%d" % q][:, 0:NQ], A.mult), "vpr%d" % k)
             need("t", "vpr%d" % k, "sbs")
             done(P.matmul(T[bank][:, 0:n], T.BS[:], T.PROD[:, lo:lo + n], False, True), "pE%d" % k)
+        if a == 0:
+            pairs_t(pb, "H2", "H1")
+            pairs_s("H1")
+            keeps()
         for k, (bank, lo, n, qs) in enumerate(parts):
+            if a == 0 and k == 2:
+                pairs_v("H2")
             need("v", "pE%d" % k)
-            done(V.tensor_scalar(T.AB[:, lo:lo + n], T[bank][:, 0:n], 0.0, 63.0, A.max, A.min), "vab")
+            done(V.tensor_scalar(T.AB[:, lo:lo + n], T[bank][:, 0:n], 1.0, 63.0, A.max, A.min), "vab")
+        if a == 0:
+            need("t", "vpk")
+            P.matmul(T.H3[:, 0:128], bo, T.KEEP[:], True, False)
+            heads()
+        else:
+            keeps("H0")
         need("v", "vab", "ePL")
         need("s", "vab", "ePL")
         for b in range(2):
-            lo = 512 * b
-            done(V.tensor_scalar(T.GB[:, lo:lo + 256], T.AB[:].indirect(T.PL[:, lo // 16:lo // 16 + 16]), 159.53125, None, A.add), "gG%d" % b)
-            done(S.activation(T.GB[:, lo + 256:lo + 512], T.AB[:].indirect(T.PL[:, lo // 16 + 16:lo // 16 + 32]), IDENT, bias=159.53125), "gG%d" % b)
-            need("t", "gG%d" % b, "glb")
+            lo, out = 512 * b, "H0" if a + b == 2 else "QA"
+            done(V.tensor_scalar(T.GB[:, lo:lo + 256], T.AB[:].indirect(T.PL[:, lo // 16:lo // 16 + 16]), cg(6), None, A.add), "gG%d" % b)
+            done(S.activation(T.GB[:, lo + 256:lo + 512], T.AB[:].indirect(T.PL[:, lo // 16 + 16:lo // 16 + 32]), IDENT, bias=cg(6)), "gG%d" % b)
+            need("t", "gG%d" % b, "glb", "slc")
+            for h in range(8 * (1 - a)):
+                ins = P.matmul(T.H3[:, 64 * b:64 * b + 64], T.LC[:], T.GB[:, lo + h:lo + 512:8], False, b == 1 and h == 7)
+            if b > a:
+                done(ins, "pA")
             for h in range(8):
-                ins = P.matmul(T.QA[:, 64 * b:64 * b + 64], T.LB[:, 16 - 2 * h:144 - 2 * h], T.GB[:, lo + h:lo + 512:8], False, b == 1 and h == 7)
-        done(ins, "pO")
+                ins = P.matmul(T[out][:, 64 * b:64 * b + 64], T.LB[:, 16 - 2 * h:144 - 2 * h], T.GB[:, lo + h:lo + 512:8], False, a + b > 0 and h == 7)
+            if a + b:
+                done(ins, "pO%d" % b)
         if a == 0:
-            ahead("v", 768, 1024)
-            ahead("s", 1024, 2048)
+            ahead("v", 768, 1152)
+            ahead("s", 1152, 2048)
             merge()
-        need("v", "pO", "vkeep")
-        done(V.tensor_tensor((T.YO if a else T.PB1)[:], T.QA[:, 0:128], T.KEEP[:], A.max), "vP")
-    need("y", "vP")
-    done(g.sync.dma_start(T.y[:], T.YO[:]), "dy", 16)
+    for b, bank in enumerate(("QA", "H0")):
+        cols = slice(64 * b, 64 * b + 64)
+        need("v", "pO%d" % b)
+        done(V.tensor_tensor(T.YO[:, cols], T[bank][:, cols], T.KEEP[:, cols], A.max), "vY%d" % b)
+        need("y", "vY%d" % b)
+        done(g.sync.dma_start(T.y[:, cols], T.YO[:, cols]), "dy", 16)
     need("y", "dy")
     for n in sorted(tot):
         if max([got.get((q, n), 0) for q in Q]) < tot[n]:

from concourse.bass import DstId, RemoteDMATransfer
from concourse.mybir import dt, AluOpType, AxisListType, ActivationFunctionType

F16, BF, F32, I32, U16 = "float16", "bfloat16", "float32", "int32", "uint16"
NS, NC, NQ = 640, 40, 160
LISTS = ["L0", "L1", "M1", "L2", "M2", "L3", "M3"]
SCRATCH = {
    "PRI": ("sbuf", [128, 128], I32), "PB0": ("sbuf", [128, 128], BF), "PB1": ("sbuf", [128, 128], BF),
    "X": ("sbuf", [128, 2048], BF), "VALB": ("sbuf", [128, 8192], BF), "KO": ("sbuf", [128, NC], BF), "PW": ("sbuf", [128, 2048], I32),
    "IM": ("sbuf", [128, 160], I32), "I16": ("sbuf", [128, 128], I32), "KP": ("sbuf", [128, 1], I32), "THR": ("sbuf", [128, NS], I32),
    "CI": ("sbuf", [128, 8], I32), "CF": ("sbuf", [128, 8], F32), "CG": ("sbuf", [128, 8], F32),
    "BO": ("sbuf", [128, 8, 16], BF), "TU": ("sbuf", [128, 128], BF), "IDW": ("sbuf", [128, 160], BF), "ONB": ("sbuf", [128, NC], BF),
    "BY": ("sbuf", [128, 8, NC], BF), "BX": ("sbuf", [128, 128], BF), "C1K": ("sbuf", [128, 128], BF), "CK": ("sbuf", [128, 4], F32), "JI": ("sbuf", [128, 448], BF), "C128": ("sbuf", [128, 128], BF),
    "CNEG": ("sbuf", [128, 128], BF), "ZER": ("sbuf", [128, 144], BF), "EQP": ("sbuf", [128, 8, 48], BF), "UU": ("sbuf", [128, 128], BF),
    "SG": ("sbuf", [128, 8 * NC], BF), "PM": ("sbuf", [128, 512], BF), "ZA": ("sbuf", [128, 144], BF), "ZN": ("sbuf", [128, 144], BF),
    "BS": ("sbuf", [128, 128], BF), "KEEP": ("sbuf", [128, 128], BF), "ER": ("sbuf", [128, 128], BF), "LB": ("sbuf", [128, 144], BF),
    "LC": ("sbuf", [128, 128], BF), "STEP": ("sbuf", [128, 128], F32), "XC": ("sbuf", [128, 2048], BF), "PS": ("sbuf", [128, 4, 144], BF), "SD": ("sbuf", [128, 4, 128], BF),
    "ONE": ("sbuf", [128, 128], F32), "CS": ("sbuf", [128, 128], F32), "SS": ("sbuf", [128, 128], F32),
    "KA": ("sbuf", [128, 128], F16), "K1": ("sbuf", [128, 144], F16), "K4": ("sbuf", [128, 128], F16),
    "K40": ("sbuf", [128, 128], BF), "COL": ("sbuf", [128, NC], U16), "C16": ("sbuf", [128, NC], F16), "CM": ("sbuf", [128, NS], BF),
    "R0": ("sbuf", [128, NS], F16), "RT": ("sbuf", [128, NS // 32, 32], F16), "L0": ("sbuf", [128, NC], U16),
    "KS0": ("sbuf", [128, NC], U16), "KS1": ("sbuf", [128, NC], U16), "KL0": ("sbuf", [128, 32], U16), "KL1": ("sbuf", [128, 32], U16),
    "VS0": ("sbuf", [128, 3 * NQ], BF), "VS1": ("sbuf", [128, 2 * NQ], BF), "VR0": ("sbuf", [128, NS], BF), "VR1": ("sbuf", [128, NS], BF),
    "PROD": ("sbuf", [128, NS], F16), "AB": ("sbuf", [128, NS + 16], F32), "PL": ("sbuf", [128, 64], U16), "GB": ("sbuf", [128, 1024], BF),
    "PK": ("sbuf", [128, 128], F32), "YO": ("sbuf", [128, 128], F32),
    "WS": ("sbuf", [128, 7], BF), "WF": ("sbuf", [128, 7], F32), "WR": ("sbuf", [128, 32], BF),
    "DG": ("sbuf", [128, 28 * 128], BF), "TI": ("sbuf", [128, 8, 32], I32), "TX": ("sbuf", [128, 8, 32], F16), "TT": ("sbuf", [128, 8, 32], F16),
    "PV": ("sbuf", [128, 256], U16), "PN": ("sbuf", [128, 2048], I32), "XB": ("sbuf", [128, 2048], BF),
}
for _n in LISTS:
    SCRATCH["X" + _n] = ("sbuf", [128, NS], BF)
for _n in "123":
    SCRATCH["LM" + _n] = ("sbuf", [128, 3 * NC], U16)
for _n in "12":
    SCRATCH["R" + _n] = ("sbuf", [128, 2, NS], F16)
for _n in ["QA", "QB", "E0", "E1", "H0", "H1", "H2", "H3"]:
    SCRATCH[_n] = ("psum", [128, 512], F32)
SEMAPHORES = (["dpri", "dw", "dx", "dval", "dpw", "dy", "dtab", "gi", "gj", "gtu", "gthr", "glb0", "glb", "gps", "gz0", "gzz", "gsd0", "gsd", "gko",
               "vz", "sz", "vcon", "vc", "vc0", "vc2", "vc3", "vi8", "vbo", "vby", "vck", "sck", "vpb", "vid", "vone", "veqp", "vza", "vlate", "sperm", "sbs", "ser",
               "vscan", "vS", "vka", "vpr2", "pE2", "veq", "vuu", "ssg0", "ssg1", "gneg", "sk", "eC", "eC16", "vcm", "gR0", "gR1", "gR2", "vrt", "eK", "gV", "vpk", "vkeep",
               "ePL", "vpr0", "vpr1", "vab", "gG0", "gG1", "vP", "pA", "pB", "pX", "pY", "pC", "pK", "pPL", "pS", "ph0", "ph1", "ph2", "ph3",
               "pE0", "pE1", "pO0", "pO1", "vY0", "vY1", "swf", "sdg", "vcv", "vtr", "ptab", "vpv", "gXB", "gXC", "gp0", "gp1", "slc", "gPN", "dpn", "gz4", "tl", "tr", "wl", "wr", "kl", "vl", "kr0", "kr1",
               "eL0", "eL1", "eL2", "eL3", "pL0", "pL1", "pL2", "pL3", "vr0_0", "vr0_1", "vr0_2", "vr0_3", "vr1_0", "vr1_1"]
              + ["w" + n for n in LISTS] + ["s" + n for n in LISTS] + ["s" + n + k for n in ("L3", "M3") for k in "bc"])


def rank_program(g, core, T, topo):
    rank = T.rank_of(core)
    if rank is None:
        return
    A = AluOpType
    AF = ActivationFunctionType
    COPY, IDENT = AF.Copy, AF.Identity
    V, S, P = g.vector, g.scalar, g.tensor
    Q = {"v": V, "s": S, "t": P, "y": g.sync, "g": g}
    tot, got = {}, {}

    def done(ins, name, n=1):
        ins.then_inc(T.sem[name], n)
        tot[name] = tot.get(name, 0) + n

    def need(q, *names):
        for n in names:
            if got.get((q, n), 0) < tot.get(n, 0):
                Q[q].wait_ge(T.sem[n], tot[n])
                got[(q, n)] = tot[n]

    def off_of(src):
        return [c for c in T.cores if c not in topo.cores_of(src)]

    def on_of(src):
        return [c for c in T.cores if c != src and c in topo.cores_of(src)]

    def engines_of(src):
        off, out = off_of(src), {}
        eo = topo.engines(src, off[0])
        n = len(eo) // len(off)
        for k, c in enumerate(off):
            out[c] = eo[k * n:(k + 1) * n]
        for c in on_of(src):
            out[c] = [e for e in topo.engines(src, c) if e not in eo][::2]
        return out

    def place(c, at):
        return (off_of(at) + on_of(at)).index(c)

    off, on = off_of(core), on_of(core)
    peers = on + off
    others = [T.rank_of(c) for c in peers]
    eng = engines_of(core)
    inc = {c: len(engines_of(c)[core]) for c in peers}
    twin = [c for c in off if topo.die(c) == topo.die(core)][0]
    wide = {twin: topo.engines(core, twin)}
    mine, theirs = rank // 2, 1 - rank // 2

    def send(to, src_of, dst_of, sem_of, local, eng=eng):
        tr = []
        for c in to:
            rid, pid = topo.addr(c, core)
            m = 0
            for e in eng[c]:
                m |= 1 << e
            tr.append(RemoteDMATransfer(dst_ids=[DstId(rid=rid, pnc=pid)], dma_engine_mask=m, remote_sem=sem_of(c), src=src_of(c), dst=dst_of(c)))
        g.remote_dma_fused(tr, local_sem=T.sem[local])
        tot[local] = tot.get(local, 0) + sum(len(eng[c]) for c in to)

    own_val = T.VALB[:, 4096 * (rank % 2):4096 * (rank % 2) + 4096]
    done(g.sync.dma_start(T.PRI[:], T.pri[:]), "dpri", 16)
    done(S.dma_start(T.WS[:], T.w[:]), "dw", 16)
    done(g.sync.dma_start(T.TI[:, 0:4, :], T.prv[:]), "dtab", 16)
    done(S.dma_start(T.TI[:, 4:8, :], T.nxt[:]), "dtab", 16)
    done(g.sync.dma_start(T.X[:], T.x[:]), "dx", 16)

    done(g.iota(T.KP[:], [[0, 1]], 0, 1), "gi")
    done(g.iota(T.IM[:], [[1, 160]], -16, 0), "gi")
    done(g.iota(T.JI[:, 0:128], [[0, 8], [1, 16]], 1, 0, allow_small_or_imprecise_dtypes=True), "gj")
    done(g.iota(T.JI[:, 128:448], [[0, 8], [1, 4], [4, 10]], 0, 0, allow_small_or_imprecise_dtypes=True), "gj")

    done(V.memset(T.PW[:, 0:384], 0), "vz")
    need("s", "vz")
    for lo in range(384, 2048, 384):
        hi = min(lo + 384, 2048)
        done(S.activation(T.PW[:, lo:hi], T.PW[:, 0:hi - lo], COPY), "sz")
    need("y", "vz", "sz")
    for k, n in enumerate(["nxt", "prv", "key", "rw"]):
        done(g.sync.dma_start(T.PW[k:128:16, :], T[n][:]), "dpw", 16)
    done(g.sync.dma_start(own_val, T.val[:]), "dval", 16)

    kp = T.KP[:]
    m = T.IM[:, 16:144]
    ident = T.IDW[:, 16:144]
    bo = T.BO[:]
    cf = lambda j: T.CF[:, j:j + 1]
    cg = lambda j: T.CG[:, j:j + 1]
    ck = lambda j: T.CK[:, j:j + 1]

    def bits(j, sh, msk):
        done(V.tensor_scalar(T.CI[:, j:j + 1], kp, sh, msk, A.logical_shift_right, A.bitwise_and), "vc")

    done(V.memset(T.ONE[:], 1.0), "vone")
    done(V.memset(T.C128[:], 1.0 / 128), "vcon")
    done(V.memset(T.C1K[:], 1024.0), "vcon")
    done(V.memset(T.EQP[:], 0.0), "veqp")
    need("v", "gi")
    bits(0, 4, 7)
    done(V.tensor_scalar(T.I16[:], m, 4, None, A.logical_shift_right), "vi8")
    done(V.memset(T.ZER[:], 0.0), "veqp")
    need("v", "vc")
    done(V.tensor_copy(cf(0), T.CI[:, 0:1]), "vc0")
    bits(2, 0, 127)
    bits(1, 4, 1)
    bits(3, 0, 15)
    need("v", "vc0", "vi8")
    done(V.tensor_scalar(bo, T.I16[:], cf(0), None, A.is_equal), "vbo")
    bits(4, 0, 112)
    bits(5, 0, 3)
    bits(6, 3, 1)
    bits(7, 0, 1)
    done(V.memset(T.ONB[:], 1.0), "veqp")
    need("v", "vc")
    done(V.tensor_copy(T.CF[:, 1:8], T.CI[:, 1:8]), "vc2")
    need("v", "dpri")
    done(V.tensor_copy(T.PB0[:], T.PRI[:]), "vpb")
    need("v", "vc2")
    need("s", "vc2")
    done(S.activation(ck(0), cf(6), IDENT, bias=5.0, scale=-5.125), "sck")
    done(S.activation(ck(1), cf(6), IDENT, bias=-0.125, scale=0.125), "sck")
    done(V.tensor_scalar(ck(2), cf(6), 1.0 / 128, 1.0 / 5120, A.mult, A.max), "vck")
    done(V.tensor_scalar(ck(3), cf(6), 1024.50390625, 1024.5001220703125, A.mult, A.max), "vck")
    done(V.tensor_scalar(T.IDW[:], T.IM[:], cf(2), None, A.is_equal), "vid")
    done(V.tensor_scalar(cg(0), cf(1), 0.0, None, A.is_equal), "vid")
    done(V.tensor_scalar(cg(4), cf(5), 3.0, None, A.is_equal), "vid")
    need("s", "vbo", "sck")
    for lo, n in ((0, 16), (16, 16), (32, 8)):
        done(S.activation(T.BY[:, :, lo:lo + n], T.BO[:, :, 0:n], COPY, scale=ck(0)), "vby")
    done(S.activation(T.BX[:], bo, COPY, scale=ck(1)), "vby")
    need("g", "vbo")
    done(g.affine_select(T.TU[:], bo, [[-1, 128]], A.is_gt, 0.0, 0, 1), "gtu")
    done(g.iota(T.THR[:], [[128, 4], [512, 10], [5120, 16]], 128, 0), "gthr")
    need("g", "dw")
    send(peers, lambda c: T.WS[:], lambda c: T.WR[:, 8 * rank:8 * rank + 7], lambda c: T.sem.wr, "wl")
    tot["wr"] = sum(inc.values())

    def consts_a():
        perms()
        need("v", "dtab")
        done(V.tensor_copy(T.TX[:], T.TI[:]), "vcv")
        done(V.tensor_scalar(T.ZA[:], T.IM[:, 0:144], cf(4), None, A.is_equal), "vza")
        done(V.memset(T.K1[:, 0:16], 1025.0), "vc3")

    def consts_b():
        done(V.tensor_scalar(cg(1), cf(3), 2.0, -2048.0, A.is_equal, A.mult), "vc3")
        done(V.tensor_scalar(cg(2), cf(3), 1.0, None, A.not_equal), "vc3")
        done(V.tensor_scalar(cg(3), cf(3), 1.0, None, A.is_equal), "vc3")
        done(V.tensor_scalar(cg(5), cf(3), 4.0, None, A.is_ge), "vc3")
        done(V.tensor_scalar(cg(6), cf(7), -1.0, 159.53125, A.mult, A.add), "vc3")
        done(V.tensor_scalar(cg(7), cf(3), 1.0, None, A.is_le), "vc3")

    def consts_c():
        done(V.tensor_scalar(T.AB[:, NS:NS + 16], T.ZER[:, 0:16], cf(7), None, A.add), "vc3")

    def perms():
        need("s", "vid", "vc2")
        for n, (lo, msk) in enumerate([(16, cg(0)), (32, cf(1)), (0, cg(0)), (16, cf(1))]):
            done(S.activation(T.PM[:, 128 * n:128 * n + 128], T.IDW[:, lo:lo + 128], COPY, scale=msk), "sperm")
        for k in range(2):
            done(S.activation(T.BS[:, k:128:2], T.BO[:, :, k:16:2], COPY, scale=0.0625 - 0.125 * k), "sbs")

    def mark(out, pattern, base, value, sem, over=None):
        need("g", over or "veqp")
        n = pattern[0][1] * 16
        done(g.affine_select(out, out if over else T.ZER[:, 0:n], pattern, A.not_equal, value, base, 1), sem)

    def marks_a():
        mark(T.ZN[:], [[-16, 9], [-1000, 16]], 16, 1.0, "gz0")
        mark(T.PS[:, 0, :], [[-16, 9], [-1000, 2], [-2, 8]], 17, 1024.0, "gp0")
        mark(T.ZN[:], [[-16, 9], [-1000, 16]], 15, 1.0, "gzz", "gz0")

    def marks_b():
        need("g", "gp0")
        done(g.affine_select(T.PS[:, 0, :], T.PS[:, 0, :], [[0, 9], [1, 16]], A.not_equal, 0.0, 0, 0), "gp1")
        mark(T.SD[:, 1, :], [[-16, 8], [-1, 16]], 1, -4096.0, "gsd0")
        mark(T.PS[:, 0, :], [[-16, 9], [-1000, 2], [-2, 8]], 15, 160.0 - 1024.0, "gps", "gp1")
        for n, wt in ((1, -624.0), (2, -159.0)):
            mark(T.PS[:, n, :], [[-16, 9], [-1000, 2], [-2, 8]], 15, wt, "gps")
        need("g", "gsd0")
        done(g.affine_select(T.SD[:, 1, :], T.SD[:, 1, :], [[0, 8], [1, 16]], A.not_equal, 0.0, 0, 0), "gsd")

    def marks_c():
        mark(T.PS[:, 3, :], [[-16, 9], [-1000, 16]], 1, 1024.0, "gps")
        mark(T.SD[:, 0, :], [[-16, 8], [-1, 16]], 0, 4096.0, "gsd")
        mark(T.SD[:, 2, :], [[-16, 8], [-1000, 16]], -15, -4096.0, "gsd")
        mark(T.SD[:, 3, :], [[-16, 8], [-1, 16]], 0, -1.0, "gsd")
        done(g.iota(T.CNEG[:], [[0, 128]], -4416, 0, allow_small_or_imprecise_dtypes=True), "gneg")
        mark(T.LB[:], [[-16, 9], [-1000, 8], [0, 2]], 16, 1.0, "glb0")
        done(g.affine_select(T.KO[:], T.ZER[:, 0:NC], [[0, 2], [1, 2], [0, 10]], A.not_equal, 4096.0, -1, 0), "gko")
        mark(T.LB[:], [[-16, 9], [-1000, 8], [0, 2]], 15, 1.0, "glb", "glb0")

    def marks_d():
        done(g.iota(T.STEP[:], [[0, 128]], -2560, 0, allow_small_or_imprecise_dtypes=True), "vlate")
        mark(T.ZN[:], [[-16, 9], [-1000, 16]], 12, 1.0, "gz4", "pL3")

    STEP = {"L0": 3, "L1": 4, "L2": 5, "L3": 6, "M1": 2, "M2": 1, "M3": 0}

    def diags_own():
        need("s", "sbs")
        done(S.activation(T.ER[:], T.BS[:], COPY, scale=cg(4)), "ser")
        need("s", "dw", "vid")
        done(S.activation(T.WF[:], T.WS[:], COPY), "swf")
        need("s", "swf")
        for d in range(7):
            done(S.activation(T.DG[:, (7 * rank + d) * 128:(7 * rank + d) * 128 + 128], ident, COPY, scale=T.WF[:, d:d + 1]), "sdg")

    def diags(*lists):
        need("v", "wr", "vid")
        for lst in lists:
            for o in others:
                d = STEP[lst]
                done(V.tensor_scalar(T.DG[:, (7 * o + d) * 128:(7 * o + d) * 128 + 128], ident, T.WR[:, 8 * o + d:8 * o + d + 1], None, A.mult), "w" + lst)

    WHERE = {"L0": ("L0", 0, "eL0")}
    WHERE.update({d + k: ("LM" + k, NC * (d == "M"), "eL" + k) for d in "LM" for k in "123"})

    def lst_ap(lst, lo, hi):
        buf, o, _ = WHERE[lst]
        return T[buf][:, o + lo // 16:o + hi // 16]

    def gather(q, out, win, offs, sem):
        src = win.indirect(offs)
        done(S.activation(out, src, COPY) if q == "s" else V.tensor_copy(out, src), sem)

    def pick_x(lst, q, lo=0, hi=NS, tag="", win="X", at=None):
        at = at or lst
        need(q, "dx" if win == "X" else "g" + win, WHERE[at][2])
        gather(q, T["X" + lst][:, lo:hi], T[win][:], lst_ap(at, lo, hi), "s" + lst + tag)

    def back(out, q, lo, hi):
        src = "X" if out == "XB" else "XB"
        need(q, "vpv", "dx" if out == "XB" else "gXB")
        gather(q, T[out][:, lo:hi], T[src][:], T.PV[:, lo // 16:hi // 16], "g" + out)

    def ahead(q, lo, hi):
        need(q, "vpv", "dpw")
        gather(q, T.PN[:, lo:hi], T.PW[:], T.PV[:, 128 + lo // 16:128 + hi // 16], "gPN")

    def merge():
        need("y", "gPN", "gR0", "gR1", "gR2")
        done(g.sync.dma_start(T.PW[4:128:16, :], T.PN[0:128:16, :]), "dpn", 16)
        done(g.sync.dma_start(T.PW[7:128:16, :], T.PN[3:128:16, :]), "dpn", 16)

    def prv_turn():
        need("v", "vcv")
        done(V.transpose(T.TT[:], T.TX[:]), "vtr")
        consts_b()
        consts_c()
        need("t", "sperm", "vtr")
        for b1 in range(8):
            for ga in range(2):
                n = 2 * ga + b1 % 2
                ins = P.matmul(T.E0[:, b1:256:8], T.PM[:, 128 * n:128 * n + 128], T.TT[:, b1 // 2:8:4, 16 * ga:16 * ga + 16], ga == 0, ga == 1)
        done(ins, "ptab")

    def keeps(bank="QA"):
        need("t", "eK", "eL2", "gneg")
        P.matmul(T[bank][:, 0:128], T.C128[:], T.CNEG[:], True, False)
        sampled(bank, False, False)

    def pick_p(lst, q, lo=0, hi=NS, far=False):
        need(q, "dpw", WHERE[lst][2])
        bk = int(lst[0] == "M")
        keep = cg(5 if far else 2 + bk)
        out, src = T["R" + lst[1]][:, bk, lo:hi], T.PW[:].indirect(lst_ap(lst, lo, hi))
        done(S.activation(out, src, COPY, scale=keep) if q == "s" else V.tensor_scalar(out, src, keep, None, A.mult), "gR" + lst[1])

    def chase(k, bank, both, after, src=None):
        src = src or k - 1
        need("t", "gzz", "gz4", "gR%d" % src, after)
        rows, n = T["R%d" % src], 1 + both
        for ro in range(16):
            ins = P.matmul(T[bank][:, 0:NC * n], T.ZN[:, 16 - ro:144 - ro], rows[:, 0:n, ro:NS:16], ro == 0, ro == 15)
        done(ins, "pL%d" % k)

    def evac(k, bank, more):
        need("v", "pL%d" % k)
        n = NC * (1 + more)
        done(V.tensor_copy(T["LM%d" % k][:, 0:n], T[bank][:, 0:n]), "eL%d" % k)

    def hsum(lst, k, qs=None, tag=""):
        need("t", "s" + lst + tag, "sdg", "w" + lst)
        for q in qs or [rank] + others:
            o = (7 * q + STEP[lst]) * 128
            ins = P.matmul(T["H%d" % q][:, 0:NQ], T.DG[:, o:o + 128], T["X" + lst][:, NQ * q:NQ * q + NQ], k == 0, k == 6)
            if k == 6:
                done(ins, "ph%d" % q)

    parts = [("E0", 2 * NQ * mine, 2 * NQ, [rank, others[0]])] + [(b, NQ * q, NQ, [q]) for b, q in zip(("E1", "QB"), others[1:])]

    def reward(k, which=parts[:2]):
        need("t", "ser", "gR%d" % k, "vpv", "vab", *(["eL3"] if which[0][0] == "QB" else []))
        for bank, lo, n, qs in which:
            rows = T["R%d" % k][:, 0, lo:lo + n] if k else T.R0[:, lo:lo + n]
            P.matmul(T[bank][:, 0:n], T.ER[:], rows, k == 0, False)

    def sampled(bank, first, last):
        need("t", "gsd", "sk")
        P.matmul(T[bank][:, 0:128], T.SD[:, 0, :], T.K1[:, 16:144], first, False)
        P.matmul(T[bank][:, 0:128], T.SD[:, 1, :], T.K1[:, 16:144], False, False)
        return P.matmul(T[bank][:, 0:128], T.SD[:, 2, :], T.K1[:, 15:143], False, last)

    def serve(a):
        KL, VS, VR = T["KL%d" % a], T["VS%d" % a], T["VR%d" % a]
        if a == 0:
            need("s", "dval", "kr0")
            gather("s", VS[:], own_val, KL[:, 0:30], "gV")
            need("g", "gV")
            send(peers, lambda c: VS[:, NQ * place(c, core):NQ * place(c, core) + NQ], lambda c: VR[:, NQ * rank:NQ * rank + NQ],
                 lambda c: T.sem["vr0_%d" % rank], "vl")
            for c in peers:
                tot["vr0_%d" % T.rank_of(c)] = inc[c]
            send(on, lambda c: own_val, lambda c: own_val, lambda c: T.sem.tr, "tl", {c: topo.engines(core, c) for c in on})
            tot["tr"] = len(topo.engines(on[0], core))
        else:
            for q, lo, hi in (("v", 0, 10), ("s", 10, 20)):
                need(q, "tr", "kr1")
                gather(q, VS[:, 16 * lo:16 * hi], T.VALB[:], KL[:, lo:hi], "gV")
            need("g", "gV")
            send([twin], lambda c: VS[:], lambda c: VR[:, 320 * mine:320 * mine + 320], lambda c: T.sem.vr1_0, "vl", wide)
            tot["vr1_0"] = len(topo.engines(twin, core))

    def serve_own(a, q):
        if a == 0:
            need(q, "dval", "eK")
            gather(q, T.VR0[:, NQ * rank:NQ * rank + NQ], own_val, T.KS0[:, 10 * rank:10 * rank + 10], "vr0_%d" % rank)
        else:
            need(q, "tr", "eK")
            gather(q, T.VR1[:, 320 * mine:320 * mine + 320], T.VALB[:], T.KS1[:, 20 * mine:20 * mine + 20], "vr1_1")

    def heads():
        need("t", "gj", "vcon")
        P.matmul(T.H0[:, 0:128], T.C128[:], T.JI[:, 0:128], True, False)
        P.matmul(T.H0[:, 0:128], T.C128[:], T.C1K[:], False, False)
        P.matmul(T.H1[:, 0:320], T.C128[:], T.JI[:, 128:448], True, False)

    def tails(pb):
        need("t", "gtu")
        done(P.matmul(T.QB[:, 0:128], T.TU[:], pb[:], True, True), "pB")

    def counts():
        need("s", "vS", "vc3")
        done(S.activation(T.K1[:, 16:144], T.SS[:], IDENT, bias=1024.50390625, scale=1.0 / 128), "sk")
        done(S.activation(T.K4[:], T.SS[:], IDENT, bias=1025.2509765625, scale=1.0 / 512), "sk")
        done(S.activation(T.K40[:], T.SS[:], IDENT, bias=129.4751, scale=1.0 / 5120), "sk")

    def pairs_t(pb, bank, bank2):
        need("t", "gps", "sk")
        for cp in range(2):
            for n, src in enumerate((T.K1[:, 16 + cp:144:2], T.K4[:, cp:128:2], T.K40[:, cp:128:2], T.K1[:, 15 + cp:143:2])):
                ins = P.matmul(T[bank][:, 0:64], T.PS[:, n, 16 - 8 * cp:144 - 8 * cp], src, cp + n == 0, cp + n == 4)
        done(ins, "pPL")
        need("t", "gsd")
        P.matmul(T[bank2][:, 0:128], T.SD[:, 3, :], pb[:], True, False)
        done(sampled(bank2, False, True), "pS")

    def pairs_v(bank):
        need("v", "pPL", "gG0", "gG1")
        done(V.tensor_scalar(T.PL[:], T[bank][:, 0:64], 496734.0 + 1024.0, float(NS), A.add, A.min), "ePL")

    def pairs_s(bank):
        need("s", "pS", "vP")
        done(S.activation(T.KEEP[:], T[bank][:, 0:128], AF.Relu, scale=-1.0), "vpk")

    def new_priorities(out):
        need("v", "pO1", "vpk")
        done(V.tensor_tensor(out[:], T.QA[:, 0:128], T.KEEP[:], A.max), "vP")

    for a in range(2):
        pb = T.PB0 if a == 0 else T.PB1
        KS, KL, VR = T["KS%d" % a], T["KL%d" % a], T["VR%d" % a]
        if a == 0:
            need("t", "vbo", "vpb")
            done(P.matmul(T.QA[:, 0:128], bo, pb[:], True, True), "pA")
            heads()
            tails(pb)
            need("v", "pA", "vone")
            done(V.tensor_tensor_scan(T.CS[:], T.ONE[:], T.QA[:, 0:128], 0.0, A.mult, A.add), "vscan")
        else:
            need("v", "pA", "vlate")
            done(V.tensor_tensor_scan(T.CS[:], T.STEP[:], T.H3[:, 0:128], 0.0, A.add, A.add), "vscan")
            new_priorities(T.PB1)
        need("v", "vscan", "vck")
        done(V.tensor_scalar(T.KA[:], T.CS[:], ck(2), ck(3), A.mult, A.add), "vka")
        if a:
            need("t", "vP")
            tails(pb)
        need("t", "vka", "vby")
        done(P.matmul(T.H1[:, 0:320], T.KA[:], T.BY[:], False, True), "pY")
        done(P.matmul(T.H0[:, 0:128], T.KA[:], T.BX[:], False, True), "pX")
        need("v", "pB")
        done(V.tensor_tensor(T.SS[:], T.CS[:], T.QB[:, 0:128], A.subtract), "vS")
        if a == 0:
            consts_a()
        need("v", "pX", "veqp")
        done(V.tensor_scalar(T.EQP[:, :, 16:32], T.H0[:, 0:128], 0.0, 0.5, A.is_equal, A.mult), "veq")
        done(V.tensor_scalar(T.UU[:], T.H0[:, 0:128], -0.5, 0.5, A.max, A.min), "vuu")
        need("s", "pY")
        for k in range(2):
            done(S.activation(T.SG[:, 160 * k:160 * k + 160], T.H1[:, 160 * k:160 * k + 160], AF.Sign, bias=-39974.5), "ssg%d" % k)
        need("t", "veqp")
        P.matmul(T.H2[:, 0:NC], bo, T.ZER[:, 0:NC], True, False)
        for gr in range(8):
            need("t", "veq", "ssg%d" % (gr // 4))
            lo = 16 - 16 * (gr % 2)
            P.matmul(T.H2[32 * (gr // 2):32 * (gr // 2) + 32, 0:NC], T.EQP[:, gr, lo:lo + 32], T.SG[:, NC * gr:NC * gr + NC], False, False)
        need("t", "vuu")
        done(P.matmul(T.H2[:, 0:NC], T.UU[:], T.ONB[:], False, True), "pC")
        if a:
            back("XC", "v", 0, 320)
        else:
            marks_a()
            prv_turn()
            diags_own()
        need("v", "pC")
        done(V.tensor_scalar(T.COL[:], T.H2[:, 0:NC], 64.0, 127.0, A.add, A.min), "eC")
        done(V.tensor_scalar(T.C16[:], T.H2[:, 0:NC], 64.0, 16.0, A.add, A.mult), "eC16")
        if a == 0:
            need("s", "ptab")
            done(S.activation(T.PV[:], T.E0[:, 0:256], COPY), "vpv")
        counts()
        need("v", "eC", "vS", "gthr")
        done(V.tensor_tensor(T.CM[:], T.SS[:].indirect(T.COL[:]), T.THR[:], A.is_lt), "vcm")
        need("t", "eC16", "vid", "vza")
        P.matmul(T.H3[:, 0:NC], ident, T.C16[:], True, False)
        if a:
            pairs_t(pb, "E0", "E1")
            back("XC", "s", 320, 1664)
        else:
            back("XB", "s", 0, 640)
        need("t", "vcm")
        for ro in range(16):
            ins = P.matmul(T.H3[:, 0:NC], T.ZA[:, 16 - ro:144 - ro], T.CM[:, ro:NS:16], False, ro == 15)
        done(ins, "pL0")
        if a == 0:
            back("XB", "v", 640, 1088)
        else:
            pairs_v("E0")
            pairs_s("E1")
            back("XC", "v", 1664, 2048)
        need("v", "pL0")
        done(V.tensor_scalar(T.L0[:], T.H3[:, 0:NC], 2047.0, None, A.min), "eL0")
        need("v", "eL0", "dpw", "vc3", "dpn")
        done(V.tensor_scalar(T.R0[:, 0:320], T.PW[:].indirect(T.L0[:, 0:20]), cg(1), None, A.add), "gR0")
        need("s", "eL0", "dpw", "vc3", "dpn")
        done(S.activation(T.R0[:, 320:NS], T.PW[:].indirect(T.L0[:, 20:40]), IDENT, bias=cg(1)), "gR0")
        pick_x("L0", "s")
        need("v", "gR0")
        done(V.transpose(T.RT[:], T.R0[:]), "vrt")
        if a:
            pick_x("M1", "s", 0, 320, "", "XB", "L0")
            pick_x("M1", "v", 320, NS, "", "XB", "L0")
        else:
            back("XB", "v", 1088, 1344)
            back("XB", "s", 1344, 1536)
        need("t", "sperm", "vscan", "vS", "gko", "ePL", "vpk")
        if a:
            P.matmul(T.QA[:, 0:NC], T.C128[:], T.KO[:], True, False)
        need("t", "vrt")
        rows = [("QA", 0, 2, "pK"), ("QB", 0, 0, None), ("QB", NC, 1, "pL1")] + [("E0", 0, 4, "pL2")] * a
        for bank, col, row, sem in rows:
            for h in range(2):
                for gb in range(2):
                    n = 2 * gb + h
                    first, end = (False, n == 3) if a and bank == "QA" else (gb == 0, gb == 1)
                    ins = P.matmul(T[bank][:, col + h:col + NC:2], T.PM[:, 128 * n:128 * n + 128], T.RT[:, :, 16 * gb + row], first, end)
            if sem:
                done(ins, sem)
        need("v", "pK")
        done(V.tensor_scalar(KS[:], T.QA[:, 0:NC], 2048.0, None, A.add), "eK")
        evac(1, "QB", True)
        need("g", "eK")
        if a == 0:
            send(peers, lambda c: KS[:, 10 * T.rank_of(c):10 * T.rank_of(c) + 10], lambda c: KL[:, 10 * place(core, c):10 * place(core, c) + 10],
                 lambda c: T.sem.kr0, "kl")
            tot["kr0"] = sum(inc.values())
            marks_b()
        else:
            send([twin], lambda c: KS[:, 20 * theirs:20 * theirs + 20], lambda c: KL[:, 0:20], lambda c: T.sem.kr1, "kl", wide)
            tot["kr1"] = len(topo.engines(twin, core))
        need("t", "eC16", "eL0", "vuu", "ssg1")
        if a == 0:
            pick_p("M1", "v")
            pick_p("L1", "s")
            chase(2, "QA", True, "eK")
            pick_x("L1", "s")
            back("XB", "v", 1536, 2048)
            diags("L0", "L1")
            hsum("L0", 0)
            evac(2, "QA", True)
            serve_own(a, "s")
            hsum("L1", 1)
            reward(0)
            reward(1)
            pick_p("L2", "v")
            serve(a)
            marks_c()
            pick_x("L2", "s")
            chase(3, "QB", False, "eL1")
            marks_d()
            diags("L2", "M1", "M2")
            reward(2)
            hsum("L2", 2)
            pick_x("M1", "v", win="XB", at="L0")
            evac(3, "QB", False)
            diags("M3", "L3")
            pick_x("M2", "s", win="XB", at="M1")
            hsum("M1", 3)
            for k in range(3):
                reward(k, parts[2:])
            hsum("M2", 4)
            last = (("L3", "v", "X", "L3"), ("M3", "s", "XB", "M2"))
        else:
            pick_p("L1", "v", far=True)
            pick_x("L1", "s")
            hsum("L0", 0)
            keeps()
            hsum("M1", 1)
            chase(3, "QB", False, "eL1", 1)
            evac(2, "E0", False)
            serve_own(a, "v")
            pick_x("M2", "s", 0, 320, "", "XB", "M1")
            serve(a)
            need("t", "eL2")
            reward(0)
            reward(1)
            hsum("L1", 2)
            evac(3, "QB", False)
            for k in range(2):
                reward(k, parts[2:])
            pick_x("M2", "s", 320, NS, "", "XB", "M1")
            pick_x("L2", "v", 0, 448)
            pick_x("L2", "s", 448, NS)
            hsum("M2", 3)
            hsum("L2", 4)
            last = (("L3", "v", "X", "L3"), ("M3", "s", "XC", "M1"))
        for tag, (bank, lo, n, qs) in zip(("", "b", "c"), parts):
            for lst, q, win, at in last:
                pick_x(lst, q, lo, lo + n, tag, win, at)
            for k, (lst, q, win, at) in enumerate(last):
                hsum(lst, 5 + k, qs, tag)
        if a == 0:
            ahead("s", 0, 768)
            done(S.activation(T.LC[:], bo, COPY, scale=cg(7)), "slc")
        for k, (bank, lo, n, qs) in enumerate(parts):
            for q in qs:
                need("v", "ph%d" % q, "vr1_%d" % (k == 0) if a else "vr0_%d" % q)
                done(V.tensor_tensor(T.PROD[:, NQ * q:NQ * q + NQ], VR[:, NQ * q:NQ * q + NQ], T["H%d" % q][:, 0:NQ], A.mult), "vpr%d" % k)
            need("t", "vpr%d" % k, "sbs")
            done(P.matmul(T[bank][:, 0:n], T.BS[:], T.PROD[:, lo:lo + n], False, True), "pE%d" % k)
        if a == 0:
            pairs_t(pb, "H2", "H1")
            pairs_s("H1")
            keeps()
        for k, (bank, lo, n, qs) in enumerate(parts):
            if a == 0 and k == 2:
                pairs_v("H2")
            need("v", "pE%d" % k)
            done(V.tensor_scalar(T.AB[:, lo:lo + n], T[bank][:, 0:n], 1.0, 63.0, A.max, A.min), "vab")
        if a == 0:
            need("t", "vpk")
            P.matmul(T.H3[:, 0:128], bo, T.KEEP[:], True, False)
            heads()
        else:
            keeps("H0")
        need("v", "vab", "ePL")
        need("s", "vab", "ePL")
        for b in range(2):
            lo, out = 512 * b, "H0" if a + b == 2 else "QA"
            done(V.tensor_scalar(T.GB[:, lo:lo + 256], T.AB[:].indirect(T.PL[:, lo // 16:lo // 16 + 16]), cg(6), None, A.add), "gG%d" % b)
            done(S.activation(T.GB[:, lo + 256:lo + 512], T.AB[:].indirect(T.PL[:, lo // 16 + 16:lo // 16 + 32]), IDENT, bias=cg(6)), "gG%d" % b)
            need("t", "gG%d" % b, "glb", "slc")
            for h in range(8 * (1 - a)):
                ins = P.matmul(T.H3[:, 64 * b:64 * b + 64], T.LC[:], T.GB[:, lo + h:lo + 512:8], False, b == 1 and h == 7)
            if b > a:
                done(ins, "pA")
            for h in range(8):
                ins = P.matmul(T[out][:, 64 * b:64 * b + 64], T.LB[:, 16 - 2 * h:144 - 2 * h], T.GB[:, lo + h:lo + 512:8], False, a + b > 0 and h == 7)
            if a + b:
                done(ins, "pO%d" % b)
        if a == 0:
            ahead("v", 768, 1152)
            ahead("s", 1152, 2048)
            merge()
    for b, bank in enumerate(("QA", "H0")):
        cols = slice(64 * b, 64 * b + 64)
        need("v", "pO%d" % b)
        done(V.tensor_tensor(T.YO[:, cols], T[bank][:, cols], T.KEEP[:, cols], A.max), "vY%d" % b)
        need("y", "vY%d" % b)
        done(g.sync.dma_start(T.y[:, cols], T.YO[:, cols]), "dy", 16)
    need("y", "dy")
    for n in sorted(tot):
        if max([got.get((q, n), 0) for q in Q]) < tot[n]:
            need("g", n)
